import numpy as np
import ml_dtypes


def mxq(x, axis, fmt="e4m3"):
    dtype, down = {"e4m3": (ml_dtypes.float8_e4m3fn, 7), "e5m2": (ml_dtypes.float8_e5m2, 14)}[fmt]
    v = np.moveaxis(np.asarray(x, np.float32).astype(ml_dtypes.bfloat16).astype(np.float64), axis, -1)
    blocks = v.reshape(v.shape[:-1] + (-1, 32))
    amax = np.abs(blocks).max(-1, keepdims=True)
    byte = np.maximum(np.where(amax > 0, np.frexp(amax)[1] - 1 + 127, 0) - down, 1)
    scale = np.exp2(byte - 127.0)
    codes = (blocks / scale).astype(np.float32).astype(dtype).astype(np.float64)
    return np.moveaxis((codes * scale).reshape(v.shape), -1, axis)


WIDE = False


def mx_kscale(k):
    if not WIDE:
        return np.ones(k)
    levels = np.array([18, -18])
    if k % 512:
        return np.exp2(np.random.permutation(np.resize(levels, k // 32))).repeat(32)
    a = np.empty((k // 512, 16))
    for p in range(k // 512):
        a[p, :8] = np.random.permutation(np.resize(levels, 8))
        for g in range(8):
            far = levels[np.abs(levels - a[p, g]) >= 10]
            a[p, g + 8] = far[np.random.randint(len(far))]
    return np.exp2(a.ravel()).repeat(32)


def f64(x):
    return np.asarray(x).astype(np.float64)


def striped(idx):
    return np.tile(np.asarray(idx).reshape(-1, 16).T, (8, 1)).astype(np.uint16)


def unstriped(offs):
    return offs[:16].T.reshape(-1).astype(np.int64)


B = 2


def sig(x):
    return 1.0 / (1.0 + np.exp(-x))


def setup_inputs():
    n = np.random.standard_normal
    uni = np.random.uniform
    idx = np.random.permutation(2048)[:1024]
    f_d = mx_kscale(512)
    f_i = np.ones(2048)
    f_i[idx] = mx_kscale(1024)
    return {
        "xT": (n((512, 2048)) / np.sqrt(512) * f_d[:, None]).astype(np.float32),
        "dyT": (n((512, 2048)) * f_i[None, :]).astype(np.float32),
        "w1": (n((2, 512, 512)) / f_d[:, None]).astype(np.float32),
        "ts": np.tile(uni(0.75, 1.3, 2048) / np.sqrt(512) / f_i, (128, 1)).astype(np.float32),
        "tx": np.tile(uni(0.75, 1.3, 2048), (128, 1)).astype(np.float32),
        "cf": (uni(0.75, 1.3, (512, 1))).astype(np.float32),
        "offs": striped(idx),
    }


def reference(xT, dyT, w1, ts, tx, cf, offs):
    idx = unstriped(offs).reshape(B, 512)
    xT_i = f64(xT)[:, idx].transpose(1, 0, 2)
    dyT_i = f64(dyT)[:, idx].transpose(1, 0, 2)
    ts_i = f64(ts)[:1][:, idx].transpose(1, 0, 2)
    tx_i = f64(tx)[:1][:, idx].transpose(1, 0, 2)
    a = mxq(f64(w1), 1, "e4m3").transpose(0, 2, 1) @ mxq(xT_i, 1, "e4m3")
    z = f64(cf) * tx_i * a
    h = ts_i * z * sig(z)
    out = mxq(h, 2, "e4m3") @ mxq(dyT_i, 2, "e5m2").transpose(0, 2, 1)
    return out

@@ -1,0 +1,344 @@
+from contextlib import ExitStack
+
+import concourse.mybir as mybir
+from concourse.masks import make_identity
+
+F32 = mybir.dt.float32
+BF16 = mybir.dt.bfloat16
+I32 = mybir.dt.int32
+U32 = mybir.dt.uint32
+U16 = mybir.dt.uint16
+U8 = mybir.dt.uint8
+E4M3X4 = mybir.dt.float8_e4m3fn_x4
+E5M2X4 = mybir.dt.float8_e5m2_x4
+COPY = mybir.ActivationFunctionType.Copy
+SILU = mybir.ActivationFunctionType.Silu
+MULT = mybir.AluOpType.mult
+
+P = 128
+PACK = 4
+EXPERTS = 2
+SLOTS = 512
+TOKENS = 2048
+D = 512
+F = 512
+E = 512
+LIST_COLS = SLOTS // 16
+HALF = TOKENS // 2
+
+FLOPS = 2 * EXPERTS * SLOTS * F * (D + E)
+BYTES = 4 * (D * TOKENS + E * TOKENS + EXPERTS * D * F + 2 * TOKENS + F + EXPERTS * F * E) + 2 * P * EXPERTS * LIST_COLS
+
+
+def tile_attend_gxfull_sil_W2_kernel(tc, xT, dyT, w1, ts, tx, cf, offs, out):
+    nc = tc.nc
+    with ExitStack() as ctx:
+        keep = ctx.enter_context(tc.tile_pool(name="keep", bufs=1))
+        raw = ctx.enter_context(tc.tile_pool(name="raw", bufs=5))
+        psum = ctx.enter_context(tc.psum_pool(name="psum", bufs=1))
+        banks = [psum.tile([P, 512], F32, name=f"bank{n}") for n in range(8)]
+
+        offsets = keep.tile([P, EXPERTS * LIST_COLS], U16, name="offsets")
+        nc.sync.dma_start(offsets[:], offs)
+
+        tx_row = keep.tile([1, TOKENS], F32, name="tx_row")
+        ts_row = keep.tile([1, TOKENS], F32, name="ts_row")
+        nc.sync.dma_start(ts_row[:], ts[0:1, :])
+        nc.sync.dma_start(tx_row[:], tx[0:1, :])
+        cf_stage = keep.tile([PACK, P], F32, name="cf_stage")
+        nc.sync.dma_start(cf_stage[:], cf.rearrange("(c p) o -> c (p o)", c=PACK))
+
+        def slots_of(b):
+            return offsets[:, b * LIST_COLS : (b + 1) * LIST_COLS]
+
+        warm = keep.tile([P, 2], F32, name="warm")
+        nc.vector.memset(warm[:, 0:1], 0.0)
+        nc.scalar.activation(warm[:, 1:2], warm[:, 0:1], SILU)
+
+        tx_win = keep.tile([P, TOKENS], F32, name="tx_win")
+        ts_win = keep.tile([P, TOKENS], F32, name="ts_win")
+        cf_rows = keep.tile([P, P], F32, name="cf_rows")
+        ident = keep.tile([P, P], F32, name="ident")
+        nc.gpsimd.memset(ts_win[:], 0.0)
+        nc.vector.memset(tx_win[:], 0.0)
+        nc.vector.tensor_copy(ts_win[0:1, :], ts_row[:])
+        nc.scalar.activation(tx_win[0:1, :], tx_row[:], COPY)
+        make_identity(nc, ident[:])
+        nc.gpsimd.memset(cf_rows[:], 0.0)
+        nc.gpsimd.tensor_copy(cf_rows[0:PACK, :], cf_stage[:])
+
+        x_rows = xT.rearrange("(p u j) t -> p u j t", u=2, j=2)
+        x_raw, w_raw, dy_win = {}, {}, {}
+
+        def load_x(u, h):
+            x_raw[u, h] = raw.tile([P, 2, HALF], F32, name="raw")
+            nc.sync.dma_start(x_raw[u, h][:], x_rows[:, u, :, h * HALF : (h + 1) * HALF])
+
+        def load_w(b):
+            w_raw[b] = raw.tile([P, PACK, F], F32, name="raw")
+            nc.sync.dma_start(w_raw[b][:], w1[b].rearrange("(p j) f -> p j f", j=PACK))
+
+        def load_dy(k):
+            dy_win[k] = raw.tile([P, TOKENS], F32, name="raw")
+            nc.sync.dma_start(dy_win[k][:], dyT[k * P : (k + 1) * P, :])
+
+        load_x(0, 0)
+        load_x(0, 1)
+        load_x(1, 0)
+        load_x(1, 1)
+
+        def turn_slot_scales(win, name, first_col):
+            picked = keep.tile([P, EXPERTS * SLOTS], F32, name=name + "_picked")
+            nc.vector.tensor_copy(picked[:], win[:].indirect(offsets[:]))
+            for b in range(EXPERTS):
+                for r in range(PACK):
+                    col = first_col + b * PACK + r
+                    nc.tensor.transpose(
+                        banks[0][:, col : col + P],
+                        picked[:, b * SLOTS + r : (b + 1) * SLOTS : PACK],
+                        ident[:],
+                    )
+
+        turn_slot_scales(ts_win, "ts", 0)
+        turn_slot_scales(tx_win, "tx", 8)
+        nc.tensor.transpose(banks[0][:, 16 : 16 + P], cf_rows[:], ident[:])
+
+        def mx_tiles(name, width):
+            codes = keep.tile([P, width], U32, name=name + "_codes", align_bytes=64)
+            scales = keep.tile([P, width], U8, name=name + "_scales", align_bytes=64)
+            return codes, scales
+
+        x_mx, x_picked = {}, {}
+
+        x_in = {b: keep.tile([P, SLOTS * PACK], BF16, name=f"x_in{b}", align_bytes=64) for b in range(EXPERTS)}
+        w_in = {0: keep.tile([P, F * PACK], BF16, name="w_in0", align_bytes=64), 1: keep.tile([P, F * PACK], BF16, name="w_in1", align_bytes=64)}
+        w_mx = {b: mx_tiles(f"w{b}", F) for b in range(EXPERTS)}
+
+        def weave_w(b, lo, hi, on_vector):
+            dst = w_in[b][:, lo * PACK : hi * PACK].rearrange("p (c i j) -> p c j i", i=4, j=PACK)
+            src = w_raw[b][:, :, lo:hi].rearrange("p j (c i) -> p c j i", i=4)
+            if on_vector:
+                nc.vector.tensor_copy(dst, src)
+            else:
+                nc.scalar.activation(dst, src, COPY)
+
+        def quantize_w(b, lo, hi):
+            nc.vector.quantize_mx(
+                w_mx[b][0][:, lo:hi].bitcast(E4M3X4), w_mx[b][1][:, lo:hi], w_in[b][:, lo * PACK : hi * PACK]
+            )
+
+        x_pairs = [keep.tile([P, TOKENS], U32, name=f"x_pairs{u}") for u in range(2)]
+
+        def cast_x(u, h, lo, hi, on_vector):
+            dst = x_pairs[u][:, h * HALF + lo : h * HALF + hi].bitcast(BF16).rearrange("p (t j) -> p t j", j=2)
+            src = x_raw[u, h][:, :, lo:hi].rearrange("p j t -> p t j")
+            if on_vector:
+                nc.vector.tensor_copy(dst, src)
+            else:
+                nc.scalar.activation(dst, src, COPY)
+
+        for b in range(EXPERTS):
+            x_picked[b] = keep.tile([P, 2, SLOTS], U32, name=f"x_picked{b}")
+
+        spent = x_picked[0][:, 0, :].bitcast(F32)
+        ts_cols = spent[:, 0:8].rearrange("p (b r) -> p b r", r=PACK)
+        tx_cols = spent[:, 8:16].rearrange("p (b r) -> p b r", r=PACK)
+        cf_cols = spent[:, 16:20]
+
+        def fetch_columns():
+            nc.vector.tensor_copy(spent[:, 0:20], banks[0][:, 0:20])
+
+        def gather_x(u, b):
+            nc.vector.tensor_copy(x_picked[b][:, u, :], x_pairs[u][:].indirect(slots_of(b)))
+
+        def weave_x(b):
+            nc.vector.tensor_copy(
+                x_in[b][:].bitcast(I32).rearrange("p (n u) -> p n u", u=2),
+                x_picked[b][:].bitcast(I32).rearrange("p u n -> p n u"),
+            )
+
+        def quantize_x(b):
+            x_mx[b] = mx_tiles(f"x{b}", SLOTS)
+            nc.vector.quantize_mx(x_mx[b][0][:].bitcast(E4M3X4), x_mx[b][1][:], x_in[b][:])
+
+        act, scaled = {}, {}
+
+        def first_product(b, c):
+            cols = slice(c * P, (c + 1) * P)
+            acc = banks[4 + c]
+            nc.tensor.matmul_mx(
+                acc[:],
+                lhsT=w_mx[b][0][:, cols].bitcast(E4M3X4),
+                lhsT_scale=w_mx[b][1][:, cols],
+                rhs=x_mx[b][0][:].bitcast(E4M3X4),
+                rhs_scale=x_mx[b][1][:],
+                start=True,
+                stop=True,
+            )
+            scaled[b, c] = keep.tile([P, PACK, P], F32, name=f"scaled{b}{c}")
+            nc.scalar.activation(
+                scaled[b, c][:], acc[:].rearrange("p (s r) -> p r s", r=PACK), COPY, scale=cf_cols[:, c : c + 1]
+            )
+
+        def turn(b, c, r):
+            nc.tensor.transpose(banks[r][:, c * P : (c + 1) * P], scaled[b, c][:, r, :], ident[:])
+
+        for b in range(EXPERTS):
+            act[b] = keep.tile([P, PACK, F], F32, name=f"act{b}")
+
+        def activate(b, r):
+            nc.scalar.activation(act[b][:, r, :], banks[r][:], SILU, scale=tx_cols[:, b, r : r + 1])
+
+        h_in, h_mx = {}, {}
+
+        def gate_h(b, c):
+            h_in[b, c] = keep.tile([P, P * PACK], BF16, name=f"h_in{b}{c}", align_bytes=64)
+            nc.vector.tensor_tensor(
+                h_in[b, c][:].rearrange("p (g i r) -> p g r i", i=4, r=PACK),
+                act[b][:, :, c * P : (c + 1) * P].rearrange("p r (g i) -> p g r i", i=4),
+                ts_cols[:, b, :].unsqueeze(1).unsqueeze(3).to_broadcast([P, P // 4, PACK, 4]),
+                MULT,
+            )
+
+        gated = {}
+
+        def gate_rows(b, r):
+            if b not in gated:
+                gated[b] = keep.tile([P, PACK, F], BF16, name=f"gated{b}")
+            nc.scalar.activation(gated[b][:, r, :], act[b][:, r, :], COPY, scale=ts_cols[:, b, r : r + 1])
+
+        def weave_h(b, c):
+            h_in[b, c] = keep.tile([P, P * PACK], BF16, name=f"h_in{b}{c}", align_bytes=64)
+            nc.vector.tensor_copy(
+                h_in[b, c][:].rearrange("p (g i r) -> p g r i", i=4, r=PACK),
+                gated[b][:, :, c * P : (c + 1) * P].rearrange("p r (g i) -> p g r i", i=4),
+            )
+
+        def quantize_h(b, c):
+            h_mx[b, c] = mx_tiles(f"h{b}{c}", P)
+            nc.vector.quantize_mx(h_mx[b, c][0][:].bitcast(E4M3X4), h_mx[b, c][1][:], h_in[b, c][:])
+
+        dy_picked, dy_in = {}, {}
+        dy_mx = {b: mx_tiles(f"dy{b}", E) for b in range(EXPERTS)}
+
+        def gather_dy(k, b, into):
+            dy_picked[k, b] = into
+            nc.vector.tensor_copy(into, dy_win[k][:].indirect(slots_of(b)))
+
+        def quarter(tile, n):
+            return tile[:, n * SLOTS : (n + 1) * SLOTS]
+
+        def turn_dy(b, half, bank_no):
+            bank = banks[bank_no][:].rearrange("p (u e) -> p u e", u=2)
+            for kk in range(2):
+                words = dy_picked[2 * half + kk, b].bitcast(F32)
+                for u in range(2):
+                    nc.tensor.transpose(bank[:, u, kk * P : (kk + 1) * P], words[:, u : SLOTS // 2 : 2], ident[:])
+            dy_in[b, half] = keep.tile([P, 2 * P * PACK], BF16, name=f"dy_in{b}{half}", align_bytes=64)
+            nc.scalar.copy(
+                dy_in[b, half][:].bitcast(F32).rearrange("p (e u) -> p e u", u=2),
+                bank.rearrange("p u e -> p e u"),
+            )
+
+        def quantize_dy(b, half):
+            cols = slice(half * 2 * P, (half + 1) * 2 * P)
+            nc.vector.quantize_mx(dy_mx[b][0][:, cols].bitcast(E5M2X4), dy_mx[b][1][:, cols], dy_in[b, half][:])
+
+        def second_product(b, c, bank_no, on_vector, queue):
+            acc = banks[bank_no]
+            nc.tensor.matmul_mx(
+                acc[:],
+                lhsT=h_mx[b, c][0][:].bitcast(E4M3X4),
+                lhsT_scale=h_mx[b, c][1][:],
+                rhs=dy_mx[b][0][:].bitcast(E5M2X4),
+                rhs_scale=dy_mx[b][1][:],
+                start=True,
+                stop=True,
+            )
+            result = keep.tile([P, E], F32, name=f"result{b}{c}")
+            if on_vector:
+                nc.vector.tensor_copy(result[:], acc[:])
+            else:
+                nc.scalar.copy(result[:], acc[:])
+            queue.dma_start(out[b, c * P : (c + 1) * P, :], result[:])
+
+        def dyp(n):
+            return keep.tile([P, SLOTS], BF16, name=f"dyp{n}")[:]
+
+        load_w(0)
+        cast_x(0, 0, 0, HALF, False)
+        load_w(1)
+        cast_x(0, 1, 0, 640, False)
+        cast_x(0, 1, 640, HALF, True)
+        load_dy(0)
+        cast_x(1, 0, 0, HALF, False)
+        load_dy(1)
+        gather_x(0, 0)
+        gather_x(0, 1)
+        cast_x(1, 1, 0, 512, False)
+        cast_x(1, 1, 512, HALF, True)
+        load_dy(2)
+        gather_x(1, 0)
+        gather_x(1, 1)
+        weave_w(0, 0, F // 2, False)
+        weave_w(0, F // 2, F, False)
+        load_dy(3)
+        weave_x(0)
+        weave_x(1)
+        quantize_w(0, 0, F // 2)
+        quantize_x(0)
+        fetch_columns()
+        quantize_w(0, F // 2, F)
+        quantize_x(1)
+        weave_w(1, 0, F, False)
+        for c in range(F // P):
+            first_product(0, c)
+        quantize_w(1, 0, F)
+        gather_dy(0, 0, quarter(w_in[1], 0))
+        for c in range(F // P):
+            if c == 2:
+                first_product(1, 0)
+            for r in range(PACK):
+                turn(0, c, r)
+        gather_dy(1, 0, quarter(w_in[1], 2))
+        gather_dy(0, 1, quarter(w_in[1], 1))
+        gather_dy(1, 1, quarter(w_in[1], 3))
+        for r in range(PACK):
+            activate(0, r)
+        for c in range(1, F // P):
+            first_product(1, c)
+        turn_dy(0, 0, 4)
+        for c in range(F // P):
+            for r in range(PACK):
+                turn(1, c, r)
+        for r in range(PACK):
+            gate_rows(0, r)
+        gather_dy(2, 0, dyp(4))
+        gather_dy(3, 0, dyp(5))
+        gather_dy(2, 1, dyp(6))
+        gather_dy(3, 1, dyp(7))
+        turn_dy(0, 1, 5)
+        for r in range(PACK):
+            activate(1, r)
+        turn_dy(1, 0, 6)
+        turn_dy(1, 1, 7)
+        quantize_dy(0, 0)
+        weave_h(0, 0)
+        quantize_dy(0, 1)
+        weave_h(0, 1)
+        for c in range(F // P):
+            quantize_h(0, c)
+            if c + 2 < F // P:
+                weave_h(0, c + 2)
+        for c in range(F // P):
+            second_product(0, c, c, False, nc.sync)
+        gate_h(1, 0)
+        quantize_dy(1, 0)
+        gate_h(1, 1)
+        quantize_dy(1, 1)
+        for c in range(F // P):
+            quantize_h(1, c)
+            if c + 2 < F // P:
+                gate_h(1, c + 2)
+        for c in range(F // P):
+            second_product(1, c, 4 + c, c == 3, nc.scalar if c == 2 else nc.sync)

@@ -115,8 +115,8 @@ def tile_attend_gxfull_sil_W2_kernel(tc, xT, dyT, w1, ts, tx, cf, offs, out):
         w_mx = {b: mx_tiles(f"w{b}", F) for b in range(EXPERTS)}
 
         def weave_w(b, lo, hi, on_vector):
-            dst = w_in[b][:, lo * PACK : hi * PACK].rearrange("p (c i j) -> p c j i", i=4, j=PACK)
-            src = w_raw[b][:, :, lo:hi].rearrange("p j (c i) -> p c j i", i=4)
+            dst = w_in[b][:, lo * PACK : hi * PACK].rearrange("p (c i j) -> p c j i", i=2, j=PACK)
+            src = w_raw[b][:, :, lo:hi].rearrange("p j (c i) -> p c j i", i=2)
             if on_vector:
                 nc.vector.tensor_copy(dst, src)
             else:
@@ -130,8 +130,8 @@ def tile_attend_gxfull_sil_W2_kernel(tc, xT, dyT, w1, ts, tx, cf, offs, out):
         x_pairs = [keep.tile([P, TOKENS], U32, name=f"x_pairs{u}") for u in range(2)]
 
         def cast_x(u, h, lo, hi, on_vector):
-            dst = x_pairs[u][:, h * HALF + lo : h * HALF + hi].bitcast(BF16).rearrange("p (t j) -> p t j", j=2)
-            src = x_raw[u, h][:, :, lo:hi].rearrange("p j t -> p t j")
+            dst = x_pairs[u][:, h * HALF + lo : h * HALF + hi].bitcast(BF16).rearrange("p (g i j) -> p g j i", i=4, j=2)
+            src = x_raw[u, h][:, :, lo:hi].rearrange("p j (g i) -> p g j i", i=4)
             if on_vector:
                 nc.vector.tensor_copy(dst, src)
             else:
@@ -153,8 +153,8 @@ def tile_attend_gxfull_sil_W2_kernel(tc, xT, dyT, w1, ts, tx, cf, offs, out):
 
         def weave_x(b):
             nc.vector.tensor_copy(
-                x_in[b][:].bitcast(I32).rearrange("p (n u) -> p n u", u=2),
-                x_picked[b][:].bitcast(I32).rearrange("p u n -> p n u"),
+                x_in[b][:].bitcast(I32).rearrange("p (g i u) -> p g u i", i=2, u=2),
+                x_picked[b][:].bitcast(I32).rearrange("p u (g i) -> p g u i", i=2),
             )
 
         def quantize_x(b):
@@ -191,21 +191,15 @@ def tile_attend_gxfull_sil_W2_kernel(tc, xT, dyT, w1, ts, tx, cf, offs, out):
 
         h_in, h_mx = {}, {}
 
-        def gate_h(b, c):
-            h_in[b, c] = keep.tile([P, P * PACK], BF16, name=f"h_in{b}{c}", align_bytes=64)
-            nc.vector.tensor_tensor(
-                h_in[b, c][:].rearrange("p (g i r) -> p g r i", i=4, r=PACK),
-                act[b][:, :, c * P : (c + 1) * P].rearrange("p r (g i) -> p g r i", i=4),
-                ts_cols[:, b, :].unsqueeze(1).unsqueeze(3).to_broadcast([P, P // 4, PACK, 4]),
-                MULT,
-            )
-
         gated = {}
 
-        def gate_rows(b, r):
+        def gate_rows(b, r, on_vector):
             if b not in gated:
                 gated[b] = keep.tile([P, PACK, F], BF16, name=f"gated{b}")
-            nc.scalar.activation(gated[b][:, r, :], act[b][:, r, :], COPY, scale=ts_cols[:, b, r : r + 1])
+            if on_vector:
+                nc.vector.tensor_scalar(gated[b][:, r, :], act[b][:, r, :], ts_cols[:, b, r : r + 1], None, MULT)
+            else:
+                nc.scalar.activation(gated[b][:, r, :], act[b][:, r, :], COPY, scale=ts_cols[:, b, r : r + 1])
 
         def weave_h(b, c):
             h_in[b, c] = keep.tile([P, P * PACK], BF16, name=f"h_in{b}{c}", align_bytes=64)
@@ -236,8 +230,8 @@ def tile_attend_gxfull_sil_W2_kernel(tc, xT, dyT, w1, ts, tx, cf, offs, out):
                     nc.tensor.transpose(bank[:, u, kk * P : (kk + 1) * P], words[:, u : SLOTS // 2 : 2], ident[:])
             dy_in[b, half] = keep.tile([P, 2 * P * PACK], BF16, name=f"dy_in{b}{half}", align_bytes=64)
             nc.scalar.copy(
-                dy_in[b, half][:].bitcast(F32).rearrange("p (e u) -> p e u", u=2),
-                bank.rearrange("p u e -> p e u"),
+                dy_in[b, half][:].bitcast(F32).rearrange("p (g i u) -> p g u i", i=2, u=2),
+                bank.rearrange("p u (g i) -> p g u i", i=2),
             )
 
         def quantize_dy(b, half):
@@ -312,7 +306,7 @@ def tile_attend_gxfull_sil_W2_kernel(tc, xT, dyT, w1, ts, tx, cf, offs, out):
             for r in range(PACK):
                 turn(1, c, r)
         for r in range(PACK):
-            gate_rows(0, r)
+            gate_rows(0, r, False)
         gather_dy(2, 0, dyp(4))
         gather_dy(3, 0, dyp(5))
         gather_dy(2, 1, dyp(6))
@@ -332,13 +326,15 @@ def tile_attend_gxfull_sil_W2_kernel(tc, xT, dyT, w1, ts, tx, cf, offs, out):
                 weave_h(0, c + 2)
         for c in range(F // P):
             second_product(0, c, c, False, nc.sync)
-        gate_h(1, 0)
+        for r in range(PACK):
+            gate_rows(1, r, True)
         quantize_dy(1, 0)
-        gate_h(1, 1)
+        weave_h(1, 0)
+        weave_h(1, 1)
         quantize_dy(1, 1)
         for c in range(F // P):
             quantize_h(1, c)
             if c + 2 < F // P:
-                gate_h(1, c + 2)
+                weave_h(1, c + 2)
         for c in range(F // P):
-            second_product(1, c, 4 + c, c == 3, nc.scalar if c == 2 else nc.sync)
+            second_product(1, c, 4 + c, c == 3, nc.scalar if c == 3 else nc.sync)

@@ -5,7 +5,6 @@ from concourse.masks import make_identity
 
 F32 = mybir.dt.float32
 BF16 = mybir.dt.bfloat16
-I32 = mybir.dt.int32
 U32 = mybir.dt.uint32
 U16 = mybir.dt.uint16
 U8 = mybir.dt.uint8
@@ -24,7 +23,7 @@ D = 512
 F = 512
 E = 512
 LIST_COLS = SLOTS // 16
-HALF = TOKENS // 2
+F_HALF = F // 2
 
 FLOPS = 2 * EXPERTS * SLOTS * F * (D + E)
 BYTES = 4 * (D * TOKENS + E * TOKENS + EXPERTS * D * F + 2 * TOKENS + F + EXPERTS * F * E) + 2 * P * EXPERTS * LIST_COLS
@@ -34,216 +33,196 @@ def tile_attend_gxfull_sil_W2_kernel(tc, xT, dyT, w1, ts, tx, cf, offs, out):
     nc = tc.nc
     with ExitStack() as ctx:
         keep = ctx.enter_context(tc.tile_pool(name="keep", bufs=1))
-        raw = ctx.enter_context(tc.tile_pool(name="raw", bufs=5))
+        windows = ctx.enter_context(tc.tile_pool(name="windows", bufs=6))
         psum = ctx.enter_context(tc.psum_pool(name="psum", bufs=1))
         banks = [psum.tile([P, 512], F32, name=f"bank{n}") for n in range(8)]
 
         offsets = keep.tile([P, EXPERTS * LIST_COLS], U16, name="offsets")
         nc.sync.dma_start(offsets[:], offs)
-
         tx_row = keep.tile([1, TOKENS], F32, name="tx_row")
         ts_row = keep.tile([1, TOKENS], F32, name="ts_row")
-        nc.sync.dma_start(ts_row[:], ts[0:1, :])
-        nc.sync.dma_start(tx_row[:], tx[0:1, :])
-        cf_stage = keep.tile([PACK, P], F32, name="cf_stage")
-        nc.sync.dma_start(cf_stage[:], cf.rearrange("(c p) o -> c (p o)", c=PACK))
+        cf_cols = keep.tile([P, PACK], F32, name="cf_cols")
+        nc.scalar.dma_start(tx_row[:], tx[0:1, :])
+        nc.scalar.dma_start(ts_row[:], ts[0:1, :])
+        nc.scalar.dma_start(cf_cols[:], cf.rearrange("(p c) o -> p (c o)", c=PACK))
 
-        def slots_of(b):
-            return offsets[:, b * LIST_COLS : (b + 1) * LIST_COLS]
+        def slots_of(b, lo=0, hi=SLOTS):
+            return offsets[:, b * LIST_COLS + lo // 16 : b * LIST_COLS + hi // 16]
+
+        def copy_on(on_vector, dst, src):
+            if on_vector:
+                nc.vector.tensor_copy(dst, src)
+            else:
+                nc.scalar.activation(dst, src, COPY)
 
         warm = keep.tile([P, 2], F32, name="warm")
         nc.vector.memset(warm[:, 0:1], 0.0)
         nc.scalar.activation(warm[:, 1:2], warm[:, 0:1], SILU)
 
-        tx_win = keep.tile([P, TOKENS], F32, name="tx_win")
         ts_win = keep.tile([P, TOKENS], F32, name="ts_win")
-        cf_rows = keep.tile([P, P], F32, name="cf_rows")
+        tx_win = keep.tile([P, TOKENS], F32, name="tx_win")
         ident = keep.tile([P, P], F32, name="ident")
-        nc.gpsimd.memset(ts_win[:], 0.0)
         nc.vector.memset(tx_win[:], 0.0)
+        nc.vector.memset(ts_win[:], 0.0)
+        nc.vector.tensor_copy(tx_win[0:1, :], tx_row[:])
         nc.vector.tensor_copy(ts_win[0:1, :], ts_row[:])
-        nc.scalar.activation(tx_win[0:1, :], tx_row[:], COPY)
         make_identity(nc, ident[:])
-        nc.gpsimd.memset(cf_rows[:], 0.0)
-        nc.gpsimd.tensor_copy(cf_rows[0:PACK, :], cf_stage[:])
 
-        x_rows = xT.rearrange("(p u j) t -> p u j t", u=2, j=2)
-        x_raw, w_raw, dy_win = {}, {}, {}
+        x_rows = xT.rearrange("(p j) t -> p j t", j=PACK)
+        x_win, w_raw, dy_win = {}, {}, {}
 
-        def load_x(u, h):
-            x_raw[u, h] = raw.tile([P, 2, HALF], F32, name="raw")
-            nc.sync.dma_start(x_raw[u, h][:], x_rows[:, u, :, h * HALF : (h + 1) * HALF])
+        def load_x(j):
+            x_win[j] = windows.tile([P, TOKENS], F32, name="window")
+            nc.sync.dma_start(x_win[j][:], x_rows[:, j, :])
 
         def load_w(b):
-            w_raw[b] = raw.tile([P, PACK, F], F32, name="raw")
+            w_raw[b] = keep.tile([P, PACK, F], F32, name=f"w_raw{b}")
             nc.sync.dma_start(w_raw[b][:], w1[b].rearrange("(p j) f -> p j f", j=PACK))
 
         def load_dy(k):
-            dy_win[k] = raw.tile([P, TOKENS], F32, name="raw")
+            dy_win[k] = windows.tile([P, TOKENS], F32, name="window")
             nc.sync.dma_start(dy_win[k][:], dyT[k * P : (k + 1) * P, :])
 
-        load_x(0, 0)
-        load_x(0, 1)
-        load_x(1, 0)
-        load_x(1, 1)
+        for j in range(PACK):
+            load_x(j)
+        load_w(0)
+        load_dy(0)
+        load_dy(1)
 
-        def turn_slot_scales(win, name, first_col):
+        cf_all = keep.tile([P, F], F32, name="cf_all")
+        for c in range(PACK):
+            nc.tensor.transpose(banks[1][:, c * P : (c + 1) * P], cf_cols[:, c : c + 1].to_broadcast([P, P]), ident[:])
+        nc.scalar.copy(cf_all[:].rearrange("p (n c) -> p n c", c=PACK), banks[1][:].rearrange("p (c n) -> p n c", c=PACK))
+
+        x_picked = {b: keep.tile([P, PACK, SLOTS], BF16, name=f"x_picked{b}") for b in range(EXPERTS)}
+        slot_scales = x_picked[0][:, 0, 0 : 4 * EXPERTS * PACK].bitcast(F32)
+
+        def turn_slot_scales(win, name, first_col, on_vector):
             picked = keep.tile([P, EXPERTS * SLOTS], F32, name=name + "_picked")
-            nc.vector.tensor_copy(picked[:], win[:].indirect(offsets[:]))
+            copy_on(on_vector, picked[:], win[:].indirect(offsets[:]))
             for b in range(EXPERTS):
                 for r in range(PACK):
                     col = first_col + b * PACK + r
                     nc.tensor.transpose(
-                        banks[0][:, col : col + P],
-                        picked[:, b * SLOTS + r : (b + 1) * SLOTS : PACK],
-                        ident[:],
+                        banks[0][:, col : col + P], picked[:, b * SLOTS + r : (b + 1) * SLOTS : PACK], ident[:]
                     )
 
-        turn_slot_scales(ts_win, "ts", 0)
-        turn_slot_scales(tx_win, "tx", 8)
-        nc.tensor.transpose(banks[0][:, 16 : 16 + P], cf_rows[:], ident[:])
+        turn_slot_scales(tx_win, "tx", 0, False)
+        turn_slot_scales(ts_win, "ts", EXPERTS * PACK, True)
+        tx_cols = slot_scales[:, 0 : EXPERTS * PACK].rearrange("p (b r) -> p b r", r=PACK)
+        ts_cols = slot_scales[:, EXPERTS * PACK :].rearrange("p (b r) -> p b r", r=PACK)
+
+        def fetch_slot_scales():
+            nc.scalar.copy(slot_scales, banks[0][:, 0 : 2 * EXPERTS * PACK])
 
         def mx_tiles(name, width):
             codes = keep.tile([P, width], U32, name=name + "_codes", align_bytes=64)
             scales = keep.tile([P, width], U8, name=name + "_scales", align_bytes=64)
             return codes, scales
 
-        x_mx, x_picked = {}, {}
+        x_mx = {b: mx_tiles(f"x{b}", SLOTS) for b in range(EXPERTS)}
+        x_in, w_in, w_mx = {}, {}, {}
 
-        x_in = {b: keep.tile([P, SLOTS * PACK], BF16, name=f"x_in{b}", align_bytes=64) for b in range(EXPERTS)}
-        w_in = {0: keep.tile([P, F * PACK], BF16, name="w_in0", align_bytes=64), 1: keep.tile([P, F * PACK], BF16, name="w_in1", align_bytes=64)}
-        w_mx = {b: mx_tiles(f"w{b}", F) for b in range(EXPERTS)}
-
-        def weave_w(b, lo, hi, on_vector):
-            dst = w_in[b][:, lo * PACK : hi * PACK].rearrange("p (c i j) -> p c j i", i=2, j=PACK)
-            src = w_raw[b][:, :, lo:hi].rearrange("p j (c i) -> p c j i", i=2)
-            if on_vector:
-                nc.vector.tensor_copy(dst, src)
-            else:
-                nc.scalar.activation(dst, src, COPY)
-
-        def quantize_w(b, lo, hi):
-            nc.vector.quantize_mx(
-                w_mx[b][0][:, lo:hi].bitcast(E4M3X4), w_mx[b][1][:, lo:hi], w_in[b][:, lo * PACK : hi * PACK]
-            )
-
-        x_pairs = [keep.tile([P, TOKENS], U32, name=f"x_pairs{u}") for u in range(2)]
-
-        def cast_x(u, h, lo, hi, on_vector):
-            dst = x_pairs[u][:, h * HALF + lo : h * HALF + hi].bitcast(BF16).rearrange("p (g i j) -> p g j i", i=4, j=2)
-            src = x_raw[u, h][:, :, lo:hi].rearrange("p j (g i) -> p g j i", i=4)
-            if on_vector:
-                nc.vector.tensor_copy(dst, src)
-            else:
-                nc.scalar.activation(dst, src, COPY)
-
-        for b in range(EXPERTS):
-            x_picked[b] = keep.tile([P, 2, SLOTS], U32, name=f"x_picked{b}")
-
-        spent = x_picked[0][:, 0, :].bitcast(F32)
-        ts_cols = spent[:, 0:8].rearrange("p (b r) -> p b r", r=PACK)
-        tx_cols = spent[:, 8:16].rearrange("p (b r) -> p b r", r=PACK)
-        cf_cols = spent[:, 16:20]
-
-        def fetch_columns():
-            nc.vector.tensor_copy(spent[:, 0:20], banks[0][:, 0:20])
-
-        def gather_x(u, b):
-            nc.vector.tensor_copy(x_picked[b][:, u, :], x_pairs[u][:].indirect(slots_of(b)))
+        def gather_x(j, b, on_vector, lo=0, hi=SLOTS):
+            copy_on(on_vector, x_picked[b][:, j, lo:hi], x_win[j][:].indirect(slots_of(b, lo, hi)))
 
         def weave_x(b):
+            x_in[b] = keep.tile([P, SLOTS * PACK], BF16, name=f"x_in{b}", align_bytes=64)
             nc.vector.tensor_copy(
-                x_in[b][:].bitcast(I32).rearrange("p (g i u) -> p g u i", i=2, u=2),
-                x_picked[b][:].bitcast(I32).rearrange("p u (g i) -> p g u i", i=2),
+                x_in[b][:].rearrange("p (r s h j) -> p s j h r", r=PACK, h=2, j=PACK),
+                x_picked[b][:].rearrange("p j (s h r) -> p s j h r", h=2, r=PACK),
             )
 
         def quantize_x(b):
-            x_mx[b] = mx_tiles(f"x{b}", SLOTS)
             nc.vector.quantize_mx(x_mx[b][0][:].bitcast(E4M3X4), x_mx[b][1][:], x_in[b][:])
 
-        act, scaled = {}, {}
-
-        def first_product(b, c):
-            cols = slice(c * P, (c + 1) * P)
-            acc = banks[4 + c]
-            nc.tensor.matmul_mx(
-                acc[:],
-                lhsT=w_mx[b][0][:, cols].bitcast(E4M3X4),
-                lhsT_scale=w_mx[b][1][:, cols],
-                rhs=x_mx[b][0][:].bitcast(E4M3X4),
-                rhs_scale=x_mx[b][1][:],
-                start=True,
-                stop=True,
-            )
-            scaled[b, c] = keep.tile([P, PACK, P], F32, name=f"scaled{b}{c}")
-            nc.scalar.activation(
-                scaled[b, c][:], acc[:].rearrange("p (s r) -> p r s", r=PACK), COPY, scale=cf_cols[:, c : c + 1]
+        def weave_w(b, half, on_vector):
+            w_in[b, half] = keep.tile([P, F_HALF * PACK], BF16, name=f"w_in{b}{half}", align_bytes=64)
+            copy_on(
+                on_vector,
+                w_in[b, half][:].rearrange("p (c i j) -> p c j i", i=4, j=PACK),
+                w_raw[b][:, :, half * F_HALF : (half + 1) * F_HALF].rearrange("p j (c i) -> p c j i", i=4),
             )
 
-        def turn(b, c, r):
-            nc.tensor.transpose(banks[r][:, c * P : (c + 1) * P], scaled[b, c][:, r, :], ident[:])
+        def quantize_w(b, half):
+            w_mx[b, half] = mx_tiles(f"w{b}{half}", F_HALF)
+            nc.vector.quantize_mx(w_mx[b, half][0][:].bitcast(E4M3X4), w_mx[b, half][1][:], w_in[b, half][:])
 
-        for b in range(EXPERTS):
-            act[b] = keep.tile([P, PACK, F], F32, name=f"act{b}")
+        scaled, act, h_in, h_mx = {}, {}, {}, {}
 
-        def activate(b, r):
-            nc.scalar.activation(act[b][:, r, :], banks[r][:], SILU, scale=tx_cols[:, b, r : r + 1])
+        def first_product(b, half, pair):
+            bank = banks[2 + 2 * half + pair][:].rearrange("p (r f) -> p r f", r=2)
+            for rr in range(2):
+                cols = slice((2 * pair + rr) * P, (2 * pair + rr + 1) * P)
+                nc.tensor.matmul_mx(
+                    bank[:, rr, :],
+                    lhsT=x_mx[b][0][:, cols].bitcast(E4M3X4),
+                    lhsT_scale=x_mx[b][1][:, cols],
+                    rhs=w_mx[b, half][0][:].bitcast(E4M3X4),
+                    rhs_scale=w_mx[b, half][1][:],
+                    start=True,
+                    stop=True,
+                )
 
-        h_in, h_mx = {}, {}
+        def scale_units(b, half, pair):
+            bank = banks[2 + 2 * half + pair][:].rearrange("p (r f) -> p r f", r=2)
+            scaled[b, half, pair] = keep.tile([P, 2, F_HALF], F32, name=f"scaled{b}{half}{pair}")
+            cf_half = cf_all[:, half * F_HALF : (half + 1) * F_HALF].unsqueeze(1).broadcast_to([P, 2, F_HALF])
+            nc.vector.tensor_tensor(scaled[b, half, pair][:], bank, cf_half, MULT)
 
-        gated = {}
+        def activate(b, half, pair):
+            if pair == 0:
+                act[b, half] = keep.tile([P, PACK, F_HALF], F32, name=f"act{b}{half}")
+            for rr in range(2):
+                r = 2 * pair + rr
+                nc.scalar.activation(
+                    act[b, half][:, r, :], scaled[b, half, pair][:, rr, :], SILU, scale=tx_cols[:, b, r : r + 1]
+                )
 
-        def gate_rows(b, r, on_vector):
-            if b not in gated:
-                gated[b] = keep.tile([P, PACK, F], BF16, name=f"gated{b}")
-            if on_vector:
-                nc.vector.tensor_scalar(gated[b][:, r, :], act[b][:, r, :], ts_cols[:, b, r : r + 1], None, MULT)
-            else:
-                nc.scalar.activation(gated[b][:, r, :], act[b][:, r, :], COPY, scale=ts_cols[:, b, r : r + 1])
-
-        def weave_h(b, c):
-            h_in[b, c] = keep.tile([P, P * PACK], BF16, name=f"h_in{b}{c}", align_bytes=64)
-            nc.vector.tensor_copy(
-                h_in[b, c][:].rearrange("p (g i r) -> p g r i", i=4, r=PACK),
-                gated[b][:, :, c * P : (c + 1) * P].rearrange("p r (g i) -> p g r i", i=4),
+        def gate(b, half):
+            h_in[b, half] = keep.tile([P, F_HALF * PACK], BF16, name=f"h_in{b}{half}", align_bytes=64)
+            nc.vector.tensor_tensor(
+                h_in[b, half][:].rearrange("p (c i r) -> p c r i", i=4, r=PACK),
+                act[b, half][:].rearrange("p r (c i) -> p c r i", i=4),
+                ts_cols[:, b, :].unsqueeze(1).unsqueeze(3).broadcast_to([P, F_HALF // 4, PACK, 4]),
+                MULT,
             )
 
-        def quantize_h(b, c):
-            h_mx[b, c] = mx_tiles(f"h{b}{c}", P)
-            nc.vector.quantize_mx(h_mx[b, c][0][:].bitcast(E4M3X4), h_mx[b, c][1][:], h_in[b, c][:])
+        def quantize_h(b, half):
+            h_mx[b, half] = mx_tiles(f"h{b}{half}", F_HALF)
+            nc.vector.quantize_mx(h_mx[b, half][0][:].bitcast(E4M3X4), h_mx[b, half][1][:], h_in[b, half][:])
 
-        dy_picked, dy_in = {}, {}
+        dy_picked = {}
+        dy_in = {b: keep.tile([P, E * PACK], BF16, name=f"dy_in{b}", align_bytes=64) for b in range(EXPERTS)}
         dy_mx = {b: mx_tiles(f"dy{b}", E) for b in range(EXPERTS)}
 
-        def gather_dy(k, b, into):
-            dy_picked[k, b] = into
-            nc.vector.tensor_copy(into, dy_win[k][:].indirect(slots_of(b)))
+        def gather_dy(k, b, on_vector):
+            dy_picked[k, b] = keep.tile([P, SLOTS], BF16, name=f"dy_picked{k}{b}")
+            copy_on(on_vector, dy_picked[k, b][:], dy_win[k][:].indirect(slots_of(b)))
 
-        def quarter(tile, n):
-            return tile[:, n * SLOTS : (n + 1) * SLOTS]
-
-        def turn_dy(b, half, bank_no):
-            bank = banks[bank_no][:].rearrange("p (u e) -> p u e", u=2)
-            for kk in range(2):
-                words = dy_picked[2 * half + kk, b].bitcast(F32)
+        def turn_dy(b, first, count, bank_no, on_vector):
+            bank = banks[bank_no][:, 0 : 2 * count * P].rearrange("p (u e) -> p u e", u=2)
+            for kk in range(count):
+                words = dy_picked[first + kk, b][:].bitcast(F32)
                 for u in range(2):
                     nc.tensor.transpose(bank[:, u, kk * P : (kk + 1) * P], words[:, u : SLOTS // 2 : 2], ident[:])
-            dy_in[b, half] = keep.tile([P, 2 * P * PACK], BF16, name=f"dy_in{b}{half}", align_bytes=64)
-            nc.scalar.copy(
-                dy_in[b, half][:].bitcast(F32).rearrange("p (g i u) -> p g u i", i=2, u=2),
-                bank.rearrange("p u (g i) -> p g u i", i=2),
-            )
+            dst = dy_in[b][:, first * P * PACK : (first + count) * P * PACK].bitcast(F32).rearrange("p (g i u) -> p g u i", i=2, u=2)
+            src = bank.rearrange("p u (g i) -> p g u i", i=2)
+            if on_vector:
+                nc.vector.tensor_copy(dst, src)
+            else:
+                nc.scalar.copy(dst, src)
 
-        def quantize_dy(b, half):
-            cols = slice(half * 2 * P, (half + 1) * 2 * P)
-            nc.vector.quantize_mx(dy_mx[b][0][:, cols].bitcast(E5M2X4), dy_mx[b][1][:, cols], dy_in[b, half][:])
+        def quantize_dy(b):
+            nc.vector.quantize_mx(dy_mx[b][0][:].bitcast(E5M2X4), dy_mx[b][1][:], dy_in[b][:])
 
-        def second_product(b, c, bank_no, on_vector, queue):
+        def second_product(b, c, bank_no, on_vector):
             acc = banks[bank_no]
+            cols = slice((c % 2) * P, (c % 2 + 1) * P)
             nc.tensor.matmul_mx(
                 acc[:],
-                lhsT=h_mx[b, c][0][:].bitcast(E4M3X4),
-                lhsT_scale=h_mx[b, c][1][:],
+                lhsT=h_mx[b, c // 2][0][:, cols].bitcast(E4M3X4),
+                lhsT_scale=h_mx[b, c // 2][1][:, cols],
                 rhs=dy_mx[b][0][:].bitcast(E5M2X4),
                 rhs_scale=dy_mx[b][1][:],
                 start=True,
@@ -254,87 +233,69 @@ def tile_attend_gxfull_sil_W2_kernel(tc, xT, dyT, w1, ts, tx, cf, offs, out):
                 nc.vector.tensor_copy(result[:], acc[:])
             else:
                 nc.scalar.copy(result[:], acc[:])
-            queue.dma_start(out[b, c * P : (c + 1) * P, :], result[:])
+            nc.sync.dma_start(out[b, c * P : (c + 1) * P, :], result[:])
 
-        def dyp(n):
-            return keep.tile([P, SLOTS], BF16, name=f"dyp{n}")[:]
-
-        load_w(0)
-        cast_x(0, 0, 0, HALF, False)
-        load_w(1)
-        cast_x(0, 1, 0, 640, False)
-        cast_x(0, 1, 640, HALF, True)
-        load_dy(0)
-        cast_x(1, 0, 0, HALF, False)
-        load_dy(1)
-        gather_x(0, 0)
-        gather_x(0, 1)
-        cast_x(1, 1, 0, 512, False)
-        cast_x(1, 1, 512, HALF, True)
+        for j in range(PACK - 1):
+            gather_x(j, 0, True)
+            gather_x(j, 1, False)
         load_dy(2)
-        gather_x(1, 0)
-        gather_x(1, 1)
-        weave_w(0, 0, F // 2, False)
-        weave_w(0, F // 2, F, False)
+        load_w(1)
         load_dy(3)
+        gather_x(3, 0, True, 0, SLOTS // 2)
+        gather_x(3, 0, False, SLOTS // 2, SLOTS)
+        gather_x(3, 1, False)
         weave_x(0)
-        weave_x(1)
-        quantize_w(0, 0, F // 2)
+        weave_w(0, 0, False)
         quantize_x(0)
-        fetch_columns()
-        quantize_w(0, F // 2, F)
+        weave_w(0, 1, True)
+        fetch_slot_scales()
+        quantize_w(0, 0)
+        quantize_w(0, 1)
+        weave_x(1)
+        for half in range(2):
+            for pair in range(2):
+                first_product(0, half, pair)
         quantize_x(1)
-        weave_w(1, 0, F, False)
+        gather_dy(0, 0, False)
+        for half in range(2):
+            for pair in range(2):
+                scale_units(0, half, pair)
+                activate(0, half, pair)
+        gather_dy(0, 1, False)
+        gate(0, 0)
+        gather_dy(1, 0, False)
+        gate(0, 1)
+        quantize_h(0, 0)
+        quantize_h(0, 1)
+        gather_dy(1, 1, False)
+        turn_dy(0, 0, 2, 6, False)
+        gather_dy(2, 0, True)
+        turn_dy(1, 0, 2, 7, False)
+        weave_w(1, 0, True)
+        gather_dy(2, 1, False)
+        weave_w(1, 1, True)
+        quantize_w(1, 0)
+        quantize_w(1, 1)
+        for half in range(2):
+            for pair in range(2):
+                first_product(1, half, pair)
+        gather_dy(3, 0, True)
+        gather_dy(3, 1, False)
+        turn_dy(0, 2, 2, 6, False)
+        for pair in range(2):
+            scale_units(1, 0, pair)
+            activate(1, 0, pair)
+        quantize_dy(0)
+        for pair in range(2):
+            scale_units(1, 1, pair)
+            activate(1, 1, pair)
+        turn_dy(1, 2, 2, 2, False)
+        gate(1, 0)
         for c in range(F // P):
-            first_product(0, c)
-        quantize_w(1, 0, F)
-        gather_dy(0, 0, quarter(w_in[1], 0))
+            second_product(0, c, (0, 1, 7, 6)[c], False)
+        quantize_dy(1)
+        gate(1, 1)
+        quantize_h(1, 0)
+        quantize_h(1, 1)
         for c in range(F // P):
-            if c == 2:
-                first_product(1, 0)
-            for r in range(PACK):
-                turn(0, c, r)
-        gather_dy(1, 0, quarter(w_in[1], 2))
-        gather_dy(0, 1, quarter(w_in[1], 1))
-        gather_dy(1, 1, quarter(w_in[1], 3))
-        for r in range(PACK):
-            activate(0, r)
-        for c in range(1, F // P):
-            first_product(1, c)
-        turn_dy(0, 0, 4)
-        for c in range(F // P):
-            for r in range(PACK):
-                turn(1, c, r)
-        for r in range(PACK):
-            gate_rows(0, r, False)
-        gather_dy(2, 0, dyp(4))
-        gather_dy(3, 0, dyp(5))
-        gather_dy(2, 1, dyp(6))
-        gather_dy(3, 1, dyp(7))
-        turn_dy(0, 1, 5)
-        for r in range(PACK):
-            activate(1, r)
-        turn_dy(1, 0, 6)
-        turn_dy(1, 1, 7)
-        quantize_dy(0, 0)
-        weave_h(0, 0)
-        quantize_dy(0, 1)
-        weave_h(0, 1)
-        for c in range(F // P):
-            quantize_h(0, c)
-            if c + 2 < F // P:
-                weave_h(0, c + 2)
-        for c in range(F // P):
-            second_product(0, c, c, False, nc.sync)
-        for r in range(PACK):
-            gate_rows(1, r, True)
-        quantize_dy(1, 0)
-        weave_h(1, 0)
-        weave_h(1, 1)
-        quantize_dy(1, 1)
-        for c in range(F // P):
-            quantize_h(1, c)
-            if c + 2 < F // P:
-                weave_h(1, c + 2)
-        for c in range(F // P):
-            second_product(1, c, 4 + c, c == 3, nc.scalar if c == 3 else nc.sync)
+            second_product(1, c, (3, 2, 4, 5)[c], c % 2 == 0)

@@ -43,7 +43,7 @@ def tile_attend_gxfull_sil_W2_kernel(tc, xT, dyT, w1, ts, tx, cf, offs, out):
         ts_row = keep.tile([1, TOKENS], F32, name="ts_row")
         cf_cols = keep.tile([P, PACK], F32, name="cf_cols")
         nc.scalar.dma_start(tx_row[:], tx[0:1, :])
-        nc.scalar.dma_start(ts_row[:], ts[0:1, :])
+        nc.sync.dma_start(ts_row[:], ts[0:1, :])
         nc.scalar.dma_start(cf_cols[:], cf.rearrange("(p c) o -> p (c o)", c=PACK))
 
         def slots_of(b, lo=0, hi=SLOTS):
@@ -80,13 +80,17 @@ def tile_attend_gxfull_sil_W2_kernel(tc, xT, dyT, w1, ts, tx, cf, offs, out):
             nc.sync.dma_start(w_raw[b][:], w1[b].rearrange("(p j) f -> p j f", j=PACK))
 
         def load_dy(k):
-            dy_win[k] = windows.tile([P, TOKENS], F32, name="window")
+            if k == E // P - 1:
+                dy_win[k] = keep.tile([P, TOKENS], F32, name="last_window")
+            else:
+                dy_win[k] = windows.tile([P, TOKENS], F32, name="window")
             nc.sync.dma_start(dy_win[k][:], dyT[k * P : (k + 1) * P, :])
 
         for j in range(PACK):
             load_x(j)
         load_w(0)
         load_dy(0)
+        load_w(1)
         load_dy(1)
 
         cf_all = keep.tile([P, F], F32, name="cf_all")
@@ -95,7 +99,8 @@ def tile_attend_gxfull_sil_W2_kernel(tc, xT, dyT, w1, ts, tx, cf, offs, out):
         nc.scalar.copy(cf_all[:].rearrange("p (n c) -> p n c", c=PACK), banks[1][:].rearrange("p (c n) -> p n c", c=PACK))
 
         x_picked = {b: keep.tile([P, PACK, SLOTS], BF16, name=f"x_picked{b}") for b in range(EXPERTS)}
-        slot_scales = x_picked[0][:, 0, 0 : 4 * EXPERTS * PACK].bitcast(F32)
+        x_in = {b: keep.tile([P, SLOTS * PACK], BF16, name=f"x_in{b}", align_bytes=64) for b in range(EXPERTS)}
+        slot_scales = x_in[0][:, 0 : 4 * EXPERTS * PACK].bitcast(F32)
 
         def turn_slot_scales(win, name, first_col, on_vector):
             picked = keep.tile([P, EXPERTS * SLOTS], F32, name=name + "_picked")
@@ -120,24 +125,29 @@ def tile_attend_gxfull_sil_W2_kernel(tc, xT, dyT, w1, ts, tx, cf, offs, out):
             scales = keep.tile([P, width], U8, name=name + "_scales", align_bytes=64)
             return codes, scales
 
-        x_mx = {b: mx_tiles(f"x{b}", SLOTS) for b in range(EXPERTS)}
-        x_in, w_in, w_mx = {}, {}, {}
+        w_in = {
+            (b, half): keep.tile([P, F_HALF * PACK], BF16, name=f"w_in{b}{half}", align_bytes=64)
+            for b in range(EXPERTS)
+            for half in range(2)
+        }
+        x_codes = {}
+        x_scales = {b: keep.tile([P, SLOTS], U8, name=f"x_scales{b}", align_bytes=64) for b in range(EXPERTS)}
+        w_mx = {}
 
         def gather_x(j, b, on_vector, lo=0, hi=SLOTS):
             copy_on(on_vector, x_picked[b][:, j, lo:hi], x_win[j][:].indirect(slots_of(b, lo, hi)))
 
         def weave_x(b):
-            x_in[b] = keep.tile([P, SLOTS * PACK], BF16, name=f"x_in{b}", align_bytes=64)
             nc.vector.tensor_copy(
                 x_in[b][:].rearrange("p (r s h j) -> p s j h r", r=PACK, h=2, j=PACK),
                 x_picked[b][:].rearrange("p j (s h r) -> p s j h r", h=2, r=PACK),
             )
 
         def quantize_x(b):
-            nc.vector.quantize_mx(x_mx[b][0][:].bitcast(E4M3X4), x_mx[b][1][:], x_in[b][:])
+            x_codes[b] = keep.tile([P, SLOTS], U32, name=("x_codes0", "w_in00")[b], align_bytes=64)[:]
+            nc.vector.quantize_mx(x_codes[b].bitcast(E4M3X4), x_scales[b][:], x_in[b][:])
 
         def weave_w(b, half, on_vector):
-            w_in[b, half] = keep.tile([P, F_HALF * PACK], BF16, name=f"w_in{b}{half}", align_bytes=64)
             copy_on(
                 on_vector,
                 w_in[b, half][:].rearrange("p (c i j) -> p c j i", i=4, j=PACK),
@@ -148,7 +158,7 @@ def tile_attend_gxfull_sil_W2_kernel(tc, xT, dyT, w1, ts, tx, cf, offs, out):
             w_mx[b, half] = mx_tiles(f"w{b}{half}", F_HALF)
             nc.vector.quantize_mx(w_mx[b, half][0][:].bitcast(E4M3X4), w_mx[b, half][1][:], w_in[b, half][:])
 
-        scaled, act, h_in, h_mx = {}, {}, {}, {}
+        scaled, act = {}, {}
 
         def first_product(b, half, pair):
             bank = banks[2 + 2 * half + pair][:].rearrange("p (r f) -> p r f", r=2)
@@ -156,8 +166,8 @@ def tile_attend_gxfull_sil_W2_kernel(tc, xT, dyT, w1, ts, tx, cf, offs, out):
                 cols = slice((2 * pair + rr) * P, (2 * pair + rr + 1) * P)
                 nc.tensor.matmul_mx(
                     bank[:, rr, :],
-                    lhsT=x_mx[b][0][:, cols].bitcast(E4M3X4),
-                    lhsT_scale=x_mx[b][1][:, cols],
+                    lhsT=x_codes[b][:, cols].bitcast(E4M3X4),
+                    lhsT_scale=x_scales[b][:, cols],
                     rhs=w_mx[b, half][0][:].bitcast(E4M3X4),
                     rhs_scale=w_mx[b, half][1][:],
                     start=True,
@@ -166,136 +176,152 @@ def tile_attend_gxfull_sil_W2_kernel(tc, xT, dyT, w1, ts, tx, cf, offs, out):
 
         def scale_units(b, half, pair):
             bank = banks[2 + 2 * half + pair][:].rearrange("p (r f) -> p r f", r=2)
-            scaled[b, half, pair] = keep.tile([P, 2, F_HALF], F32, name=f"scaled{b}{half}{pair}")
+            if (b, half) == (0, 0):
+                spent = x_in[1][:].bitcast(F32).rearrange("p (q r f) -> p q r f", q=2, r=2)
+                scaled[b, half, pair] = spent[:, pair, :, :]
+            else:
+                scaled[b, half, pair] = keep.tile([P, 2, F_HALF], F32, name=f"scaled{b}{half}{pair}")[:]
             cf_half = cf_all[:, half * F_HALF : (half + 1) * F_HALF].unsqueeze(1).broadcast_to([P, 2, F_HALF])
-            nc.vector.tensor_tensor(scaled[b, half, pair][:], bank, cf_half, MULT)
+            nc.vector.tensor_tensor(scaled[b, half, pair], bank, cf_half, MULT)
 
         def activate(b, half, pair):
-            if pair == 0:
-                act[b, half] = keep.tile([P, PACK, F_HALF], F32, name=f"act{b}{half}")
+            if half == 0 and pair == 0:
+                act[b] = keep.tile([P, 2, PACK, F_HALF], F32, name="last_window" if b == EXPERTS - 1 else "act")
             for rr in range(2):
                 r = 2 * pair + rr
                 nc.scalar.activation(
-                    act[b, half][:, r, :], scaled[b, half, pair][:, rr, :], SILU, scale=tx_cols[:, b, r : r + 1]
+                    act[b][:, half, r, :], scaled[b, half, pair][:, rr, :], SILU, scale=tx_cols[:, b, r : r + 1]
                 )
 
-        def gate(b, half):
-            h_in[b, half] = keep.tile([P, F_HALF * PACK], BF16, name=f"h_in{b}{half}", align_bytes=64)
+        h_in = {b: keep.tile([P, F * PACK], BF16, name=f"h_in{b}", align_bytes=64) for b in range(EXPERTS)}
+        h_mx = {b: mx_tiles(f"h{b}", F) for b in range(EXPERTS)}
+
+        def gate(b, lo, hi):
+            half, first = divmod(lo, F_HALF)
             nc.vector.tensor_tensor(
-                h_in[b, half][:].rearrange("p (c i r) -> p c r i", i=4, r=PACK),
-                act[b, half][:].rearrange("p r (c i) -> p c r i", i=4),
-                ts_cols[:, b, :].unsqueeze(1).unsqueeze(3).broadcast_to([P, F_HALF // 4, PACK, 4]),
+                h_in[b][:, lo * PACK : hi * PACK].rearrange("p (c i r) -> p c r i", i=4, r=PACK),
+                act[b][:, half, :, first : first + hi - lo].rearrange("p r (c i) -> p c r i", i=4),
+                ts_cols[:, b, :].unsqueeze(1).unsqueeze(3).broadcast_to([P, (hi - lo) // 4, PACK, 4]),
                 MULT,
             )
 
-        def quantize_h(b, half):
-            h_mx[b, half] = mx_tiles(f"h{b}{half}", F_HALF)
-            nc.vector.quantize_mx(h_mx[b, half][0][:].bitcast(E4M3X4), h_mx[b, half][1][:], h_in[b, half][:])
+        def quantize_h(b, lo, hi):
+            nc.vector.quantize_mx(
+                h_mx[b][0][:, lo:hi].bitcast(E4M3X4), h_mx[b][1][:, lo:hi], h_in[b][:, lo * PACK : hi * PACK]
+            )
 
         dy_picked = {}
-        dy_in = {b: keep.tile([P, E * PACK], BF16, name=f"dy_in{b}", align_bytes=64) for b in range(EXPERTS)}
+        dy_stage = keep.tile([P, 3 * E * PACK // 2], BF16, name="dy_stage", align_bytes=64)
+        dy_in = {0: dy_stage[:, E * PACK // 2 :], 1: dy_stage[:, 0 : E * PACK]}
         dy_mx = {b: mx_tiles(f"dy{b}", E) for b in range(EXPERTS)}
 
         def gather_dy(k, b, on_vector):
             dy_picked[k, b] = keep.tile([P, SLOTS], BF16, name=f"dy_picked{k}{b}")
             copy_on(on_vector, dy_picked[k, b][:], dy_win[k][:].indirect(slots_of(b)))
 
-        def turn_dy(b, first, count, bank_no, on_vector):
-            bank = banks[bank_no][:, 0 : 2 * count * P].rearrange("p (u e) -> p u e", u=2)
-            for kk in range(count):
-                words = dy_picked[first + kk, b][:].bitcast(F32)
-                for u in range(2):
-                    nc.tensor.transpose(bank[:, u, kk * P : (kk + 1) * P], words[:, u : SLOTS // 2 : 2], ident[:])
-            dst = dy_in[b][:, first * P * PACK : (first + count) * P * PACK].bitcast(F32).rearrange("p (g i u) -> p g u i", i=2, u=2)
-            src = bank.rearrange("p u (g i) -> p g u i", i=2)
+        def turn_dy(k, b, bank_no):
+            bank = banks[bank_no][:].rearrange("p (u e) -> p u e", u=2)
+            words = dy_picked[k, b][:].bitcast(F32)
+            for u in range(2):
+                nc.tensor.transpose(bank[:, u, (k % 2) * P : (k % 2 + 1) * P], words[:, u : SLOTS // 2 : 2], ident[:])
+
+        def fetch_dy(b, half, bank_no, on_vector):
+            dst = dy_in[b][:, half * 2 * P * PACK : (half + 1) * 2 * P * PACK].bitcast(F32)
+            dst = dst.rearrange("p (g i u) -> p g u i", i=2, u=2)
+            src = banks[bank_no][:].rearrange("p (u g i) -> p g u i", u=2, i=2)
             if on_vector:
                 nc.vector.tensor_copy(dst, src)
             else:
                 nc.scalar.copy(dst, src)
 
         def quantize_dy(b):
-            nc.vector.quantize_mx(dy_mx[b][0][:].bitcast(E5M2X4), dy_mx[b][1][:], dy_in[b][:])
+            nc.vector.quantize_mx(dy_mx[b][0][:].bitcast(E5M2X4), dy_mx[b][1][:], dy_in[b])
 
-        def second_product(b, c, bank_no, on_vector):
-            acc = banks[bank_no]
-            cols = slice((c % 2) * P, (c % 2 + 1) * P)
+        def second_product(b, c, bank_no, on_vector, lo=0, hi=E):
+            acc = banks[bank_no][:, 0 : hi - lo]
+            cols = slice(c * P, (c + 1) * P)
             nc.tensor.matmul_mx(
-                acc[:],
-                lhsT=h_mx[b, c // 2][0][:, cols].bitcast(E4M3X4),
-                lhsT_scale=h_mx[b, c // 2][1][:, cols],
-                rhs=dy_mx[b][0][:].bitcast(E5M2X4),
-                rhs_scale=dy_mx[b][1][:],
+                acc,
+                lhsT=h_mx[b][0][:, cols].bitcast(E4M3X4),
+                lhsT_scale=h_mx[b][1][:, cols],
+                rhs=dy_mx[b][0][:, lo:hi].bitcast(E5M2X4),
+                rhs_scale=dy_mx[b][1][:, lo:hi],
                 start=True,
                 stop=True,
             )
-            result = keep.tile([P, E], F32, name=f"result{b}{c}")
+            result = keep.tile([P, hi - lo], F32, name=f"result{b}{c}{lo}")
             if on_vector:
-                nc.vector.tensor_copy(result[:], acc[:])
+                nc.vector.tensor_copy(result[:], acc)
             else:
-                nc.scalar.copy(result[:], acc[:])
-            nc.sync.dma_start(out[b, c * P : (c + 1) * P, :], result[:])
+                nc.scalar.copy(result[:], acc)
+            nc.sync.dma_start(out[b, c * P : (c + 1) * P, lo:hi], result[:])
 
         for j in range(PACK - 1):
             gather_x(j, 0, True)
             gather_x(j, 1, False)
         load_dy(2)
-        load_w(1)
         load_dy(3)
         gather_x(3, 0, True, 0, SLOTS // 2)
         gather_x(3, 0, False, SLOTS // 2, SLOTS)
         gather_x(3, 1, False)
         weave_x(0)
         weave_w(0, 0, False)
+        weave_w(0, 1, False)
+        weave_x(1)
         quantize_x(0)
-        weave_w(0, 1, True)
         fetch_slot_scales()
         quantize_w(0, 0)
+        quantize_x(1)
         quantize_w(0, 1)
-        weave_x(1)
         for half in range(2):
             for pair in range(2):
                 first_product(0, half, pair)
-        quantize_x(1)
         gather_dy(0, 0, False)
+        gather_dy(0, 1, False)
         for half in range(2):
             for pair in range(2):
                 scale_units(0, half, pair)
                 activate(0, half, pair)
-        gather_dy(0, 1, False)
-        gate(0, 0)
-        gather_dy(1, 0, False)
-        gate(0, 1)
-        quantize_h(0, 0)
-        quantize_h(0, 1)
-        gather_dy(1, 1, False)
-        turn_dy(0, 0, 2, 6, False)
-        gather_dy(2, 0, True)
-        turn_dy(1, 0, 2, 7, False)
         weave_w(1, 0, True)
-        gather_dy(2, 1, False)
         weave_w(1, 1, True)
         quantize_w(1, 0)
         quantize_w(1, 1)
         for half in range(2):
             for pair in range(2):
                 first_product(1, half, pair)
-        gather_dy(3, 0, True)
-        gather_dy(3, 1, False)
-        turn_dy(0, 2, 2, 6, False)
-        for pair in range(2):
-            scale_units(1, 0, pair)
-            activate(1, 0, pair)
+        gate(0, 0, F_HALF)
+        gate(0, F_HALF, F)
+        quantize_h(0, 0, F_HALF)
+        quantize_h(0, F_HALF, F)
+        for k in range(1, E // P):
+            for b in range(EXPERTS):
+                gather_dy(k, b, False)
+        for half in range(2):
+            for pair in range(2):
+                scale_units(1, half, pair)
+        for half in range(2):
+            for b in range(EXPERTS):
+                turn_dy(2 * half, b, (6, 7, 1, 0)[2 * half + b])
+                turn_dy(2 * half + 1, b, (6, 7, 1, 0)[2 * half + b])
+        fetch_dy(0, 0, 6, True)
+        fetch_dy(1, 0, 7, True)
+        fetch_dy(0, 1, 1, True)
         quantize_dy(0)
-        for pair in range(2):
-            scale_units(1, 1, pair)
-            activate(1, 1, pair)
-        turn_dy(1, 2, 2, 2, False)
-        gate(1, 0)
-        for c in range(F // P):
-            second_product(0, c, (0, 1, 7, 6)[c], False)
+        fetch_dy(1, 1, 0, True)
+        for half in range(2):
+            for pair in range(2):
+                activate(1, half, pair)
+        gate(1, 0, F_HALF)
         quantize_dy(1)
-        gate(1, 1)
-        quantize_h(1, 0)
-        quantize_h(1, 1)
+        quantize_h(1, 0, F_HALF)
+        gate(1, 2 * P, 3 * P)
+        quantize_h(1, 2 * P, 3 * P)
+        gate(1, 3 * P, F)
+        quantize_h(1, 3 * P, F)
         for c in range(F // P):
-            second_product(1, c, (3, 2, 4, 5)[c], c % 2 == 0)
+            second_product(0, c, (2, 3, 4, 5)[c], False)
+        second_product(1, 0, 6, False)
+        second_product(1, 1, 7, False)
+        second_product(1, 2, 0, True)
+        second_product(1, 3, 1, False, 0, E // 2)
+        second_product(1, 3, 2, True, E // 2, E)

@@ -62,9 +62,11 @@ def tile_attend_gxfull_sil_W2_kernel(tc, xT, dyT, w1, ts, tx, cf, offs, out):
         ts_win = keep.tile([P, TOKENS], F32, name="ts_win")
         tx_win = keep.tile([P, TOKENS], F32, name="tx_win")
         ident = keep.tile([P, P], F32, name="ident")
-        nc.vector.memset(tx_win[:], 0.0)
-        nc.vector.memset(ts_win[:], 0.0)
-        nc.vector.tensor_copy(tx_win[0:1, :], tx_row[:])
+        nc.gpsimd.memset(ts_win[:], 0.0)
+        nc.vector.memset(tx_win[:, 0 : TOKENS - 1], 0.0)
+        nc.vector.memset(tx_win[:, TOKENS - 1 :], 0.0)
+        nc.vector.tensor_copy(tx_win[0:1, 0 : TOKENS // 2], tx_row[:, 0 : TOKENS // 2])
+        nc.scalar.activation(tx_win[0:1, TOKENS // 2 :], tx_row[:, TOKENS // 2 :], COPY)
         nc.vector.tensor_copy(ts_win[0:1, :], ts_row[:])
         make_identity(nc, ident[:])
 
@@ -93,10 +95,8 @@ def tile_attend_gxfull_sil_W2_kernel(tc, xT, dyT, w1, ts, tx, cf, offs, out):
         load_w(1)
         load_dy(1)
 
-        cf_all = keep.tile([P, F], F32, name="cf_all")
         for c in range(PACK):
             nc.tensor.transpose(banks[1][:, c * P : (c + 1) * P], cf_cols[:, c : c + 1].to_broadcast([P, P]), ident[:])
-        nc.scalar.copy(cf_all[:].rearrange("p (n c) -> p n c", c=PACK), banks[1][:].rearrange("p (c n) -> p n c", c=PACK))
 
         x_picked = {b: keep.tile([P, PACK, SLOTS], BF16, name=f"x_picked{b}") for b in range(EXPERTS)}
         x_in = {b: keep.tile([P, SLOTS * PACK], BF16, name=f"x_in{b}", align_bytes=64) for b in range(EXPERTS)}
@@ -114,6 +114,8 @@ def tile_attend_gxfull_sil_W2_kernel(tc, xT, dyT, w1, ts, tx, cf, offs, out):
 
         turn_slot_scales(tx_win, "tx", 0, False)
         turn_slot_scales(ts_win, "ts", EXPERTS * PACK, True)
+        cf_all = keep.tile([P, F], F32, name="tx_win")
+        nc.scalar.copy(cf_all[:].rearrange("p (n c) -> p n c", c=PACK), banks[1][:].rearrange("p (c n) -> p n c", c=PACK))
         tx_cols = slot_scales[:, 0 : EXPERTS * PACK].rearrange("p (b r) -> p b r", r=PACK)
         ts_cols = slot_scales[:, EXPERTS * PACK :].rearrange("p (b r) -> p b r", r=PACK)
 
@@ -215,9 +217,10 @@ def tile_attend_gxfull_sil_W2_kernel(tc, xT, dyT, w1, ts, tx, cf, offs, out):
         dy_in = {0: dy_stage[:, E * PACK // 2 :], 1: dy_stage[:, 0 : E * PACK]}
         dy_mx = {b: mx_tiles(f"dy{b}", E) for b in range(EXPERTS)}
 
-        def gather_dy(k, b, on_vector):
-            dy_picked[k, b] = keep.tile([P, SLOTS], BF16, name=f"dy_picked{k}{b}")
-            copy_on(on_vector, dy_picked[k, b][:], dy_win[k][:].indirect(slots_of(b)))
+        def gather_dy(k, b, on_vector, lo=0, hi=SLOTS):
+            if lo == 0:
+                dy_picked[k, b] = keep.tile([P, SLOTS], BF16, name=f"dy_picked{k}{b}")
+            copy_on(on_vector, dy_picked[k, b][:, lo:hi], dy_win[k][:].indirect(slots_of(b, lo, hi)))
 
         def turn_dy(k, b, bank_no):
             bank = banks[bank_no][:].rearrange("p (u e) -> p u e", u=2)

@@ -13,6 +13,7 @@ E5M2X4 = mybir.dt.float8_e5m2_x4
 COPY = mybir.ActivationFunctionType.Copy
 SILU = mybir.ActivationFunctionType.Silu
 MULT = mybir.AluOpType.mult
+ADD = mybir.AluOpType.add
 
 P = 128
 PACK = 4
@@ -100,7 +101,7 @@ def tile_attend_gxfull_sil_W2_kernel(tc, xT, dyT, w1, ts, tx, cf, offs, out):
 
         x_picked = {b: keep.tile([P, PACK, SLOTS], BF16, name=f"x_picked{b}") for b in range(EXPERTS)}
         x_in = {b: keep.tile([P, SLOTS * PACK], BF16, name=f"x_in{b}", align_bytes=64) for b in range(EXPERTS)}
-        slot_scales = x_in[0][:, 0 : 4 * EXPERTS * PACK].bitcast(F32)
+        slot_scales = x_in[0][:, 0 : 2 * EXPERTS * PACK].bitcast(F32)
 
         def turn_slot_scales(win, name, first_col, on_vector):
             picked = keep.tile([P, EXPERTS * SLOTS], F32, name=name + "_picked")
@@ -117,21 +118,17 @@ def tile_attend_gxfull_sil_W2_kernel(tc, xT, dyT, w1, ts, tx, cf, offs, out):
         cf_all = keep.tile([P, F], F32, name="tx_win")
         nc.scalar.copy(cf_all[:].rearrange("p (n c) -> p n c", c=PACK), banks[1][:].rearrange("p (c n) -> p n c", c=PACK))
         tx_cols = slot_scales[:, 0 : EXPERTS * PACK].rearrange("p (b r) -> p b r", r=PACK)
-        ts_cols = slot_scales[:, EXPERTS * PACK :].rearrange("p (b r) -> p b r", r=PACK)
+        ts_cols = banks[0][:, EXPERTS * PACK : 2 * EXPERTS * PACK].rearrange("p (b r) -> p b r", r=PACK)
 
         def fetch_slot_scales():
-            nc.scalar.copy(slot_scales, banks[0][:, 0 : 2 * EXPERTS * PACK])
+            nc.scalar.copy(slot_scales, banks[0][:, 0 : EXPERTS * PACK])
 
         def mx_tiles(name, width):
             codes = keep.tile([P, width], U32, name=name + "_codes", align_bytes=64)
             scales = keep.tile([P, width], U8, name=name + "_scales", align_bytes=64)
             return codes, scales
 
-        w_in = {
-            (b, half): keep.tile([P, F_HALF * PACK], BF16, name=f"w_in{b}{half}", align_bytes=64)
-            for b in range(EXPERTS)
-            for half in range(2)
-        }
+        w_in = {}
         x_codes = {}
         x_scales = {b: keep.tile([P, SLOTS], U8, name=f"x_scales{b}", align_bytes=64) for b in range(EXPERTS)}
         w_mx = {}
@@ -149,16 +146,21 @@ def tile_attend_gxfull_sil_W2_kernel(tc, xT, dyT, w1, ts, tx, cf, offs, out):
             x_codes[b] = keep.tile([P, SLOTS], U32, name=("x_codes0", "w_in00")[b], align_bytes=64)[:]
             nc.vector.quantize_mx(x_codes[b].bitcast(E4M3X4), x_scales[b][:], x_in[b][:])
 
-        def weave_w(b, half, on_vector):
-            copy_on(
-                on_vector,
-                w_in[b, half][:].rearrange("p (c i j) -> p c j i", i=4, j=PACK),
-                w_raw[b][:, :, half * F_HALF : (half + 1) * F_HALF].rearrange("p j (c i) -> p c j i", i=4),
-            )
+        def weave_w(b, lo, hi):
+            w_in[b, lo] = keep.tile([P, (hi - lo) * PACK], BF16, name=f"w_in{b}{lo}", align_bytes=64)
+            if b == 0:
+                dst = w_in[b, lo][:].rearrange("p (c i j) -> p c j i", i=4, j=PACK)
+                nc.scalar.activation(dst, w_raw[b][:, :, lo:hi].rearrange("p j (c i) -> p c j i", i=4), COPY)
+            else:
+                dst = w_in[b, lo][:].rearrange("p (c j) -> p c j", j=PACK)
+                nc.gpsimd.tensor_scalar(dst, w_raw[b][:, :, lo:hi].rearrange("p j c -> p c j"), 1.0, 0.0, MULT, ADD)
 
-        def quantize_w(b, half):
-            w_mx[b, half] = mx_tiles(f"w{b}{half}", F_HALF)
-            nc.vector.quantize_mx(w_mx[b, half][0][:].bitcast(E4M3X4), w_mx[b, half][1][:], w_in[b, half][:])
+        def quantize_w(b, lo, hi):
+            codes, scales = mx_tiles(f"w{b}{lo}", hi - lo)
+            nc.vector.quantize_mx(codes[:].bitcast(E4M3X4), scales[:], w_in[b, lo][:])
+            for first in range(lo, hi, F_HALF):
+                cols = slice(first - lo, first - lo + F_HALF)
+                w_mx[b, first // F_HALF] = (codes[:, cols], scales[:, cols])
 
         scaled, act = {}, {}
 
@@ -170,8 +172,8 @@ def tile_attend_gxfull_sil_W2_kernel(tc, xT, dyT, w1, ts, tx, cf, offs, out):
                     bank[:, rr, :],
                     lhsT=x_codes[b][:, cols].bitcast(E4M3X4),
                     lhsT_scale=x_scales[b][:, cols],
-                    rhs=w_mx[b, half][0][:].bitcast(E4M3X4),
-                    rhs_scale=w_mx[b, half][1][:],
+                    rhs=w_mx[b, half][0].bitcast(E4M3X4),
+                    rhs_scale=w_mx[b, half][1],
                     start=True,
                     stop=True,
                 )
@@ -268,14 +270,14 @@ def tile_attend_gxfull_sil_W2_kernel(tc, xT, dyT, w1, ts, tx, cf, offs, out):
         gather_x(3, 0, False, SLOTS // 2, SLOTS)
         gather_x(3, 1, False)
         weave_x(0)
-        weave_w(0, 0, False)
-        weave_w(0, 1, False)
+        weave_w(0, 0, F_HALF)
+        weave_w(0, F_HALF, F)
         weave_x(1)
         quantize_x(0)
         fetch_slot_scales()
-        quantize_w(0, 0)
+        quantize_w(0, 0, F_HALF)
         quantize_x(1)
-        quantize_w(0, 1)
+        quantize_w(0, F_HALF, F)
         for half in range(2):
             for pair in range(2):
                 first_product(0, half, pair)
@@ -285,18 +287,19 @@ def tile_attend_gxfull_sil_W2_kernel(tc, xT, dyT, w1, ts, tx, cf, offs, out):
             for pair in range(2):
                 scale_units(0, half, pair)
                 activate(0, half, pair)
-        weave_w(1, 0, True)
-        weave_w(1, 1, True)
-        quantize_w(1, 0)
-        quantize_w(1, 1)
+        weave_w(1, 0, F)
+        gate(0, 0, F_HALF)
+        gate(0, F_HALF, F)
+        quantize_w(1, 0, F)
         for half in range(2):
             for pair in range(2):
                 first_product(1, half, pair)
-        gate(0, 0, F_HALF)
-        gate(0, F_HALF, F)
         quantize_h(0, 0, F_HALF)
         quantize_h(0, F_HALF, F)
-        for k in range(1, E // P):
+        gather_dy(1, 0, False)
+        gather_dy(1, 1, False, 0, SLOTS // 2)
+        gather_dy(1, 1, True, SLOTS // 2, SLOTS)
+        for k in range(2, E // P):
             for b in range(EXPERTS):
                 gather_dy(k, b, False)
         for half in range(2):
@@ -304,27 +307,27 @@ def tile_attend_gxfull_sil_W2_kernel(tc, xT, dyT, w1, ts, tx, cf, offs, out):
                 scale_units(1, half, pair)
         for half in range(2):
             for b in range(EXPERTS):
-                turn_dy(2 * half, b, (6, 7, 1, 0)[2 * half + b])
-                turn_dy(2 * half + 1, b, (6, 7, 1, 0)[2 * half + b])
+                turn_dy(2 * half, b, (6, 7, 1, 2)[2 * half + b])
+                turn_dy(2 * half + 1, b, (6, 7, 1, 2)[2 * half + b])
         fetch_dy(0, 0, 6, True)
         fetch_dy(1, 0, 7, True)
         fetch_dy(0, 1, 1, True)
         quantize_dy(0)
-        fetch_dy(1, 1, 0, True)
         for half in range(2):
             for pair in range(2):
                 activate(1, half, pair)
         gate(1, 0, F_HALF)
-        quantize_dy(1)
+        fetch_dy(1, 1, 2, True)
         quantize_h(1, 0, F_HALF)
+        quantize_dy(1)
         gate(1, 2 * P, 3 * P)
         quantize_h(1, 2 * P, 3 * P)
         gate(1, 3 * P, F)
         quantize_h(1, 3 * P, F)
         for c in range(F // P):
-            second_product(0, c, (2, 3, 4, 5)[c], False)
-        second_product(1, 0, 6, False)
-        second_product(1, 1, 7, False)
-        second_product(1, 2, 0, True)
-        second_product(1, 3, 1, False, 0, E // 2)
-        second_product(1, 3, 2, True, E // 2, E)
+            second_product(0, c, (3, 4, 5, 6)[c], False)
+        second_product(1, 0, 7, False)
+        second_product(1, 1, 1, False)
+        second_product(1, 2, 2, True)
+        second_product(1, 3, 3, False, 0, E // 2)
+        second_product(1, 3, 4, True, E // 2, E)

@@ -61,7 +61,7 @@ def tile_attend_gxfull_sil_W2_kernel(tc, xT, dyT, w1, ts, tx, cf, offs, out):
         nc.scalar.activation(warm[:, 1:2], warm[:, 0:1], SILU)
 
         ts_win = keep.tile([P, TOKENS], F32, name="ts_win")
-        tx_win = keep.tile([P, TOKENS], F32, name="tx_win")
+        tx_win = keep.tile([P, TOKENS], F32, name="tx_win", align_bytes=64)
         ident = keep.tile([P, P], F32, name="ident")
         nc.gpsimd.memset(ts_win[:], 0.0)
         nc.vector.memset(tx_win[:, 0 : TOKENS - 1], 0.0)
@@ -101,7 +101,7 @@ def tile_attend_gxfull_sil_W2_kernel(tc, xT, dyT, w1, ts, tx, cf, offs, out):
 
         x_picked = {b: keep.tile([P, PACK, SLOTS], BF16, name=f"x_picked{b}") for b in range(EXPERTS)}
         x_in = {b: keep.tile([P, SLOTS * PACK], BF16, name=f"x_in{b}", align_bytes=64) for b in range(EXPERTS)}
-        slot_scales = x_in[0][:, 0 : 2 * EXPERTS * PACK].bitcast(F32)
+        slot_scales = x_in[0][:, 0 : 4 * EXPERTS * PACK].bitcast(F32)
 
         def turn_slot_scales(win, name, first_col, on_vector):
             picked = keep.tile([P, EXPERTS * SLOTS], F32, name=name + "_picked")
@@ -115,13 +115,14 @@ def tile_attend_gxfull_sil_W2_kernel(tc, xT, dyT, w1, ts, tx, cf, offs, out):
 
         turn_slot_scales(tx_win, "tx", 0, False)
         turn_slot_scales(ts_win, "ts", EXPERTS * PACK, True)
-        cf_all = keep.tile([P, F], F32, name="tx_win")
+        cf_all = keep.tile([P, F], F32, name="tx_win", align_bytes=64)
         nc.scalar.copy(cf_all[:].rearrange("p (n c) -> p n c", c=PACK), banks[1][:].rearrange("p (c n) -> p n c", c=PACK))
         tx_cols = slot_scales[:, 0 : EXPERTS * PACK].rearrange("p (b r) -> p b r", r=PACK)
+        ts_rows = slot_scales[:, EXPERTS * PACK :].rearrange("p (b r) -> p b r", r=PACK)
         ts_cols = banks[0][:, EXPERTS * PACK : 2 * EXPERTS * PACK].rearrange("p (b r) -> p b r", r=PACK)
 
         def fetch_slot_scales():
-            nc.scalar.copy(slot_scales, banks[0][:, 0 : EXPERTS * PACK])
+            nc.scalar.copy(slot_scales, banks[0][:, 0 : 2 * EXPERTS * PACK])
 
         def mx_tiles(name, width):
             codes = keep.tile([P, width], U32, name=name + "_codes", align_bytes=64)
@@ -129,6 +130,7 @@ def tile_attend_gxfull_sil_W2_kernel(tc, xT, dyT, w1, ts, tx, cf, offs, out):
             return codes, scales
 
         w_in = {}
+        w_then_h = keep.tile([P, 3 * F_HALF * PACK], BF16, name="w_then_h", align_bytes=64)
         x_codes = {}
         x_scales = {b: keep.tile([P, SLOTS], U8, name=f"x_scales{b}", align_bytes=64) for b in range(EXPERTS)}
         w_mx = {}
@@ -147,17 +149,18 @@ def tile_attend_gxfull_sil_W2_kernel(tc, xT, dyT, w1, ts, tx, cf, offs, out):
             nc.vector.quantize_mx(x_codes[b].bitcast(E4M3X4), x_scales[b][:], x_in[b][:])
 
         def weave_w(b, lo, hi):
-            w_in[b, lo] = keep.tile([P, (hi - lo) * PACK], BF16, name=f"w_in{b}{lo}", align_bytes=64)
             if b == 0:
-                dst = w_in[b, lo][:].rearrange("p (c i j) -> p c j i", i=4, j=PACK)
+                w_in[b, lo] = keep.tile([P, (hi - lo) * PACK], BF16, name=f"w_in{b}{lo}", align_bytes=64)[:]
+                dst = w_in[b, lo].rearrange("p (c i j) -> p c j i", i=4, j=PACK)
                 nc.scalar.activation(dst, w_raw[b][:, :, lo:hi].rearrange("p j (c i) -> p c j i", i=4), COPY)
             else:
-                dst = w_in[b, lo][:].rearrange("p (c j) -> p c j", j=PACK)
+                w_in[b, lo] = w_then_h[:, F_HALF * PACK :]
+                dst = w_in[b, lo].rearrange("p (c j) -> p c j", j=PACK)
                 nc.gpsimd.tensor_scalar(dst, w_raw[b][:, :, lo:hi].rearrange("p j c -> p c j"), 1.0, 0.0, MULT, ADD)
 
         def quantize_w(b, lo, hi):
             codes, scales = mx_tiles(f"w{b}{lo}", hi - lo)
-            nc.vector.quantize_mx(codes[:].bitcast(E4M3X4), scales[:], w_in[b, lo][:])
+            nc.vector.quantize_mx(codes[:].bitcast(E4M3X4), scales[:], w_in[b, lo])
             for first in range(lo, hi, F_HALF):
                 cols = slice(first - lo, first - lo + F_HALF)
                 w_mx[b, first // F_HALF] = (codes[:, cols], scales[:, cols])
@@ -197,8 +200,16 @@ def tile_attend_gxfull_sil_W2_kernel(tc, xT, dyT, w1, ts, tx, cf, offs, out):
                     act[b][:, half, r, :], scaled[b, half, pair][:, rr, :], SILU, scale=tx_cols[:, b, r : r + 1]
                 )
 
-        h_in = {b: keep.tile([P, F * PACK], BF16, name=f"h_in{b}", align_bytes=64) for b in range(EXPERTS)}
-        h_mx = {b: mx_tiles(f"h{b}", F) for b in range(EXPERTS)}
+        h_in = {0: w_then_h[:, 0 : F * PACK], 1: keep.tile([P, F * PACK], BF16, name="h_in1", align_bytes=64)[:]}
+        h_mx = {1: mx_tiles("h1", F)}
+
+        def gate_on_gpsimd(b, half):
+            nc.gpsimd.tensor_tensor(
+                h_in[b][:, half * F_HALF * PACK : (half + 1) * F_HALF * PACK].rearrange("p (c r) -> p c r", r=PACK),
+                act[b][:, half, :, :].rearrange("p r c -> p c r"),
+                ts_rows[:, b, :].unsqueeze(1).broadcast_to([P, F_HALF, PACK]),
+                MULT,
+            )
 
         def gate(b, lo, hi):
             half, first = divmod(lo, F_HALF)
@@ -210,6 +221,9 @@ def tile_attend_gxfull_sil_W2_kernel(tc, xT, dyT, w1, ts, tx, cf, offs, out):
             )
 
         def quantize_h(b, lo, hi):
+            if b not in h_mx:
+                codes = keep.tile([P, F], U32, name="tx_win", align_bytes=64)
+                h_mx[b] = (codes, keep.tile([P, F], U8, name="h0_scales", align_bytes=64))
             nc.vector.quantize_mx(
                 h_mx[b][0][:, lo:hi].bitcast(E4M3X4), h_mx[b][1][:, lo:hi], h_in[b][:, lo * PACK : hi * PACK]
             )
@@ -282,23 +296,21 @@ def tile_attend_gxfull_sil_W2_kernel(tc, xT, dyT, w1, ts, tx, cf, offs, out):
             for pair in range(2):
                 first_product(0, half, pair)
         gather_dy(0, 0, False)
-        gather_dy(0, 1, False)
+        gather_dy(0, 1, False, 0, SLOTS // 2)
         for half in range(2):
             for pair in range(2):
                 scale_units(0, half, pair)
                 activate(0, half, pair)
+        gather_dy(0, 1, True, SLOTS // 2, SLOTS)
         weave_w(1, 0, F)
         gate(0, 0, F_HALF)
-        gate(0, F_HALF, F)
         quantize_w(1, 0, F)
+        gate_on_gpsimd(0, 1)
         for half in range(2):
             for pair in range(2):
                 first_product(1, half, pair)
-        quantize_h(0, 0, F_HALF)
-        quantize_h(0, F_HALF, F)
         gather_dy(1, 0, False)
-        gather_dy(1, 1, False, 0, SLOTS // 2)
-        gather_dy(1, 1, True, SLOTS // 2, SLOTS)
+        gather_dy(1, 1, True)
         for k in range(2, E // P):
             for b in range(EXPERTS):
                 gather_dy(k, b, False)
@@ -310,6 +322,7 @@ def tile_attend_gxfull_sil_W2_kernel(tc, xT, dyT, w1, ts, tx, cf, offs, out):
                 turn_dy(2 * half, b, (6, 7, 1, 2)[2 * half + b])
                 turn_dy(2 * half + 1, b, (6, 7, 1, 2)[2 * half + b])
         fetch_dy(0, 0, 6, True)
+        quantize_h(0, 0, F)
         fetch_dy(1, 0, 7, True)
         fetch_dy(0, 1, 1, True)
         quantize_dy(0)

@@ -24,7 +24,8 @@ D = 512
 F = 512
 E = 512
 LIST_COLS = SLOTS // 16
-F_HALF = F // 2
+HALF = 256
+BYTES_OF = {F32: 4, BF16: 2, U32: 4, U8: 1}
 
 FLOPS = 2 * EXPERTS * SLOTS * F * (D + E)
 BYTES = 4 * (D * TOKENS + E * TOKENS + EXPERTS * D * F + 2 * TOKENS + F + EXPERTS * F * E) + 2 * P * EXPERTS * LIST_COLS
@@ -34,15 +35,28 @@ def tile_attend_gxfull_sil_W2_kernel(tc, xT, dyT, w1, ts, tx, cf, offs, out):
     nc = tc.nc
     with ExitStack() as ctx:
         keep = ctx.enter_context(tc.tile_pool(name="keep", bufs=1))
-        windows = ctx.enter_context(tc.tile_pool(name="windows", bufs=6))
         psum = ctx.enter_context(tc.psum_pool(name="psum", bufs=1))
         banks = [psum.tile([P, 512], F32, name=f"bank{n}") for n in range(8)]
 
+        arena = ctx.enter_context(tc.tile_pool(name="arena", bufs=1))
+        place = {"end": 0}
+
+        def new(shape, dtype, name, over=None):
+            if over is None:
+                place[name] = place["end"]
+                size = BYTES_OF[dtype]
+                for extent in shape[1:]:
+                    size = size * extent
+                place["end"] = place["end"] + -(-size // 64) * 64
+            else:
+                place[name] = place[over[0]] + 1024 * over[1]
+            return arena.tile(shape, dtype, name=name, align_bytes=64, offset=place[name])
+
         offsets = keep.tile([P, EXPERTS * LIST_COLS], U16, name="offsets")
         nc.sync.dma_start(offsets[:], offs)
-        tx_row = keep.tile([1, TOKENS], F32, name="tx_row")
-        ts_row = keep.tile([1, TOKENS], F32, name="ts_row")
-        cf_cols = keep.tile([P, PACK], F32, name="cf_cols")
+        tx_row = new([1, TOKENS], F32, "tx_row")
+        ts_row = new([1, TOKENS], F32, "ts_row")
+        cf_cols = new([P, PACK], F32, "cf_cols")
         nc.scalar.dma_start(tx_row[:], tx[0:1, :])
         nc.sync.dma_start(ts_row[:], ts[0:1, :])
         nc.scalar.dma_start(cf_cols[:], cf.rearrange("(p c) o -> p (c o)", c=PACK))
@@ -56,13 +70,19 @@ def tile_attend_gxfull_sil_W2_kernel(tc, xT, dyT, w1, ts, tx, cf, offs, out):
             else:
                 nc.scalar.activation(dst, src, COPY)
 
-        warm = keep.tile([P, 2], F32, name="warm")
+        def move_on(on_vector, dst, src):
+            if on_vector:
+                nc.vector.tensor_copy(dst, src)
+            else:
+                nc.scalar.copy(dst, src)
+
+        warm = new([P, 2], F32, "warm")
         nc.vector.memset(warm[:, 0:1], 0.0)
         nc.scalar.activation(warm[:, 1:2], warm[:, 0:1], SILU)
 
-        ts_win = keep.tile([P, TOKENS], F32, name="ts_win")
-        tx_win = keep.tile([P, TOKENS], F32, name="tx_win", align_bytes=64)
-        ident = keep.tile([P, P], F32, name="ident")
+        ts_win = new([P, TOKENS], F32, "ts_win")
+        tx_win = new([P, TOKENS], F32, "tx_win")
+        ident = new([P, P], F32, "ident")
         nc.gpsimd.memset(ts_win[:], 0.0)
         nc.vector.memset(tx_win[:, 0 : TOKENS - 1], 0.0)
         nc.vector.memset(tx_win[:, TOKENS - 1 :], 0.0)
@@ -75,167 +95,167 @@ def tile_attend_gxfull_sil_W2_kernel(tc, xT, dyT, w1, ts, tx, cf, offs, out):
         x_win, w_raw, dy_win = {}, {}, {}
 
         def load_x(j):
-            x_win[j] = windows.tile([P, TOKENS], F32, name="window")
+            x_win[j] = new([P, TOKENS], F32, f"x_win{j}")
             nc.sync.dma_start(x_win[j][:], x_rows[:, j, :])
 
         def load_w(b):
-            w_raw[b] = keep.tile([P, PACK, F], F32, name=f"w_raw{b}")
+            w_raw[b] = new([P, PACK, F], F32, f"w_raw{b}")
             nc.sync.dma_start(w_raw[b][:], w1[b].rearrange("(p j) f -> p j f", j=PACK))
 
         def load_dy(k):
-            if k == E // P - 1:
-                dy_win[k] = keep.tile([P, TOKENS], F32, name="last_window")
-            else:
-                dy_win[k] = windows.tile([P, TOKENS], F32, name="window")
+            dy_win[k] = new([P, TOKENS], F32, f"dy_win{k}")
             nc.sync.dma_start(dy_win[k][:], dyT[k * P : (k + 1) * P, :])
 
-        for j in range(PACK):
-            load_x(j)
-        load_w(0)
-        load_dy(0)
-        load_w(1)
-        load_dy(1)
+        def turn_cf():
+            for c in range(PACK):
+                nc.tensor.transpose(banks[1][:, c * P : (c + 1) * P], cf_cols[:, c : c + 1].to_broadcast([P, P]), ident[:])
 
-        for c in range(PACK):
-            nc.tensor.transpose(banks[1][:, c * P : (c + 1) * P], cf_cols[:, c : c + 1].to_broadcast([P, P]), ident[:])
-
-        x_picked = {b: keep.tile([P, PACK, SLOTS], BF16, name=f"x_picked{b}") for b in range(EXPERTS)}
-        x_in = {b: keep.tile([P, SLOTS * PACK], BF16, name=f"x_in{b}", align_bytes=64) for b in range(EXPERTS)}
-        slot_scales = x_in[0][:, 0 : 4 * EXPERTS * PACK].bitcast(F32)
-
-        def turn_slot_scales(win, name, first_col, on_vector):
-            picked = keep.tile([P, EXPERTS * SLOTS], F32, name=name + "_picked")
-            copy_on(on_vector, picked[:], win[:].indirect(offsets[:]))
-            for b in range(EXPERTS):
+        def turn_slot_scales(win, name, first_col, b_lo, b_hi, on_vector):
+            count = (b_hi - b_lo) * SLOTS
+            picked = new([P, count], F32, name)
+            copy_on(on_vector, picked[:], win[:].indirect(slots_of(b_lo, 0, count)))
+            for b in range(b_lo, b_hi):
                 for r in range(PACK):
                     col = first_col + b * PACK + r
-                    nc.tensor.transpose(
-                        banks[0][:, col : col + P], picked[:, b * SLOTS + r : (b + 1) * SLOTS : PACK], ident[:]
-                    )
+                    first = (b - b_lo) * SLOTS
+                    nc.tensor.transpose(banks[0][:, col : col + P], picked[:, first + r : first + SLOTS : PACK], ident[:])
 
-        turn_slot_scales(tx_win, "tx", 0, False)
-        turn_slot_scales(ts_win, "ts", EXPERTS * PACK, True)
-        cf_all = keep.tile([P, F], F32, name="tx_win", align_bytes=64)
-        nc.scalar.copy(cf_all[:].rearrange("p (n c) -> p n c", c=PACK), banks[1][:].rearrange("p (c n) -> p n c", c=PACK))
-        tx_cols = slot_scales[:, 0 : EXPERTS * PACK].rearrange("p (b r) -> p b r", r=PACK)
-        ts_rows = slot_scales[:, EXPERTS * PACK :].rearrange("p (b r) -> p b r", r=PACK)
+        spread = {}
+
+        def fetch_cf(on_vector, over=None):
+            spread["cf"] = new([P, F], F32, "cf_all", over)
+            dst = spread["cf"][:].rearrange("p (n c) -> p n c", c=PACK)
+            move_on(on_vector, dst, banks[1][:].rearrange("p (c n) -> p n c", c=PACK))
+
         ts_cols = banks[0][:, EXPERTS * PACK : 2 * EXPERTS * PACK].rearrange("p (b r) -> p b r", r=PACK)
 
-        def fetch_slot_scales():
-            nc.scalar.copy(slot_scales, banks[0][:, 0 : 2 * EXPERTS * PACK])
+        def fetch_slot_scales(on_vector, over=None):
+            both = new([P, 2 * EXPERTS * PACK], F32, "slot_scales", over)
+            move_on(on_vector, both[:], banks[0][:, 0 : 2 * EXPERTS * PACK])
+            spread["tx"] = both[:, 0 : EXPERTS * PACK].rearrange("p (b r) -> p b r", r=PACK)
+            spread["ts"] = both[:, EXPERTS * PACK :].rearrange("p (b r) -> p b r", r=PACK)
 
-        def mx_tiles(name, width):
-            codes = keep.tile([P, width], U32, name=name + "_codes", align_bytes=64)
-            scales = keep.tile([P, width], U8, name=name + "_scales", align_bytes=64)
+        def quantize(src, name, fmt, over):
+            width = src.shape[1] // PACK
+            codes = new([P, width], U32, name + "_codes", over)
+            scales = new([P, width], U8, name + "_scales")
+            nc.vector.quantize_mx(codes[:].bitcast(fmt), scales[:], src)
             return codes, scales
 
-        w_in = {}
-        w_then_h = keep.tile([P, 3 * F_HALF * PACK], BF16, name="w_then_h", align_bytes=64)
-        x_codes = {}
-        x_scales = {b: keep.tile([P, SLOTS], U8, name=f"x_scales{b}", align_bytes=64) for b in range(EXPERTS)}
-        w_mx = {}
+        x_in = {0: new([P, SLOTS * PACK], BF16, "x_in0")}
+        x_picked = new([P, PACK, SLOTS], BF16, "x_picked")
+        x_mx, w_in, w_mx = {}, {}, {}
 
-        def gather_x(j, b, on_vector, lo=0, hi=SLOTS):
-            copy_on(on_vector, x_picked[b][:, j, lo:hi], x_win[j][:].indirect(slots_of(b, lo, hi)))
+        def gather_x_in_place(j):
+            dst = x_in[0][:].rearrange("p (r s j) -> p j s r", r=PACK, j=PACK)[:, j, :, :]
+            nc.vector.tensor_copy(dst, x_win[j][:].indirect(slots_of(0)))
 
-        def weave_x(b):
-            nc.vector.tensor_copy(
-                x_in[b][:].rearrange("p (r s h j) -> p s j h r", r=PACK, h=2, j=PACK),
-                x_picked[b][:].rearrange("p j (s h r) -> p s j h r", h=2, r=PACK),
-            )
+        def gather_x(j):
+            nc.scalar.activation(x_picked[:, j, :], x_win[j][:].indirect(slots_of(1)), COPY)
 
-        def quantize_x(b):
-            x_codes[b] = keep.tile([P, SLOTS], U32, name=("x_codes0", "w_in00")[b], align_bytes=64)[:]
-            nc.vector.quantize_mx(x_codes[b].bitcast(E4M3X4), x_scales[b][:], x_in[b][:])
+        def weave_x(pair, over=None):
+            x_in[1, pair] = new([P, SLOTS * PACK // 2], BF16, f"x_in1{pair}", over)
+            dst = x_in[1, pair][:].rearrange("p (r s h j) -> p s j h r", r=2, h=2, j=PACK)
+            src = x_picked[:].rearrange("p j (s h r) -> p s j h r", h=2, r=PACK)
+            nc.scalar.copy(dst, src[:, :, :, :, 2 * pair : 2 * pair + 2])
 
-        def weave_w(b, lo, hi):
-            if b == 0:
-                w_in[b, lo] = keep.tile([P, (hi - lo) * PACK], BF16, name=f"w_in{b}{lo}", align_bytes=64)[:]
-                dst = w_in[b, lo].rearrange("p (c i j) -> p c j i", i=4, j=PACK)
-                nc.scalar.activation(dst, w_raw[b][:, :, lo:hi].rearrange("p j (c i) -> p c j i", i=4), COPY)
-            else:
-                w_in[b, lo] = w_then_h[:, F_HALF * PACK :]
+        def quantize_x0():
+            codes, scales = quantize(x_in[0][:], "x0", E4M3X4, None)
+            for pair in range(2):
+                x_mx[0, pair] = (codes[:, pair * HALF : (pair + 1) * HALF], scales[:, pair * HALF : (pair + 1) * HALF])
+
+        def quantize_x1(pair, over=None):
+            x_mx[1, pair] = quantize(x_in[1, pair][:], f"x1{pair}", E4M3X4, over)
+
+        def weave_w(b, lo, hi, engine, over=None):
+            w_in[b, lo] = new([P, (hi - lo) * PACK], BF16, f"w_in{b}{lo}", over)[:]
+            if engine == "gpsimd":
                 dst = w_in[b, lo].rearrange("p (c j) -> p c j", j=PACK)
                 nc.gpsimd.tensor_scalar(dst, w_raw[b][:, :, lo:hi].rearrange("p j c -> p c j"), 1.0, 0.0, MULT, ADD)
+            else:
+                dst = w_in[b, lo].rearrange("p (c i j) -> p c j i", i=4, j=PACK)
+                copy_on(engine == "vector", dst, w_raw[b][:, :, lo:hi].rearrange("p j (c i) -> p c j i", i=4))
 
-        def quantize_w(b, lo, hi):
-            codes, scales = mx_tiles(f"w{b}{lo}", hi - lo)
-            nc.vector.quantize_mx(codes[:].bitcast(E4M3X4), scales[:], w_in[b, lo])
-            for first in range(lo, hi, F_HALF):
-                cols = slice(first - lo, first - lo + F_HALF)
-                w_mx[b, first // F_HALF] = (codes[:, cols], scales[:, cols])
+        def quantize_w(b, lo, hi, over=None):
+            codes, scales = quantize(w_in[b, lo], f"w{b}{lo}", E4M3X4, over)
+            for first in range(lo, hi, HALF):
+                cols = slice(first - lo, first - lo + HALF)
+                w_mx[b, first // HALF] = (codes[:, cols], scales[:, cols])
+
+        def product(acc, stationary, cols, moving, fmt):
+            nc.tensor.matmul_mx(
+                acc,
+                lhsT=stationary[0][:, cols].bitcast(E4M3X4),
+                lhsT_scale=stationary[1][:, cols],
+                rhs=moving[0].bitcast(fmt),
+                rhs_scale=moving[1],
+                start=True,
+                stop=True,
+            )
 
         scaled, act = {}, {}
 
-        def first_product(b, half, pair):
-            bank = banks[2 + 2 * half + pair][:].rearrange("p (r f) -> p r f", r=2)
+        def first_product(b, half, pair, bank_no):
+            bank = banks[bank_no][:].rearrange("p (r f) -> p r f", r=2)
             for rr in range(2):
-                cols = slice((2 * pair + rr) * P, (2 * pair + rr + 1) * P)
-                nc.tensor.matmul_mx(
-                    bank[:, rr, :],
-                    lhsT=x_codes[b][:, cols].bitcast(E4M3X4),
-                    lhsT_scale=x_scales[b][:, cols],
-                    rhs=w_mx[b, half][0].bitcast(E4M3X4),
-                    rhs_scale=w_mx[b, half][1],
-                    start=True,
-                    stop=True,
-                )
+                product(bank[:, rr, :], x_mx[b, pair], slice(rr * P, (rr + 1) * P), w_mx[b, half], E4M3X4)
 
-        def scale_units(b, half, pair):
-            bank = banks[2 + 2 * half + pair][:].rearrange("p (r f) -> p r f", r=2)
-            if (b, half) == (0, 0):
-                spent = x_in[1][:].bitcast(F32).rearrange("p (q r f) -> p q r f", q=2, r=2)
-                scaled[b, half, pair] = spent[:, pair, :, :]
-            else:
-                scaled[b, half, pair] = keep.tile([P, 2, F_HALF], F32, name=f"scaled{b}{half}{pair}")[:]
-            cf_half = cf_all[:, half * F_HALF : (half + 1) * F_HALF].unsqueeze(1).broadcast_to([P, 2, F_HALF])
+        def scale_units(b, half, pair, bank_no, over=None):
+            bank = banks[bank_no][:].rearrange("p (r f) -> p r f", r=2)
+            scaled[b, half, pair] = new([P, 2, HALF], F32, f"scaled{b}{half}{pair}", over)[:]
+            cf_half = spread["cf"][:, half * HALF : (half + 1) * HALF].unsqueeze(1).broadcast_to([P, 2, HALF])
             nc.vector.tensor_tensor(scaled[b, half, pair], bank, cf_half, MULT)
 
-        def activate(b, half, pair):
-            if half == 0 and pair == 0:
-                act[b] = keep.tile([P, 2, PACK, F_HALF], F32, name="last_window" if b == EXPERTS - 1 else "act")
+        def activate(b, half, pair, over=None):
+            if pair == 0:
+                act[b, half] = new([P, PACK, HALF], F32, f"act{b}{half}", over)
             for rr in range(2):
                 r = 2 * pair + rr
                 nc.scalar.activation(
-                    act[b][:, half, r, :], scaled[b, half, pair][:, rr, :], SILU, scale=tx_cols[:, b, r : r + 1]
+                    act[b, half][:, r, :], scaled[b, half, pair][:, rr, :], SILU, scale=spread["tx"][:, b, r : r + 1]
                 )
 
-        h_in = {0: w_then_h[:, 0 : F * PACK], 1: keep.tile([P, F * PACK], BF16, name="h_in1", align_bytes=64)[:]}
-        h_mx = {1: mx_tiles("h1", F)}
+        h_in, h_mx = {}, {}
 
-        def gate_on_gpsimd(b, half):
+        def gate_on_gpsimd(b, half, dst):
             nc.gpsimd.tensor_tensor(
-                h_in[b][:, half * F_HALF * PACK : (half + 1) * F_HALF * PACK].rearrange("p (c r) -> p c r", r=PACK),
-                act[b][:, half, :, :].rearrange("p r c -> p c r"),
-                ts_rows[:, b, :].unsqueeze(1).broadcast_to([P, F_HALF, PACK]),
+                dst.rearrange("p (c r) -> p c r", r=PACK),
+                act[b, half][:].rearrange("p r c -> p c r"),
+                spread["ts"][:, b, :].unsqueeze(1).broadcast_to([P, HALF, PACK]),
                 MULT,
             )
 
-        def gate(b, lo, hi):
-            half, first = divmod(lo, F_HALF)
+        def gate_expert0(over):
+            h_in[0] = new([P, F * PACK], BF16, "h_in0", over)
+            for half in range(2):
+                gate_on_gpsimd(0, half, h_in[0][:, half * HALF * PACK : (half + 1) * HALF * PACK])
+
+        def gate_last(over):
+            h_in[1, 1] = new([P, HALF * PACK], BF16, "h_in11", over)
+            gate_on_gpsimd(1, 1, h_in[1, 1][:])
+
+        def gate(half, over=None):
+            h_in[1, half] = new([P, HALF * PACK], BF16, f"h_in1{half}", over)
             nc.vector.tensor_tensor(
-                h_in[b][:, lo * PACK : hi * PACK].rearrange("p (c i r) -> p c r i", i=4, r=PACK),
-                act[b][:, half, :, first : first + hi - lo].rearrange("p r (c i) -> p c r i", i=4),
-                ts_cols[:, b, :].unsqueeze(1).unsqueeze(3).broadcast_to([P, (hi - lo) // 4, PACK, 4]),
+                h_in[1, half][:].rearrange("p (c i r) -> p c r i", i=4, r=PACK),
+                act[1, half][:].rearrange("p r (c i) -> p c r i", i=4),
+                ts_cols[:, 1, :].unsqueeze(1).unsqueeze(3).broadcast_to([P, HALF // 4, PACK, 4]),
                 MULT,
             )
 
-        def quantize_h(b, lo, hi):
-            if b not in h_mx:
-                codes = keep.tile([P, F], U32, name="tx_win", align_bytes=64)
-                h_mx[b] = (codes, keep.tile([P, F], U8, name="h0_scales", align_bytes=64))
-            nc.vector.quantize_mx(
-                h_mx[b][0][:, lo:hi].bitcast(E4M3X4), h_mx[b][1][:, lo:hi], h_in[b][:, lo * PACK : hi * PACK]
-            )
+        def quantize_h0(over):
+            codes, scales = quantize(h_in[0][:], "h0", E4M3X4, over)
+            for half in range(2):
+                h_mx[0, half] = (codes[:, half * HALF : (half + 1) * HALF], scales[:, half * HALF : (half + 1) * HALF])
 
-        dy_picked = {}
-        dy_stage = keep.tile([P, 3 * E * PACK // 2], BF16, name="dy_stage", align_bytes=64)
-        dy_in = {0: dy_stage[:, E * PACK // 2 :], 1: dy_stage[:, 0 : E * PACK]}
-        dy_mx = {b: mx_tiles(f"dy{b}", E) for b in range(EXPERTS)}
+        def quantize_h1(half, over=None):
+            h_mx[1, half] = quantize(h_in[1, half][:], f"h1{half}", E4M3X4, over)
 
-        def gather_dy(k, b, on_vector, lo=0, hi=SLOTS):
-            if lo == 0:
-                dy_picked[k, b] = keep.tile([P, SLOTS], BF16, name=f"dy_picked{k}{b}")
+        dy_picked, dy_in, dy_mx = {}, {}, {}
+
+        def gather_dy(k, b, on_vector, lo=0, hi=SLOTS, over=None):
+            if (k, b) not in dy_picked:
+                dy_picked[k, b] = new([P, SLOTS], BF16, f"dy_picked{k}{b}", over)
             copy_on(on_vector, dy_picked[k, b][:, lo:hi], dy_win[k][:].indirect(slots_of(b, lo, hi)))
 
         def turn_dy(k, b, bank_no):
@@ -244,103 +264,121 @@ def tile_attend_gxfull_sil_W2_kernel(tc, xT, dyT, w1, ts, tx, cf, offs, out):
             for u in range(2):
                 nc.tensor.transpose(bank[:, u, (k % 2) * P : (k % 2 + 1) * P], words[:, u : SLOTS // 2 : 2], ident[:])
 
-        def fetch_dy(b, half, bank_no, on_vector):
-            dst = dy_in[b][:, half * 2 * P * PACK : (half + 1) * 2 * P * PACK].bitcast(F32)
-            dst = dst.rearrange("p (g i u) -> p g u i", i=2, u=2)
-            src = banks[bank_no][:].rearrange("p (u g i) -> p g u i", u=2, i=2)
-            if on_vector:
-                nc.vector.tensor_copy(dst, src)
-            else:
-                nc.scalar.copy(dst, src)
+        def fetch_dy(b, half, bank_no, on_vector, over=None):
+            dy_in[b, half] = new([P, HALF * PACK], BF16, f"dy_in{b}{half}", over)[:]
+            dst = dy_in[b, half].bitcast(F32).rearrange("p (g i u) -> p g u i", i=2, u=2)
+            move_on(on_vector, dst, banks[bank_no][:].rearrange("p (u g i) -> p g u i", u=2, i=2))
 
-        def quantize_dy(b):
-            nc.vector.quantize_mx(dy_mx[b][0][:].bitcast(E5M2X4), dy_mx[b][1][:], dy_in[b])
+        def quantize_dy(b, half, over=None):
+            codes, scales = quantize(dy_in[b, half], f"dy{b}{half}", E5M2X4, over)
+            dy_mx[b, half] = (codes[:], scales[:])
 
-        def second_product(b, c, bank_no, on_vector, lo=0, hi=E):
-            acc = banks[bank_no][:, 0 : hi - lo]
-            cols = slice(c * P, (c + 1) * P)
-            nc.tensor.matmul_mx(
-                acc,
-                lhsT=h_mx[b][0][:, cols].bitcast(E4M3X4),
-                lhsT_scale=h_mx[b][1][:, cols],
-                rhs=dy_mx[b][0][:, lo:hi].bitcast(E5M2X4),
-                rhs_scale=dy_mx[b][1][:, lo:hi],
-                start=True,
-                stop=True,
-            )
-            result = keep.tile([P, hi - lo], F32, name=f"result{b}{c}{lo}")
-            if on_vector:
-                nc.vector.tensor_copy(result[:], acc)
-            else:
-                nc.scalar.copy(result[:], acc)
-            nc.sync.dma_start(out[b, c * P : (c + 1) * P, lo:hi], result[:])
+        def second_product(b, f_half, e_half, bank_no):
+            bank = banks[bank_no][:].rearrange("p (c e) -> p c e", c=2)
+            for c in range(2):
+                product(bank[:, c, :], h_mx[b, f_half], slice(c * P, (c + 1) * P), dy_mx[b, e_half], E5M2X4)
 
-        for j in range(PACK - 1):
-            gather_x(j, 0, True)
-            gather_x(j, 1, False)
-        load_dy(2)
-        load_dy(3)
-        gather_x(3, 0, True, 0, SLOTS // 2)
-        gather_x(3, 0, False, SLOTS // 2, SLOTS)
-        gather_x(3, 1, False)
+        def store(b, f_half, e_half, bank_no, on_vector, over=None):
+            result = new([P, 2, HALF], F32, f"result{b}{f_half}{e_half}", over)
+            move_on(on_vector, result[:], banks[bank_no][:].rearrange("p (c e) -> p c e", c=2))
+            rows = out[b, f_half * HALF : (f_half + 1) * HALF, e_half * HALF : (e_half + 1) * HALF]
+            nc.sync.dma_start(rows.rearrange("(c p) e -> p c e", c=2), result[:])
+
+        for j in range(PACK):
+            load_x(j)
+        for b in range(EXPERTS):
+            load_w(b)
+        for k in range(4):
+            load_dy(k)
+        turn_cf()
+        fetch_cf(True, ("ts_row", 0))
+        turn_slot_scales(tx_win, "tx_picked", 0, 0, 2, False)
+        turn_slot_scales(ts_win, "ts_picked0", 8, 0, 1, True)
+        turn_slot_scales(ts_win, "ts_picked1", 8, 1, 2, False)
+        for j in range(3):
+            gather_x_in_place(j)
+            gather_x(j)
+        gather_x_in_place(3)
+        gather_x(3)
+        fetch_slot_scales(True, ("x_win3", 0))
         weave_x(0)
-        weave_w(0, 0, F_HALF)
-        weave_w(0, F_HALF, F)
-        weave_x(1)
-        quantize_x(0)
-        fetch_slot_scales()
-        quantize_w(0, 0, F_HALF)
-        quantize_x(1)
-        quantize_w(0, F_HALF, F)
-        for half in range(2):
-            for pair in range(2):
-                first_product(0, half, pair)
+        quantize_x0()
+        weave_w(0, 0, 256, "vector")
+        weave_w(0, 256, 512, "scalar", ("x_win1", 0))
+        weave_x(1, ("w_raw0", 0))
+        quantize_w(0, 0, 256)
+        quantize_x1(0, ("w_in00", 0))
+        quantize_w(0, 256, 512)
+        weave_w(1, 0, 512, "gpsimd", ("w_in0256", 0))
+        first_product(0, 0, 0, 2)
+        first_product(0, 0, 1, 3)
+        first_product(0, 1, 0, 4)
+        first_product(0, 1, 1, 5)
+        scale_units(0, 0, 0, 2)
+        scale_units(0, 0, 1, 3)
+        scale_units(0, 1, 0, 4)
+        scale_units(0, 1, 1, 5)
+        activate(0, 0, 0)
+        activate(0, 0, 1)
+        activate(0, 1, 0)
+        activate(0, 1, 1)
+        quantize_x1(1, ("scaled000", 0))
+        quantize_w(1, 0, 512)
+        gate_expert0(("w_in10", 0))
+        first_product(1, 0, 0, 2)
+        first_product(1, 0, 1, 3)
+        first_product(1, 1, 0, 4)
+        first_product(1, 1, 1, 5)
         gather_dy(0, 0, False)
-        gather_dy(0, 1, False, 0, SLOTS // 2)
-        for half in range(2):
-            for pair in range(2):
-                scale_units(0, half, pair)
-                activate(0, half, pair)
-        gather_dy(0, 1, True, SLOTS // 2, SLOTS)
-        weave_w(1, 0, F)
-        gate(0, 0, F_HALF)
-        quantize_w(1, 0, F)
-        gate_on_gpsimd(0, 1)
-        for half in range(2):
-            for pair in range(2):
-                first_product(1, half, pair)
+        gather_dy(0, 1, True, over=("x_in11", 0))
         gather_dy(1, 0, False)
-        gather_dy(1, 1, True)
-        for k in range(2, E // P):
-            for b in range(EXPERTS):
-                gather_dy(k, b, False)
-        for half in range(2):
-            for pair in range(2):
-                scale_units(1, half, pair)
-        for half in range(2):
-            for b in range(EXPERTS):
-                turn_dy(2 * half, b, (6, 7, 1, 2)[2 * half + b])
-                turn_dy(2 * half + 1, b, (6, 7, 1, 2)[2 * half + b])
+        gather_dy(1, 1, False)
+        turn_dy(0, 0, 6)
+        turn_dy(1, 0, 6)
+        scale_units(1, 0, 0, 2)
+        scale_units(1, 0, 1, 3)
+        scale_units(1, 1, 0, 4)
+        scale_units(1, 1, 1, 5)
+        activate(1, 0, 0, ("dy_win1", 0))
+        activate(1, 0, 1)
+        activate(1, 1, 0, ("dy_win1", 4))
+        activate(1, 1, 1)
+        turn_dy(0, 1, 7)
+        turn_dy(1, 1, 7)
         fetch_dy(0, 0, 6, True)
-        quantize_h(0, 0, F)
         fetch_dy(1, 0, 7, True)
-        fetch_dy(0, 1, 1, True)
-        quantize_dy(0)
-        for half in range(2):
-            for pair in range(2):
-                activate(1, half, pair)
-        gate(1, 0, F_HALF)
-        fetch_dy(1, 1, 2, True)
-        quantize_h(1, 0, F_HALF)
-        quantize_dy(1)
-        gate(1, 2 * P, 3 * P)
-        quantize_h(1, 2 * P, 3 * P)
-        gate(1, 3 * P, F)
-        quantize_h(1, 3 * P, F)
-        for c in range(F // P):
-            second_product(0, c, (3, 4, 5, 6)[c], False)
-        second_product(1, 0, 7, False)
-        second_product(1, 1, 1, False)
-        second_product(1, 2, 2, True)
-        second_product(1, 3, 3, False, 0, E // 2)
-        second_product(1, 3, 4, True, E // 2, E)
+        gate(0, ("x_win0", 0))
+        quantize_h0(("act10", 0))
+        quantize_h1(0)
+        quantize_dy(0, 0, ("act10", 2))
+        quantize_dy(1, 0, ("act10", 3))
+        second_product(0, 0, 0, 1)
+        second_product(0, 1, 0, 2)
+        gather_dy(2, 0, False)
+        gather_dy(2, 1, True, over=("h_in10", 0))
+        gather_dy(3, 0, False)
+        gather_dy(3, 1, False)
+        turn_dy(2, 0, 6)
+        turn_dy(3, 0, 6)
+        store(0, 0, 0, 1, True)
+        fetch_dy(0, 1, 6, True, ("x_win2", 0))
+        second_product(1, 0, 0, 6)
+        turn_dy(2, 1, 1)
+        turn_dy(3, 1, 1)
+        store(0, 1, 0, 2, False, ("dy_win3", 0))
+        quantize_dy(0, 1)
+        gate(1, ("dy_in01", 0))
+        second_product(0, 0, 1, 5)
+        second_product(0, 1, 1, 3)
+        fetch_dy(1, 1, 1, False)
+        store(1, 0, 0, 6, False)
+        quantize_dy(1, 1)
+        quantize_h1(1)
+        second_product(1, 0, 1, 2)
+        second_product(1, 1, 0, 4)
+        second_product(1, 1, 1, 7)
+        store(0, 0, 1, 5, False)
+        store(0, 1, 1, 3, False)
+        store(1, 0, 1, 2, True)
+        store(1, 1, 0, 4, False)
+        store(1, 1, 1, 7, True)

@@ -25,6 +25,9 @@ F = 512
 E = 512
 LIST_COLS = SLOTS // 16
 HALF = 256
+PIECE = 128
+ROW = P - 1
+KIB = 1024
 BYTES_OF = {F32: 4, BF16: 2, U32: 4, U8: 1}
 
 FLOPS = 2 * EXPERTS * SLOTS * F * (D + E)
@@ -49,16 +52,16 @@ def tile_attend_gxfull_sil_W2_kernel(tc, xT, dyT, w1, ts, tx, cf, offs, out):
                     size = size * extent
                 place["end"] = place["end"] + -(-size // 64) * 64
             else:
-                place[name] = place[over[0]] + 1024 * over[1]
+                place[name] = place[over[0]] + over[1]
             return arena.tile(shape, dtype, name=name, align_bytes=64, offset=place[name])
 
         offsets = keep.tile([P, EXPERTS * LIST_COLS], U16, name="offsets")
         nc.sync.dma_start(offsets[:], offs)
-        tx_row = new([1, TOKENS], F32, "tx_row")
-        ts_row = new([1, TOKENS], F32, "ts_row")
+        ts_win = new([P, TOKENS], F32, "ts_win")
+        tx_win = new([P, TOKENS], F32, "tx_win")
         cf_cols = new([P, PACK], F32, "cf_cols")
-        nc.scalar.dma_start(tx_row[:], tx[0:1, :])
-        nc.sync.dma_start(ts_row[:], ts[0:1, :])
+        nc.scalar.dma_start(tx_win[ROW : ROW + 1, :], tx[0:1, :])
+        nc.sync.dma_start(ts_win[ROW : ROW + 1, :], ts[0:1, :])
         nc.scalar.dma_start(cf_cols[:], cf.rearrange("(p c) o -> p (c o)", c=PACK))
 
         def slots_of(b, lo=0, hi=SLOTS):
@@ -80,15 +83,10 @@ def tile_attend_gxfull_sil_W2_kernel(tc, xT, dyT, w1, ts, tx, cf, offs, out):
         nc.vector.memset(warm[:, 0:1], 0.0)
         nc.scalar.activation(warm[:, 1:2], warm[:, 0:1], SILU)
 
-        ts_win = new([P, TOKENS], F32, "ts_win")
-        tx_win = new([P, TOKENS], F32, "tx_win")
         ident = new([P, P], F32, "ident")
-        nc.gpsimd.memset(ts_win[:], 0.0)
-        nc.vector.memset(tx_win[:, 0 : TOKENS - 1], 0.0)
-        nc.vector.memset(tx_win[:, TOKENS - 1 :], 0.0)
-        nc.vector.tensor_copy(tx_win[0:1, 0 : TOKENS // 2], tx_row[:, 0 : TOKENS // 2])
-        nc.scalar.activation(tx_win[0:1, TOKENS // 2 :], tx_row[:, TOKENS // 2 :], COPY)
-        nc.vector.tensor_copy(ts_win[0:1, :], ts_row[:])
+        nc.gpsimd.memset(ts_win[0:ROW, :], 0.0)
+        nc.vector.memset(tx_win[0:ROW, 0 : TOKENS - 1], 0.0)
+        nc.vector.memset(tx_win[0:ROW, TOKENS - 1 :], 0.0)
         make_identity(nc, ident[:])
 
         x_rows = xT.rearrange("(p j) t -> p j t", j=PACK)
@@ -110,15 +108,13 @@ def tile_attend_gxfull_sil_W2_kernel(tc, xT, dyT, w1, ts, tx, cf, offs, out):
             for c in range(PACK):
                 nc.tensor.transpose(banks[1][:, c * P : (c + 1) * P], cf_cols[:, c : c + 1].to_broadcast([P, P]), ident[:])
 
-        def turn_slot_scales(win, name, first_col, b_lo, b_hi, on_vector):
-            count = (b_hi - b_lo) * SLOTS
-            picked = new([P, count], F32, name)
-            copy_on(on_vector, picked[:], win[:].indirect(slots_of(b_lo, 0, count)))
-            for b in range(b_lo, b_hi):
-                for r in range(PACK):
-                    col = first_col + b * PACK + r
-                    first = (b - b_lo) * SLOTS
-                    nc.tensor.transpose(banks[0][:, col : col + P], picked[:, first + r : first + SLOTS : PACK], ident[:])
+        def turn_slot_scales(win, name, first_col, on_vector):
+            picked = new([P, EXPERTS * SLOTS], F32, name)
+            copy_on(on_vector, picked[:], win[:].indirect(offsets[:]))
+            for b in reversed(range(EXPERTS)):
+                for r in reversed(range(PACK)):
+                    col = first_col + b * PACK + r - ROW
+                    nc.tensor.transpose(banks[0][:, col : col + P], picked[:, b * SLOTS + r : (b + 1) * SLOTS : PACK], ident[:])
 
         spread = {}
 
@@ -127,18 +123,18 @@ def tile_attend_gxfull_sil_W2_kernel(tc, xT, dyT, w1, ts, tx, cf, offs, out):
             dst = spread["cf"][:].rearrange("p (n c) -> p n c", c=PACK)
             move_on(on_vector, dst, banks[1][:].rearrange("p (c n) -> p n c", c=PACK))
 
-        ts_cols = banks[0][:, EXPERTS * PACK : 2 * EXPERTS * PACK].rearrange("p (b r) -> p b r", r=PACK)
+        ts_cols = banks[0][:, P + EXPERTS * PACK : P + 2 * EXPERTS * PACK].rearrange("p (b r) -> p b r", r=PACK)
 
         def fetch_slot_scales(on_vector, over=None):
             both = new([P, 2 * EXPERTS * PACK], F32, "slot_scales", over)
-            move_on(on_vector, both[:], banks[0][:, 0 : 2 * EXPERTS * PACK])
+            move_on(on_vector, both[:], banks[0][:, P : P + 2 * EXPERTS * PACK])
             spread["tx"] = both[:, 0 : EXPERTS * PACK].rearrange("p (b r) -> p b r", r=PACK)
             spread["ts"] = both[:, EXPERTS * PACK :].rearrange("p (b r) -> p b r", r=PACK)
 
-        def quantize(src, name, fmt, over):
+        def quantize(src, name, fmt, over, scales_over=None):
             width = src.shape[1] // PACK
             codes = new([P, width], U32, name + "_codes", over)
-            scales = new([P, width], U8, name + "_scales")
+            scales = new([P, width], U8, name + "_scales", scales_over)
             nc.vector.quantize_mx(codes[:].bitcast(fmt), scales[:], src)
             return codes, scales
 
@@ -171,7 +167,10 @@ def tile_attend_gxfull_sil_W2_kernel(tc, xT, dyT, w1, ts, tx, cf, offs, out):
             w_in[b, lo] = new([P, (hi - lo) * PACK], BF16, f"w_in{b}{lo}", over)[:]
             if engine == "gpsimd":
                 dst = w_in[b, lo].rearrange("p (c j) -> p c j", j=PACK)
-                nc.gpsimd.tensor_scalar(dst, w_raw[b][:, :, lo:hi].rearrange("p j c -> p c j"), 1.0, 0.0, MULT, ADD)
+                src = w_raw[b][:].rearrange("p j c -> p c j")
+                for first in range(lo, hi, PIECE):
+                    cols = slice(first, first + PIECE)
+                    nc.gpsimd.tensor_scalar(dst[:, cols, :], src[:, cols, :], 1.0, 0.0, MULT, ADD)
             else:
                 dst = w_in[b, lo].rearrange("p (c i j) -> p c j i", i=4, j=PACK)
                 copy_on(engine == "vector", dst, w_raw[b][:, :, lo:hi].rearrange("p j (c i) -> p c j i", i=4))
@@ -206,9 +205,12 @@ def tile_attend_gxfull_sil_W2_kernel(tc, xT, dyT, w1, ts, tx, cf, offs, out):
             cf_half = spread["cf"][:, half * HALF : (half + 1) * HALF].unsqueeze(1).broadcast_to([P, 2, HALF])
             nc.vector.tensor_tensor(scaled[b, half, pair], bank, cf_half, MULT)
 
-        def activate(b, half, pair, over=None):
-            if pair == 0:
-                act[b, half] = new([P, PACK, HALF], F32, f"act{b}{half}", over)
+        def new_act(b, halves, over=None):
+            rows = new([P, len(halves), PACK, HALF], F32, f"act{b}{halves[0]}", over)
+            for n, half in enumerate(halves):
+                act[b, half] = rows[:, n, :, :]
+
+        def activate(b, half, pair):
             for rr in range(2):
                 r = 2 * pair + rr
                 nc.scalar.activation(
@@ -217,72 +219,63 @@ def tile_attend_gxfull_sil_W2_kernel(tc, xT, dyT, w1, ts, tx, cf, offs, out):
 
         h_in, h_mx = {}, {}
 
-        def gate_on_gpsimd(b, half, dst):
-            nc.gpsimd.tensor_tensor(
-                dst.rearrange("p (c r) -> p c r", r=PACK),
-                act[b, half][:].rearrange("p r c -> p c r"),
-                spread["ts"][:, b, :].unsqueeze(1).broadcast_to([P, HALF, PACK]),
-                MULT,
-            )
+        def gate(b, lo, hi, on_vector, over=None):
+            h_in[b, lo] = new([P, (hi - lo) * PACK], BF16, f"h_in{b}{lo}", over)
+            dst = h_in[b, lo][:]
+            half, first = divmod(lo, HALF)
+            rows = act[b, half][:, :, first : first + hi - lo]
+            if on_vector:
+                nc.vector.tensor_tensor(
+                    dst.rearrange("p (c i r) -> p c r i", i=4, r=PACK),
+                    rows.rearrange("p r (c i) -> p c r i", i=4),
+                    ts_cols[:, b, :].unsqueeze(1).unsqueeze(3).broadcast_to([P, (hi - lo) // 4, PACK, 4]),
+                    MULT,
+                )
+            else:
+                nc.gpsimd.tensor_tensor(
+                    dst.rearrange("p (c r) -> p c r", r=PACK),
+                    rows.rearrange("p r c -> p c r"),
+                    spread["ts"][:, b, :].unsqueeze(1).broadcast_to([P, hi - lo, PACK]),
+                    MULT,
+                )
 
-        def gate_expert0(over):
-            h_in[0] = new([P, F * PACK], BF16, "h_in0", over)
-            for half in range(2):
-                gate_on_gpsimd(0, half, h_in[0][:, half * HALF * PACK : (half + 1) * HALF * PACK])
-
-        def gate_last(over):
-            h_in[1, 1] = new([P, HALF * PACK], BF16, "h_in11", over)
-            gate_on_gpsimd(1, 1, h_in[1, 1][:])
-
-        def gate(half, over=None):
-            h_in[1, half] = new([P, HALF * PACK], BF16, f"h_in1{half}", over)
-            nc.vector.tensor_tensor(
-                h_in[1, half][:].rearrange("p (c i r) -> p c r i", i=4, r=PACK),
-                act[1, half][:].rearrange("p r (c i) -> p c r i", i=4),
-                ts_cols[:, 1, :].unsqueeze(1).unsqueeze(3).broadcast_to([P, HALF // 4, PACK, 4]),
-                MULT,
-            )
-
-        def quantize_h0(over):
-            codes, scales = quantize(h_in[0][:], "h0", E4M3X4, over)
-            for half in range(2):
-                h_mx[0, half] = (codes[:, half * HALF : (half + 1) * HALF], scales[:, half * HALF : (half + 1) * HALF])
-
-        def quantize_h1(half, over=None):
-            h_mx[1, half] = quantize(h_in[1, half][:], f"h1{half}", E4M3X4, over)
+        def quantize_h(b, lo, scales_over=None):
+            both = quantize(h_in[b, lo][:], f"h{b}{lo}", E4M3X4, None, scales_over)
+            for first in range(0, both[0][:].shape[1], P):
+                h_mx[b, (lo + first) // P] = (both, slice(first, first + P))
 
         dy_picked, dy_in, dy_mx = {}, {}, {}
 
         def gather_dy(k, b, on_vector, lo=0, hi=SLOTS, over=None):
             if (k, b) not in dy_picked:
-                dy_picked[k, b] = new([P, SLOTS], BF16, f"dy_picked{k}{b}", over)
+                dy_picked[k, b] = new([P, SLOTS], BF16, f"dy_picked{k}{b}", over)[:]
             copy_on(on_vector, dy_picked[k, b][:, lo:hi], dy_win[k][:].indirect(slots_of(b, lo, hi)))
 
         def turn_dy(k, b, bank_no):
             bank = banks[bank_no][:].rearrange("p (u e) -> p u e", u=2)
-            words = dy_picked[k, b][:].bitcast(F32)
+            words = dy_picked[k, b].bitcast(F32)
             for u in range(2):
                 nc.tensor.transpose(bank[:, u, (k % 2) * P : (k % 2 + 1) * P], words[:, u : SLOTS // 2 : 2], ident[:])
 
         def fetch_dy(b, half, bank_no, on_vector, over=None):
-            dy_in[b, half] = new([P, HALF * PACK], BF16, f"dy_in{b}{half}", over)[:]
-            dst = dy_in[b, half].bitcast(F32).rearrange("p (g i u) -> p g u i", i=2, u=2)
+            if half == 0:
+                dy_in[b] = new([P, E * PACK], BF16, f"dy_in{b}", over)
+            dst = dy_in[b][:, half * HALF * PACK : (half + 1) * HALF * PACK].bitcast(F32)
+            dst = dst.rearrange("p (g i u) -> p g u i", i=2, u=2)
             move_on(on_vector, dst, banks[bank_no][:].rearrange("p (u g i) -> p g u i", u=2, i=2))
 
-        def quantize_dy(b, half, over=None):
-            codes, scales = quantize(dy_in[b, half], f"dy{b}{half}", E5M2X4, over)
-            dy_mx[b, half] = (codes[:], scales[:])
+        def quantize_dy(b, over=None):
+            codes, scales = quantize(dy_in[b][:], f"dy{b}", E5M2X4, over)
+            dy_mx[b] = (codes[:], scales[:])
 
-        def second_product(b, f_half, e_half, bank_no):
-            bank = banks[bank_no][:].rearrange("p (c e) -> p c e", c=2)
-            for c in range(2):
-                product(bank[:, c, :], h_mx[b, f_half], slice(c * P, (c + 1) * P), dy_mx[b, e_half], E5M2X4)
+        def second_product(b, c, bank_no, lo=0, hi=E):
+            moving = (dy_mx[b][0][:, lo:hi], dy_mx[b][1][:, lo:hi])
+            product(banks[bank_no][:, 0 : hi - lo], h_mx[b, c][0], h_mx[b, c][1], moving, E5M2X4)
 
-        def store(b, f_half, e_half, bank_no, on_vector, over=None):
-            result = new([P, 2, HALF], F32, f"result{b}{f_half}{e_half}", over)
-            move_on(on_vector, result[:], banks[bank_no][:].rearrange("p (c e) -> p c e", c=2))
-            rows = out[b, f_half * HALF : (f_half + 1) * HALF, e_half * HALF : (e_half + 1) * HALF]
-            nc.sync.dma_start(rows.rearrange("(c p) e -> p c e", c=2), result[:])
+        def store(b, c, bank_no, on_vector, lo=0, hi=E, over=None):
+            result = new([P, hi - lo], F32, f"result{b}{c}{lo}", over)
+            move_on(on_vector, result[:], banks[bank_no][:, 0 : hi - lo])
+            nc.sync.dma_start(out[b, c * P : (c + 1) * P, lo:hi], result[:])
 
         for j in range(PACK):
             load_x(j)
@@ -291,94 +284,90 @@ def tile_attend_gxfull_sil_W2_kernel(tc, xT, dyT, w1, ts, tx, cf, offs, out):
         for k in range(4):
             load_dy(k)
         turn_cf()
-        fetch_cf(True, ("ts_row", 0))
-        turn_slot_scales(tx_win, "tx_picked", 0, 0, 2, False)
-        turn_slot_scales(ts_win, "ts_picked0", 8, 0, 1, True)
-        turn_slot_scales(ts_win, "ts_picked1", 8, 1, 2, False)
+        turn_slot_scales(ts_win, "ts_picked", P + EXPERTS * PACK, True)
+        turn_slot_scales(tx_win, "tx_picked", P, False)
+        fetch_cf(False)
         for j in range(3):
             gather_x_in_place(j)
             gather_x(j)
+        fetch_slot_scales(False, ("x_win2", 0))
         gather_x_in_place(3)
         gather_x(3)
-        fetch_slot_scales(True, ("x_win3", 0))
         weave_x(0)
         quantize_x0()
-        weave_w(0, 0, 256, "vector")
-        weave_w(0, 256, 512, "scalar", ("x_win1", 0))
-        weave_x(1, ("w_raw0", 0))
+        weave_w(0, 0, 256, "vector", ("ts_win", 0))
+        weave_w(0, 256, 512, "scalar", ("tx_win", 0))
         quantize_w(0, 0, 256)
-        quantize_x1(0, ("w_in00", 0))
+        weave_x(1, ("ts_win", KIB))
+        quantize_x1(0, ("ts_win", 0))
         quantize_w(0, 256, 512)
-        weave_w(1, 0, 512, "gpsimd", ("w_in0256", 0))
-        first_product(0, 0, 0, 2)
-        first_product(0, 0, 1, 3)
-        first_product(0, 1, 0, 4)
-        first_product(0, 1, 1, 5)
-        scale_units(0, 0, 0, 2)
-        scale_units(0, 0, 1, 3)
-        scale_units(0, 1, 0, 4)
-        scale_units(0, 1, 1, 5)
-        activate(0, 0, 0)
-        activate(0, 0, 1)
-        activate(0, 1, 0)
-        activate(0, 1, 1)
-        quantize_x1(1, ("scaled000", 0))
+        weave_w(1, 0, 512, "gpsimd", ("tx_win", 0))
+        for half in range(2):
+            for pair in range(2):
+                first_product(0, half, pair, 2 + 2 * half + pair)
+        for half in range(2):
+            new_act(0, (half,))
+            for pair in range(2):
+                scale_units(0, half, pair, 2 + 2 * half + pair)
+                activate(0, half, pair)
+        gather_dy(0, 1, True)
+        quantize_x1(1, ("w_raw1", 0))
         quantize_w(1, 0, 512)
-        gate_expert0(("w_in10", 0))
-        first_product(1, 0, 0, 2)
-        first_product(1, 0, 1, 3)
-        first_product(1, 1, 0, 4)
-        first_product(1, 1, 1, 5)
+        gate(0, 0, 256, True, ("w_in10", 0))
+        gate(0, 256, 512, False, ("act00", 0))
         gather_dy(0, 0, False)
-        gather_dy(0, 1, True, over=("x_in11", 0))
-        gather_dy(1, 0, False)
-        gather_dy(1, 1, False)
-        turn_dy(0, 0, 6)
-        turn_dy(1, 0, 6)
-        scale_units(1, 0, 0, 2)
-        scale_units(1, 0, 1, 3)
-        scale_units(1, 1, 0, 4)
-        scale_units(1, 1, 1, 5)
-        activate(1, 0, 0, ("dy_win1", 0))
-        activate(1, 0, 1)
-        activate(1, 1, 0, ("dy_win1", 4))
-        activate(1, 1, 1)
         turn_dy(0, 1, 7)
-        turn_dy(1, 1, 7)
-        fetch_dy(0, 0, 6, True)
-        fetch_dy(1, 0, 7, True)
-        gate(0, ("x_win0", 0))
-        quantize_h0(("act10", 0))
-        quantize_h1(0)
-        quantize_dy(0, 0, ("act10", 2))
-        quantize_dy(1, 0, ("act10", 3))
-        second_product(0, 0, 0, 1)
-        second_product(0, 1, 0, 2)
+        for half in range(2):
+            for pair in range(2):
+                first_product(1, half, pair, 2 + 2 * half + pair)
+        gather_dy(1, 1, False)
+        gather_dy(1, 0, False)
         gather_dy(2, 0, False)
-        gather_dy(2, 1, True, over=("h_in10", 0))
-        gather_dy(3, 0, False)
+        for half in range(2):
+            for pair in range(2):
+                scale_units(1, half, pair, 2 + 2 * half + pair)
+        turn_dy(1, 1, 7)
+        turn_dy(0, 0, 2)
+        turn_dy(1, 0, 2)
+        fetch_dy(1, 0, 7, True)
+        fetch_dy(0, 0, 2, True)
+        gather_dy(2, 1, True)
+        gather_dy(3, 0, False, 0, 512, ("x_win0", 8 * KIB - 512))
         gather_dy(3, 1, False)
-        turn_dy(2, 0, 6)
-        turn_dy(3, 0, 6)
-        store(0, 0, 0, 1, True)
-        fetch_dy(0, 1, 6, True, ("x_win2", 0))
-        second_product(1, 0, 0, 6)
+        turn_dy(2, 0, 1)
+        turn_dy(3, 0, 1)
+        fetch_dy(0, 1, 1, True)
         turn_dy(2, 1, 1)
         turn_dy(3, 1, 1)
-        store(0, 1, 0, 2, False, ("dy_win3", 0))
-        quantize_dy(0, 1)
-        gate(1, ("dy_in01", 0))
-        second_product(0, 0, 1, 5)
-        second_product(0, 1, 1, 3)
-        fetch_dy(1, 1, 1, False)
-        store(1, 0, 0, 6, False)
-        quantize_dy(1, 1)
-        quantize_h1(1)
-        second_product(1, 0, 1, 2)
-        second_product(1, 1, 0, 4)
-        second_product(1, 1, 1, 7)
-        store(0, 0, 1, 5, False)
-        store(0, 1, 1, 3, False)
-        store(1, 0, 1, 2, True)
-        store(1, 1, 0, 4, False)
-        store(1, 1, 1, 7, True)
+        quantize_h(0, 0, ("x_win1", 0))
+        quantize_h(0, 256, ("x_win1", 256))
+        quantize_dy(0)
+        fetch_dy(1, 1, 1, True)
+        new_act(1, (0, 1), ("x_win0", 0))
+        activate(1, 0, 0)
+        activate(1, 0, 1)
+        activate(1, 1, 0)
+        for c in range(4):
+            second_product(0, c, 2 + c)
+        store(0, 0, 2, False)
+        activate(1, 1, 1)
+        store(0, 1, 3, False)
+        store(0, 2, 4, False)
+        store(0, 3, 5, False)
+        gate(1, 0, 256, True)
+        quantize_dy(1)
+        quantize_h(1, 0)
+        second_product(1, 0, 7)
+        second_product(1, 1, 6)
+        gate(1, 256, 384, True)
+        gate(1, 384, 512, True)
+        quantize_h(1, 256)
+        quantize_h(1, 384)
+        second_product(1, 2, 1)
+        second_product(1, 3, 2, 0, 256)
+        second_product(1, 3, 3, 256, 512)
+        store(1, 0, 7, False)
+        store(1, 1, 6, False)
+        store(1, 2, 1, True)
+        store(1, 3, 2, False, 0, 256)
+        store(1, 3, 3, True, 256, 512)

@@ -28,6 +28,7 @@ HALF = 256
 PIECE = 128
 ROW = P - 1
 KIB = 1024
+ALIGN = 256
 BYTES_OF = {F32: 4, BF16: 2, U32: 4, U8: 1}
 
 FLOPS = 2 * EXPERTS * SLOTS * F * (D + E)
@@ -50,10 +51,10 @@ def tile_attend_gxfull_sil_W2_kernel(tc, xT, dyT, w1, ts, tx, cf, offs, out):
                 size = BYTES_OF[dtype]
                 for extent in shape[1:]:
                     size = size * extent
-                place["end"] = place["end"] + -(-size // 64) * 64
+                place["end"] = place["end"] + -(-size // ALIGN) * ALIGN
             else:
                 place[name] = place[over[0]] + over[1]
-            return arena.tile(shape, dtype, name=name, align_bytes=64, offset=place[name])
+            return arena.tile(shape, dtype, name=name, align_bytes=ALIGN if over is None else 64, offset=place[name])
 
         offsets = keep.tile([P, EXPERTS * LIST_COLS], U16, name="offsets")
         nc.sync.dma_start(offsets[:], offs)
@@ -220,8 +221,9 @@ def tile_attend_gxfull_sil_W2_kernel(tc, xT, dyT, w1, ts, tx, cf, offs, out):
         h_in, h_mx = {}, {}
 
         def gate(b, lo, hi, on_vector, over=None):
-            h_in[b, lo] = new([P, (hi - lo) * PACK], BF16, f"h_in{b}{lo}", over)
-            dst = h_in[b, lo][:]
+            if (b, lo) not in h_in:
+                h_in[b, lo] = new([P, (hi - lo) * PACK], BF16, f"h_in{b}{lo}", over)[:]
+            dst = h_in[b, lo][:, 0 : (hi - lo) * PACK]
             half, first = divmod(lo, HALF)
             rows = act[b, half][:, :, first : first + hi - lo]
             if on_vector:
@@ -240,7 +242,7 @@ def tile_attend_gxfull_sil_W2_kernel(tc, xT, dyT, w1, ts, tx, cf, offs, out):
                 )
 
         def quantize_h(b, lo, scales_over=None):
-            both = quantize(h_in[b, lo][:], f"h{b}{lo}", E4M3X4, None, scales_over)
+            both = quantize(h_in[b, lo], f"h{b}{lo}", E4M3X4, None, scales_over)
             for first in range(0, both[0][:].shape[1], P):
                 h_mx[b, (lo + first) // P] = (both, slice(first, first + P))
 

@@ -178,6 +178,7 @@ def tile_attend_gxfull_sil_W2_kernel(tc, xT, dyT, w1, ts, tx, cf, offs, out):
 
         def quantize_w(b, lo, hi, over=None):
             codes, scales = quantize(w_in[b, lo], f"w{b}{lo}", E4M3X4, over)
+            w_mx[b] = (codes[:], scales[:])
             for first in range(lo, hi, HALF):
                 cols = slice(first - lo, first - lo + HALF)
                 w_mx[b, first // HALF] = (codes[:, cols], scales[:, cols])
@@ -205,6 +206,24 @@ def tile_attend_gxfull_sil_W2_kernel(tc, xT, dyT, w1, ts, tx, cf, offs, out):
             scaled[b, half, pair] = new([P, 2, HALF], F32, f"scaled{b}{half}{pair}", over)[:]
             cf_half = spread["cf"][:, half * HALF : (half + 1) * HALF].unsqueeze(1).broadcast_to([P, 2, HALF])
             nc.vector.tensor_tensor(scaled[b, half, pair], bank, cf_half, MULT)
+
+        def first_product_wide(b, r, bank_no):
+            product(banks[bank_no][:], x_mx[b, r // 2], slice((r % 2) * P, (r % 2 + 1) * P), w_mx[b], E4M3X4)
+
+        def scale_wide(b, r, bank_no):
+            if r == 0:
+                scaled[b] = new([P, 2, PACK, HALF], F32, f"scaled{b}")
+            nc.vector.scalar_tensor_tensor(
+                scaled[b][:, :, r, :],
+                banks[bank_no][:].rearrange("p (h f) -> p h f", h=2),
+                spread["tx"][:, b, r : r + 1],
+                spread["cf"][:].rearrange("p (h f) -> p h f", h=2),
+                MULT,
+                MULT,
+            )
+
+        def activate_wide(b, half):
+            nc.scalar.activation(act[b, half], scaled[b][:, half, :, :], SILU)
 
         def new_act(b, halves, over=None):
             rows = new([P, len(halves), PACK, HALF], F32, f"act{b}{halves[0]}", over)
@@ -315,19 +334,17 @@ def tile_attend_gxfull_sil_W2_kernel(tc, xT, dyT, w1, ts, tx, cf, offs, out):
         gather_dy(0, 1, True)
         quantize_x1(1, ("w_raw1", 0))
         quantize_w(1, 0, 512)
-        gate(0, 0, 256, True, ("w_in10", 0))
+        gate(0, 0, 256, True, ("w_raw1", 2 * KIB))
         gate(0, 256, 512, False, ("act00", 0))
         gather_dy(0, 0, False)
         turn_dy(0, 1, 7)
-        for half in range(2):
-            for pair in range(2):
-                first_product(1, half, pair, 2 + 2 * half + pair)
+        for r in range(PACK):
+            first_product_wide(1, r, 2 + r)
         gather_dy(1, 1, False)
         gather_dy(1, 0, False)
         gather_dy(2, 0, False)
-        for half in range(2):
-            for pair in range(2):
-                scale_units(1, half, pair, 2 + 2 * half + pair)
+        for r in range(PACK):
+            scale_wide(1, r, 2 + r)
         turn_dy(1, 1, 7)
         turn_dy(0, 0, 2)
         turn_dy(1, 0, 2)
@@ -342,26 +359,24 @@ def tile_attend_gxfull_sil_W2_kernel(tc, xT, dyT, w1, ts, tx, cf, offs, out):
         turn_dy(2, 1, 1)
         turn_dy(3, 1, 1)
         quantize_h(0, 0, ("x_win1", 0))
-        quantize_h(0, 256, ("x_win1", 256))
         quantize_dy(0)
+        quantize_h(0, 256, ("x_win1", 256))
         fetch_dy(1, 1, 1, True)
         new_act(1, (0, 1), ("x_win0", 0))
-        activate(1, 0, 0)
-        activate(1, 0, 1)
-        activate(1, 1, 0)
+        activate_wide(1, 0)
+        activate_wide(1, 1)
         for c in range(4):
             second_product(0, c, 2 + c)
-        store(0, 0, 2, False)
-        activate(1, 1, 1)
-        store(0, 1, 3, False)
-        store(0, 2, 4, False)
-        store(0, 3, 5, False)
-        gate(1, 0, 256, True)
+        for c in range(4):
+            store(0, c, 2 + c, False)
+        gate(1, 0, 128, True)
         quantize_dy(1)
         quantize_h(1, 0)
         second_product(1, 0, 7)
-        second_product(1, 1, 6)
+        gate(1, 128, 256, True)
         gate(1, 256, 384, True)
+        quantize_h(1, 128)
+        second_product(1, 1, 6)
         gate(1, 384, 512, True)
         quantize_h(1, 256)
         quantize_h(1, 384)
@@ -370,6 +385,6 @@ def tile_attend_gxfull_sil_W2_kernel(tc, xT, dyT, w1, ts, tx, cf, offs, out):
         second_product(1, 3, 3, 256, 512)
         store(1, 0, 7, False)
         store(1, 1, 6, False)
-        store(1, 2, 1, True)
-        store(1, 3, 2, False, 0, 256)
+        store(1, 2, 1, False)
+        store(1, 3, 2, True, 0, 256)
         store(1, 3, 3, True, 256, 512)

@@ -29,6 +29,7 @@ PIECE = 128
 ROW = P - 1
 KIB = 1024
 ALIGN = 256
+RUN = 2
 BYTES_OF = {F32: 4, BF16: 2, U32: 4, U8: 1}
 
 FLOPS = 2 * EXPERTS * SLOTS * F * (D + E)
@@ -173,8 +174,8 @@ def tile_attend_gxfull_sil_W2_kernel(tc, xT, dyT, w1, ts, tx, cf, offs, out):
                     cols = slice(first, first + PIECE)
                     nc.gpsimd.tensor_scalar(dst[:, cols, :], src[:, cols, :], 1.0, 0.0, MULT, ADD)
             else:
-                dst = w_in[b, lo].rearrange("p (c i j) -> p c j i", i=4, j=PACK)
-                copy_on(engine == "vector", dst, w_raw[b][:, :, lo:hi].rearrange("p j (c i) -> p c j i", i=4))
+                dst = w_in[b, lo].rearrange("p (c i j) -> p c j i", i=RUN, j=PACK)
+                copy_on(engine == "vector", dst, w_raw[b][:, :, lo:hi].rearrange("p j (c i) -> p c j i", i=RUN))
 
         def quantize_w(b, lo, hi, over=None):
             codes, scales = quantize(w_in[b, lo], f"w{b}{lo}", E4M3X4, over)
@@ -247,9 +248,9 @@ def tile_attend_gxfull_sil_W2_kernel(tc, xT, dyT, w1, ts, tx, cf, offs, out):
             rows = act[b, half][:, :, first : first + hi - lo]
             if on_vector:
                 nc.vector.tensor_tensor(
-                    dst.rearrange("p (c i r) -> p c r i", i=4, r=PACK),
-                    rows.rearrange("p r (c i) -> p c r i", i=4),
-                    ts_cols[:, b, :].unsqueeze(1).unsqueeze(3).broadcast_to([P, (hi - lo) // 4, PACK, 4]),
+                    dst.rearrange("p (c i r) -> p c r i", i=RUN, r=PACK),
+                    rows.rearrange("p r (c i) -> p c r i", i=RUN),
+                    ts_cols[:, b, :].unsqueeze(1).unsqueeze(3).broadcast_to([P, (hi - lo) // RUN, PACK, RUN]),
                     MULT,
                 )
             else:

@@ -347,22 +347,22 @@ def tile_attend_gxfull_sil_W2_kernel(tc, xT, dyT, w1, ts, tx, cf, offs, out):
         for r in range(PACK):
             scale_wide(1, r, 2 + r)
         turn_dy(1, 1, 7)
-        turn_dy(0, 0, 2)
-        turn_dy(1, 0, 2)
+        turn_dy(0, 0, 3)
+        turn_dy(1, 0, 3)
         fetch_dy(1, 0, 7, True)
-        fetch_dy(0, 0, 2, True)
+        fetch_dy(0, 0, 3, True)
         gather_dy(2, 1, True)
         gather_dy(3, 0, False, 0, 512, ("x_win0", 8 * KIB - 512))
         gather_dy(3, 1, False)
         turn_dy(2, 0, 1)
         turn_dy(3, 0, 1)
         fetch_dy(0, 1, 1, True)
-        turn_dy(2, 1, 1)
-        turn_dy(3, 1, 1)
+        turn_dy(3, 1, 6)
+        turn_dy(2, 1, 6)
         quantize_h(0, 0, ("x_win1", 0))
         quantize_dy(0)
         quantize_h(0, 256, ("x_win1", 256))
-        fetch_dy(1, 1, 1, True)
+        fetch_dy(1, 1, 6, True)
         new_act(1, (0, 1), ("x_win0", 0))
         activate_wide(1, 0)
         activate_wide(1, 1)

@@ -25,7 +25,6 @@ F = 512
 E = 512
 LIST_COLS = SLOTS // 16
 HALF = 256
-PIECE = 128
 ROW = P - 1
 KIB = 1024
 ALIGN = 256
@@ -170,9 +169,7 @@ def tile_attend_gxfull_sil_W2_kernel(tc, xT, dyT, w1, ts, tx, cf, offs, out):
             if engine == "gpsimd":
                 dst = w_in[b, lo].rearrange("p (c j) -> p c j", j=PACK)
                 src = w_raw[b][:].rearrange("p j c -> p c j")
-                for first in range(lo, hi, PIECE):
-                    cols = slice(first, first + PIECE)
-                    nc.gpsimd.tensor_scalar(dst[:, cols, :], src[:, cols, :], 1.0, 0.0, MULT, ADD)
+                nc.gpsimd.tensor_scalar(dst, src, 1.0, 0.0, MULT, ADD)
             else:
                 dst = w_in[b, lo].rearrange("p (c i j) -> p c j i", i=RUN, j=PACK)
                 copy_on(engine == "vector", dst, w_raw[b][:, :, lo:hi].rearrange("p j (c i) -> p c j i", i=RUN))
@@ -223,8 +220,8 @@ def tile_attend_gxfull_sil_W2_kernel(tc, xT, dyT, w1, ts, tx, cf, offs, out):
                 MULT,
             )
 
-        def activate_wide(b, half):
-            nc.scalar.activation(act[b, half], scaled[b][:, half, :, :], SILU)
+        def activate_wide(b, half, lo=0, hi=HALF):
+            nc.scalar.activation(act[b, half][:, :, lo:hi], scaled[b][:, half, :, lo:hi], SILU)
 
         def new_act(b, halves, over=None):
             rows = new([P, len(halves), PACK, HALF], F32, f"act{b}{halves[0]}", over)
@@ -261,8 +258,8 @@ def tile_attend_gxfull_sil_W2_kernel(tc, xT, dyT, w1, ts, tx, cf, offs, out):
                     MULT,
                 )
 
-        def quantize_h(b, lo, scales_over=None):
-            both = quantize(h_in[b, lo], f"h{b}{lo}", E4M3X4, None, scales_over)
+        def quantize_h(b, lo, over=None, scales_over=None):
+            both = quantize(h_in[b, lo], f"h{b}{lo}", E4M3X4, over, scales_over)
             for first in range(0, both[0][:].shape[1], P):
                 h_mx[b, (lo + first) // P] = (both, slice(first, first + P))
 
@@ -279,23 +276,32 @@ def tile_attend_gxfull_sil_W2_kernel(tc, xT, dyT, w1, ts, tx, cf, offs, out):
             for u in range(2):
                 nc.tensor.transpose(bank[:, u, (k % 2) * P : (k % 2 + 1) * P], words[:, u : SLOTS // 2 : 2], ident[:])
 
-        def fetch_dy(b, half, bank_no, on_vector, over=None):
-            if half == 0:
-                dy_in[b] = new([P, E * PACK], BF16, f"dy_in{b}", over)
-            dst = dy_in[b][:, half * HALF * PACK : (half + 1) * HALF * PACK].bitcast(F32)
-            dst = dst.rearrange("p (g i u) -> p g u i", i=2, u=2)
+        def fetch_dy(b, half, bank_no, on_vector):
+            dy_in[b, half] = new([P, HALF * PACK], BF16, f"dy_in{b}{half}")
+            dst = dy_in[b, half][:].bitcast(F32).rearrange("p (g i u) -> p g u i", i=2, u=2)
             move_on(on_vector, dst, banks[bank_no][:].rearrange("p (u g i) -> p g u i", u=2, i=2))
 
-        def quantize_dy(b, over=None):
-            codes, scales = quantize(dy_in[b][:], f"dy{b}", E5M2X4, over)
-            dy_mx[b] = (codes[:], scales[:])
+        def quantize_dy(b, half, over=None, scales_over=None):
+            if half == 0:
+                dy_mx[b] = (new([P, E], U32, f"dy{b}_codes", over)[:], new([P, E], U8, f"dy{b}_scales", scales_over)[:])
+            cols = slice(half * HALF, (half + 1) * HALF)
+            nc.vector.quantize_mx(dy_mx[b][0][:, cols].bitcast(E5M2X4), dy_mx[b][1][:, cols], dy_in[b, half][:])
 
-        def second_product(b, c, bank_no, lo=0, hi=E):
+        def second_product(b, c, acc, lo=0, hi=E):
             moving = (dy_mx[b][0][:, lo:hi], dy_mx[b][1][:, lo:hi])
-            product(banks[bank_no][:, 0 : hi - lo], h_mx[b, c][0], h_mx[b, c][1], moving, E5M2X4)
+            product(acc, h_mx[b, c][0], h_mx[b, c][1], moving, E5M2X4)
 
-        def store(b, c, bank_no, on_vector, lo=0, hi=E, over=None):
-            result = new([P, hi - lo], F32, f"result{b}{c}{lo}", over)
+        def second_product_pair(b, pair, half, bank_no):
+            for n in range(2):
+                second_product(b, 2 * pair + n, banks[bank_no][:, n * HALF : (n + 1) * HALF], half * HALF, (half + 1) * HALF)
+
+        def store_pair(b, pair, half, bank_no, result):
+            nc.scalar.copy(result, banks[bank_no][:])
+            rows = out[b, 2 * pair * P : (2 * pair + 2) * P, half * HALF : (half + 1) * HALF]
+            nc.sync.dma_start(rows.rearrange("(n p) e -> p n e", p=P), result.rearrange("p (n e) -> p n e", n=2))
+
+        def store(b, c, bank_no, on_vector, lo=0, hi=E):
+            result = new([P, hi - lo], F32, f"result{b}{c}{lo}")
             move_on(on_vector, result[:], banks[bank_no][:, 0 : hi - lo])
             nc.sync.dma_start(out[b, c * P : (c + 1) * P, lo:hi], result[:])
 
@@ -332,60 +338,72 @@ def tile_attend_gxfull_sil_W2_kernel(tc, xT, dyT, w1, ts, tx, cf, offs, out):
             for pair in range(2):
                 scale_units(0, half, pair, 2 + 2 * half + pair)
                 activate(0, half, pair)
-        gather_dy(0, 1, True)
+        gate(0, 0, 256, True)
         quantize_x1(1, ("w_raw1", 0))
         quantize_w(1, 0, 512)
-        gate(0, 0, 256, True, ("w_raw1", 2 * KIB))
-        gate(0, 256, 512, False, ("act00", 0))
+        gather_dy(0, 1, True, 0, 512, ("x_in11", 0))
+        gate(0, 256, 512, False, ("tx_win", 0))
         gather_dy(0, 0, False)
-        turn_dy(0, 1, 7)
         for r in range(PACK):
             first_product_wide(1, r, 2 + r)
-        gather_dy(1, 1, False)
+        turn_dy(0, 1, 7)
         gather_dy(1, 0, False)
+        gather_dy(1, 1, False)
+        shared = new([P, PACK, 2 * HALF], F32, "shared")
+        dy_picked[2, 0] = shared[:, 0, HALF:].bitcast(BF16)
+        act[1, 0] = shared[:, :, 0:HALF]
+        place["act10"] = place["shared"]
         gather_dy(2, 0, False)
         for r in range(PACK):
             scale_wide(1, r, 2 + r)
+        turn_dy(0, 0, 2)
+        turn_dy(1, 0, 2)
         turn_dy(1, 1, 7)
-        turn_dy(0, 0, 3)
-        turn_dy(1, 0, 3)
+        activate_wide(1, 0)
+        fetch_dy(0, 0, 2, True)
+        quantize_h(0, 0, ("act01", 0))
+        quantize_h(0, 256, ("act01", KIB))
+        quantize_dy(0, 0, ("act01", 2 * KIB))
+        gather_dy(3, 0, False, 0, 512, ("x_win1", 0))
         fetch_dy(1, 0, 7, True)
-        fetch_dy(0, 0, 3, True)
-        gather_dy(2, 1, True)
-        gather_dy(3, 0, False, 0, 512, ("x_win0", 8 * KIB - 512))
-        gather_dy(3, 1, False)
+        gate(1, 0, 128, False, ("dy_in00", 0))
+        second_product_pair(0, 0, 0, 3)
+        second_product_pair(0, 1, 0, 4)
         turn_dy(2, 0, 1)
+        gather_dy(2, 1, True)
+        gather_dy(3, 1, False)
         turn_dy(3, 0, 1)
-        fetch_dy(0, 1, 1, True)
+        gate(1, 128, 256, True)
         turn_dy(3, 1, 6)
         turn_dy(2, 1, 6)
-        quantize_h(0, 0, ("x_win1", 0))
-        quantize_dy(0)
-        quantize_h(0, 256, ("x_win1", 256))
+        early = new([P, 2, E], F32, "early", ("x_win0", 4 * KIB + 64))
+        new_act(1, (1,), ("x_win1", KIB - 64))
+        store_pair(0, 0, 0, 3, early[:, 0, :])
+        fetch_dy(0, 1, 1, True)
+        activate_wide(1, 1, 0, 128)
+        quantize_dy(1, 0, ("act10", 0), ("x_win1", 64))
+        quantize_dy(0, 1)
+        store_pair(0, 1, 0, 4, early[:, 1, :])
         fetch_dy(1, 1, 6, True)
-        new_act(1, (0, 1), ("x_win0", 0))
-        activate_wide(1, 0)
-        activate_wide(1, 1)
-        for c in range(4):
-            second_product(0, c, 2 + c)
-        for c in range(4):
-            store(0, c, 2 + c, False)
-        gate(1, 0, 128, True)
-        quantize_dy(1)
-        quantize_h(1, 0)
-        second_product(1, 0, 7)
-        gate(1, 128, 256, True)
+        activate_wide(1, 1, 128, 256)
+        second_product_pair(0, 0, 1, 5)
+        second_product_pair(0, 1, 1, 2)
+        quantize_h(1, 0, None, ("x_win1", 576))
+        quantize_h(1, 128, None, ("x_win1", 704))
+        quantize_dy(1, 1)
+        store_pair(0, 0, 1, 5, new([P, E], F32, "late0")[:])
         gate(1, 256, 384, True)
-        quantize_h(1, 128)
-        second_product(1, 1, 6)
+        second_product(1, 0, banks[7][:])
+        store_pair(0, 1, 1, 2, new([P, E], F32, "late1")[:])
         gate(1, 384, 512, True)
+        second_product(1, 1, banks[3][:])
+        store(1, 0, 7, False)
         quantize_h(1, 256)
         quantize_h(1, 384)
-        second_product(1, 2, 1)
-        second_product(1, 3, 2, 0, 256)
-        second_product(1, 3, 3, 256, 512)
-        store(1, 0, 7, False)
-        store(1, 1, 6, False)
-        store(1, 2, 1, False)
-        store(1, 3, 2, True, 0, 256)
-        store(1, 3, 3, True, 256, 512)
+        second_product(1, 2, banks[4][:])
+        store(1, 1, 3, False)
+        second_product(1, 3, banks[1][:, 0:HALF], 0, HALF)
+        second_product(1, 3, banks[6][:, 0:HALF], HALF, E)
+        store(1, 2, 4, False)
+        store(1, 3, 1, False, 0, HALF)
+        store(1, 3, 6, True, HALF, E)

@@ -276,8 +276,8 @@ def tile_attend_gxfull_sil_W2_kernel(tc, xT, dyT, w1, ts, tx, cf, offs, out):
             for u in range(2):
                 nc.tensor.transpose(bank[:, u, (k % 2) * P : (k % 2 + 1) * P], words[:, u : SLOTS // 2 : 2], ident[:])
 
-        def fetch_dy(b, half, bank_no, on_vector):
-            dy_in[b, half] = new([P, HALF * PACK], BF16, f"dy_in{b}{half}")
+        def fetch_dy(b, half, bank_no, on_vector, over=None):
+            dy_in[b, half] = new([P, HALF * PACK], BF16, f"dy_in{b}{half}", over)
             dst = dy_in[b, half][:].bitcast(F32).rearrange("p (g i u) -> p g u i", i=2, u=2)
             move_on(on_vector, dst, banks[bank_no][:].rearrange("p (u g i) -> p g u i", u=2, i=2))
 
@@ -318,10 +318,10 @@ def tile_attend_gxfull_sil_W2_kernel(tc, xT, dyT, w1, ts, tx, cf, offs, out):
         for j in range(3):
             gather_x_in_place(j)
             gather_x(j)
-        fetch_slot_scales(False, ("x_win2", 0))
         gather_x_in_place(3)
         gather_x(3)
         weave_x(0)
+        fetch_slot_scales(False, ("x_win3", 0))
         quantize_x0()
         weave_w(0, 0, 256, "vector", ("ts_win", 0))
         weave_w(0, 256, 512, "scalar", ("tx_win", 0))
@@ -346,7 +346,6 @@ def tile_attend_gxfull_sil_W2_kernel(tc, xT, dyT, w1, ts, tx, cf, offs, out):
         gather_dy(0, 0, False)
         for r in range(PACK):
             first_product_wide(1, r, 2 + r)
-        turn_dy(0, 1, 7)
         gather_dy(1, 0, False)
         gather_dy(1, 1, False)
         shared = new([P, PACK, 2 * HALF], F32, "shared")
@@ -359,18 +358,19 @@ def tile_attend_gxfull_sil_W2_kernel(tc, xT, dyT, w1, ts, tx, cf, offs, out):
         turn_dy(0, 0, 2)
         turn_dy(1, 0, 2)
         turn_dy(1, 1, 7)
+        turn_dy(0, 1, 7)
         activate_wide(1, 0)
         fetch_dy(0, 0, 2, True)
         quantize_h(0, 0, ("act01", 0))
         quantize_h(0, 256, ("act01", KIB))
         quantize_dy(0, 0, ("act01", 2 * KIB))
         gather_dy(3, 0, False, 0, 512, ("x_win1", 0))
-        fetch_dy(1, 0, 7, True)
-        gate(1, 0, 128, False, ("dy_in00", 0))
+        gather_dy(2, 1, True)
+        fetch_dy(1, 0, 7, True, ("dy_win2", 2 * KIB))
+        gate(1, 0, 128, False, ("dy_win2", 0))
         second_product_pair(0, 0, 0, 3)
         second_product_pair(0, 1, 0, 4)
         turn_dy(2, 0, 1)
-        gather_dy(2, 1, True)
         gather_dy(3, 1, False)
         turn_dy(3, 0, 1)
         gate(1, 128, 256, True)

@@ -263,18 +263,20 @@ def tile_attend_gxfull_sil_W2_kernel(tc, xT, dyT, w1, ts, tx, cf, offs, out):
             for first in range(0, both[0][:].shape[1], P):
                 h_mx[b, (lo + first) // P] = (both, slice(first, first + P))
 
-        dy_picked, dy_in, dy_mx = {}, {}, {}
+        dy_picked, dealt, dy_in, dy_mx = {}, {}, {}, {}
 
-        def gather_dy(k, b, on_vector, lo=0, hi=SLOTS, over=None):
-            if (k, b) not in dy_picked:
-                dy_picked[k, b] = new([P, SLOTS], BF16, f"dy_picked{k}{b}", over)[:]
-            copy_on(on_vector, dy_picked[k, b][:, lo:hi], dy_win[k][:].indirect(slots_of(b, lo, hi)))
+        def gather_dy(k, b, on_vector, over=None):
+            dy_picked[k, b] = new([P, SLOTS], BF16, f"dy_picked{k}{b}", over)[:]
+            dealt[k, b] = on_vector
+            dst = dy_picked[k, b].rearrange("p (u s e) -> p s u e", u=2, e=2) if on_vector else dy_picked[k, b]
+            copy_on(on_vector, dst, dy_win[k][:].indirect(slots_of(b)))
 
         def turn_dy(k, b, bank_no):
             bank = banks[bank_no][:].rearrange("p (u e) -> p u e", u=2)
             words = dy_picked[k, b].bitcast(F32)
             for u in range(2):
-                nc.tensor.transpose(bank[:, u, (k % 2) * P : (k % 2 + 1) * P], words[:, u : SLOTS // 2 : 2], ident[:])
+                half = words[:, u * P : (u + 1) * P] if dealt[k, b] else words[:, u : SLOTS // 2 : 2]
+                nc.tensor.transpose(bank[:, u, (k % 2) * P : (k % 2 + 1) * P], half, ident[:])
 
         def fetch_dy(b, half, bank_no, on_vector, over=None):
             dy_in[b, half] = new([P, HALF * PACK], BF16, f"dy_in{b}{half}", over)
@@ -321,13 +323,13 @@ def tile_attend_gxfull_sil_W2_kernel(tc, xT, dyT, w1, ts, tx, cf, offs, out):
         gather_x_in_place(3)
         gather_x(3)
         weave_x(0)
-        fetch_slot_scales(False, ("x_win3", 0))
         quantize_x0()
         weave_w(0, 0, 256, "vector", ("ts_win", 0))
         weave_w(0, 256, 512, "scalar", ("tx_win", 0))
         quantize_w(0, 0, 256)
-        weave_x(1, ("ts_win", KIB))
+        weave_x(1, ("ts_win", KIB + 64))
         quantize_x1(0, ("ts_win", 0))
+        fetch_slot_scales(True, ("ts_win", KIB))
         quantize_w(0, 256, 512)
         weave_w(1, 0, 512, "gpsimd", ("tx_win", 0))
         for half in range(2):
@@ -341,17 +343,13 @@ def tile_attend_gxfull_sil_W2_kernel(tc, xT, dyT, w1, ts, tx, cf, offs, out):
         gate(0, 0, 256, True)
         quantize_x1(1, ("w_raw1", 0))
         quantize_w(1, 0, 512)
-        gather_dy(0, 1, True, 0, 512, ("x_in11", 0))
+        gather_dy(0, 1, True, ("x_in11", 0))
         gate(0, 256, 512, False, ("tx_win", 0))
         gather_dy(0, 0, False)
         for r in range(PACK):
             first_product_wide(1, r, 2 + r)
         gather_dy(1, 0, False)
         gather_dy(1, 1, False)
-        shared = new([P, PACK, 2 * HALF], F32, "shared")
-        dy_picked[2, 0] = shared[:, 0, HALF:].bitcast(BF16)
-        act[1, 0] = shared[:, :, 0:HALF]
-        place["act10"] = place["shared"]
         gather_dy(2, 0, False)
         for r in range(PACK):
             scale_wide(1, r, 2 + r)
@@ -359,51 +357,51 @@ def tile_attend_gxfull_sil_W2_kernel(tc, xT, dyT, w1, ts, tx, cf, offs, out):
         turn_dy(1, 0, 2)
         turn_dy(1, 1, 7)
         turn_dy(0, 1, 7)
-        activate_wide(1, 0)
         fetch_dy(0, 0, 2, True)
         quantize_h(0, 0, ("act01", 0))
-        quantize_h(0, 256, ("act01", KIB))
         quantize_dy(0, 0, ("act01", 2 * KIB))
-        gather_dy(3, 0, False, 0, 512, ("x_win1", 0))
-        gather_dy(2, 1, True)
-        fetch_dy(1, 0, 7, True, ("dy_win2", 2 * KIB))
-        gate(1, 0, 128, False, ("dy_win2", 0))
-        second_product_pair(0, 0, 0, 3)
-        second_product_pair(0, 1, 0, 4)
-        turn_dy(2, 0, 1)
+        quantize_h(0, 256, ("act01", KIB))
+        gather_dy(3, 0, False, ("x_win1", 0))
         gather_dy(3, 1, False)
+        fetch_dy(1, 0, 7, True)
+        gather_dy(2, 1, True)
+        second_product_pair(0, 0, 0, 3)
+        turn_dy(2, 0, 1)
         turn_dy(3, 0, 1)
-        gate(1, 128, 256, True)
         turn_dy(3, 1, 6)
         turn_dy(2, 1, 6)
-        early = new([P, 2, E], F32, "early", ("x_win0", 4 * KIB + 64))
-        new_act(1, (1,), ("x_win1", KIB - 64))
-        store_pair(0, 0, 0, 3, early[:, 0, :])
+        store_pair(0, 0, 0, 3, new([P, E], F32, "early0", ("dy_win3", 0))[:])
+        new_act(1, (0, 1), ("x_win1", KIB - 64))
         fetch_dy(0, 1, 1, True)
-        activate_wide(1, 1, 0, 128)
-        quantize_dy(1, 0, ("act10", 0), ("x_win1", 64))
+        second_product_pair(0, 1, 0, 1)
+        activate_wide(1, 0, 0, 128)
+        quantize_dy(1, 0, None, ("x_win1", 64))
         quantize_dy(0, 1)
-        store_pair(0, 1, 0, 4, early[:, 1, :])
-        fetch_dy(1, 1, 6, True)
-        activate_wide(1, 1, 128, 256)
+        activate_wide(1, 0, 128, 256)
+        gate(1, 0, 128, True)
         second_product_pair(0, 0, 1, 5)
         second_product_pair(0, 1, 1, 2)
-        quantize_h(1, 0, None, ("x_win1", 576))
-        quantize_h(1, 128, None, ("x_win1", 704))
+        fetch_dy(1, 1, 6, True)
+        activate_wide(1, 1, 0, 128)
+        quantize_h(1, 0)
         quantize_dy(1, 1)
-        store_pair(0, 0, 1, 5, new([P, E], F32, "late0")[:])
-        gate(1, 256, 384, True)
+        store_pair(0, 1, 0, 1, new([P, E], F32, "early1")[:])
+        gate(1, 128, 256, True)
         second_product(1, 0, banks[7][:])
-        store_pair(0, 1, 1, 2, new([P, E], F32, "late1")[:])
-        gate(1, 384, 512, True)
+        activate_wide(1, 1, 128, 256)
+        gate(1, 256, 384, True)
+        store_pair(0, 0, 1, 5, new([P, E], F32, "late0")[:])
+        quantize_h(1, 128)
         second_product(1, 1, banks[3][:])
-        store(1, 0, 7, False)
+        gate(1, 384, 512, True)
+        store_pair(0, 1, 1, 2, new([P, E], F32, "late1")[:])
         quantize_h(1, 256)
         quantize_h(1, 384)
         second_product(1, 2, banks[4][:])
-        store(1, 1, 3, False)
         second_product(1, 3, banks[1][:, 0:HALF], 0, HALF)
         second_product(1, 3, banks[6][:, 0:HALF], HALF, E)
+        store(1, 0, 7, False)
+        store(1, 1, 3, True)
         store(1, 2, 4, False)
-        store(1, 3, 1, False, 0, HALF)
-        store(1, 3, 6, True, HALF, E)
+        store(1, 3, 1, True, 0, HALF)
+        store(1, 3, 6, False, HALF, E)

@@ -181,6 +181,12 @@ def tile_attend_gxfull_sil_W2_kernel(tc, xT, dyT, w1, ts, tx, cf, offs, out):
                 cols = slice(first - lo, first - lo + HALF)
                 w_mx[b, first // HALF] = (codes[:, cols], scales[:, cols])
 
+        def quantize_w_quarter(b, lo):
+            if lo == 0:
+                w_mx[b, 0] = (new([P, HALF], U32, f"w{b}0_codes")[:], new([P, HALF], U8, f"w{b}0_scales")[:])
+            cols = slice(lo, lo + P)
+            nc.vector.quantize_mx(w_mx[b, 0][0][:, cols].bitcast(E4M3X4), w_mx[b, 0][1][:, cols], w_in[b, lo])
+
         def product(acc, stationary, cols, moving, fmt):
             nc.tensor.matmul_mx(
                 acc,
@@ -194,10 +200,12 @@ def tile_attend_gxfull_sil_W2_kernel(tc, xT, dyT, w1, ts, tx, cf, offs, out):
 
         scaled, act = {}, {}
 
-        def first_product(b, half, pair, bank_no):
+        def first_product(b, half, pair, bank_no, width=HALF):
             bank = banks[bank_no][:].rearrange("p (r f) -> p r f", r=2)
-            for rr in range(2):
-                product(bank[:, rr, :], x_mx[b, pair], slice(rr * P, (rr + 1) * P), w_mx[b, half], E4M3X4)
+            for lo in range(0, HALF, width):
+                moving = (w_mx[b, half][0][:, lo : lo + width], w_mx[b, half][1][:, lo : lo + width])
+                for rr in range(2):
+                    product(bank[:, rr, lo : lo + width], x_mx[b, pair], slice(rr * P, (rr + 1) * P), moving, E4M3X4)
 
         def scale_units(b, half, pair, bank_no, over=None):
             bank = banks[bank_no][:].rearrange("p (r f) -> p r f", r=2)
@@ -324,17 +332,19 @@ def tile_attend_gxfull_sil_W2_kernel(tc, xT, dyT, w1, ts, tx, cf, offs, out):
         gather_x(3)
         weave_x(0)
         quantize_x0()
-        weave_w(0, 0, 256, "vector", ("ts_win", 0))
+        weave_w(0, 0, 128, "vector", ("ts_win", 0))
+        weave_w(0, 128, 256, "vector", ("ts_win", KIB))
         weave_w(0, 256, 512, "scalar", ("tx_win", 0))
-        quantize_w(0, 0, 256)
-        weave_x(1, ("ts_win", KIB + 64))
-        quantize_x1(0, ("ts_win", 0))
-        fetch_slot_scales(True, ("ts_win", KIB))
+        quantize_w_quarter(0, 0)
+        quantize_w_quarter(0, 128)
+        weave_x(1, ("ts_win", KIB + 128))
+        quantize_x1(0, ("ts_win", 64))
+        fetch_slot_scales(True, ("ts_win", KIB + 64))
         quantize_w(0, 256, 512)
         weave_w(1, 0, 512, "gpsimd", ("tx_win", 0))
         for half in range(2):
             for pair in range(2):
-                first_product(0, half, pair, 2 + 2 * half + pair)
+                first_product(0, half, pair, 2 + 2 * half + pair, P if half + pair == 0 else HALF)
         for half in range(2):
             new_act(0, (half,))
             for pair in range(2):
@@ -373,35 +383,35 @@ def tile_attend_gxfull_sil_W2_kernel(tc, xT, dyT, w1, ts, tx, cf, offs, out):
         store_pair(0, 0, 0, 3, new([P, E], F32, "early0", ("dy_win3", 0))[:])
         new_act(1, (0, 1), ("x_win1", KIB - 64))
         fetch_dy(0, 1, 1, True)
-        second_product_pair(0, 1, 0, 1)
         activate_wide(1, 0, 0, 128)
         quantize_dy(1, 0, None, ("x_win1", 64))
         quantize_dy(0, 1)
         activate_wide(1, 0, 128, 256)
-        gate(1, 0, 128, True)
+        second_product(0, 2, banks[4][:])
         second_product_pair(0, 0, 1, 5)
-        second_product_pair(0, 1, 1, 2)
+        second_product(0, 3, banks[2][:])
         fetch_dy(1, 1, 6, True)
+        gate(1, 0, 128, True)
         activate_wide(1, 1, 0, 128)
-        quantize_h(1, 0)
         quantize_dy(1, 1)
-        store_pair(0, 1, 0, 1, new([P, E], F32, "early1")[:])
+        store(0, 2, 4, False)
         gate(1, 128, 256, True)
+        quantize_h(1, 0)
         second_product(1, 0, banks[7][:])
         activate_wide(1, 1, 128, 256)
         gate(1, 256, 384, True)
         store_pair(0, 0, 1, 5, new([P, E], F32, "late0")[:])
         quantize_h(1, 128)
-        second_product(1, 1, banks[3][:])
-        gate(1, 384, 512, True)
-        store_pair(0, 1, 1, 2, new([P, E], F32, "late1")[:])
         quantize_h(1, 256)
-        quantize_h(1, 384)
+        second_product(1, 1, banks[3][:])
         second_product(1, 2, banks[4][:])
+        store(0, 3, 2, False)
+        gate(1, 384, 512, True)
+        quantize_h(1, 384)
         second_product(1, 3, banks[1][:, 0:HALF], 0, HALF)
         second_product(1, 3, banks[6][:, 0:HALF], HALF, E)
         store(1, 0, 7, False)
-        store(1, 1, 3, True)
-        store(1, 2, 4, False)
+        store(1, 1, 3, False)
+        store(1, 2, 4, True)
         store(1, 3, 1, True, 0, HALF)
         store(1, 3, 6, False, HALF, E)

@@ -198,7 +198,7 @@ def tile_attend_gxfull_sil_W2_kernel(tc, xT, dyT, w1, ts, tx, cf, offs, out):
                 stop=True,
             )
 
-        scaled, act = {}, {}
+        scaled, act, act_rows = {}, {}, {}
 
         def first_product(b, half, pair, bank_no, width=HALF):
             bank = banks[bank_no][:].rearrange("p (r f) -> p r f", r=2)
@@ -228,8 +228,9 @@ def tile_attend_gxfull_sil_W2_kernel(tc, xT, dyT, w1, ts, tx, cf, offs, out):
                 MULT,
             )
 
-        def activate_wide(b, half, lo=0, hi=HALF):
-            nc.scalar.activation(act[b, half][:, :, lo:hi], scaled[b][:, half, :, lo:hi], SILU)
+        def activate_quarter(b, lo):
+            half, first = divmod(lo, HALF)
+            nc.scalar.activation(act_rows[b, lo], scaled[b][:, half, :, first : first + P], SILU)
 
         def new_act(b, halves, over=None):
             rows = new([P, len(halves), PACK, HALF], F32, f"act{b}{halves[0]}", over)
@@ -249,8 +250,7 @@ def tile_attend_gxfull_sil_W2_kernel(tc, xT, dyT, w1, ts, tx, cf, offs, out):
             if (b, lo) not in h_in:
                 h_in[b, lo] = new([P, (hi - lo) * PACK], BF16, f"h_in{b}{lo}", over)[:]
             dst = h_in[b, lo][:, 0 : (hi - lo) * PACK]
-            half, first = divmod(lo, HALF)
-            rows = act[b, half][:, :, first : first + hi - lo]
+            rows = act_rows[b, lo]
             if on_vector:
                 nc.vector.tensor_tensor(
                     dst.rearrange("p (c i r) -> p c r i", i=RUN, r=PACK),
@@ -273,8 +273,8 @@ def tile_attend_gxfull_sil_W2_kernel(tc, xT, dyT, w1, ts, tx, cf, offs, out):
 
         dy_picked, dealt, dy_in, dy_mx = {}, {}, {}, {}
 
-        def gather_dy(k, b, on_vector, over=None):
-            dy_picked[k, b] = new([P, SLOTS], BF16, f"dy_picked{k}{b}", over)[:]
+        def gather_dy(k, b, on_vector, over=None, into=None):
+            dy_picked[k, b] = new([P, SLOTS], BF16, f"dy_picked{k}{b}", over)[:] if into is None else into
             dealt[k, b] = on_vector
             dst = dy_picked[k, b].rearrange("p (u s e) -> p s u e", u=2, e=2) if on_vector else dy_picked[k, b]
             copy_on(on_vector, dst, dy_win[k][:].indirect(slots_of(b)))
@@ -350,6 +350,7 @@ def tile_attend_gxfull_sil_W2_kernel(tc, xT, dyT, w1, ts, tx, cf, offs, out):
             for pair in range(2):
                 scale_units(0, half, pair, 2 + 2 * half + pair)
                 activate(0, half, pair)
+        act_rows[0, 0], act_rows[0, HALF] = act[0, 0], act[0, 1]
         gate(0, 0, 256, True)
         quantize_x1(1, ("w_raw1", 0))
         quantize_w(1, 0, 512)
@@ -360,13 +361,16 @@ def tile_attend_gxfull_sil_W2_kernel(tc, xT, dyT, w1, ts, tx, cf, offs, out):
             first_product_wide(1, r, 2 + r)
         gather_dy(1, 0, False)
         gather_dy(1, 1, False)
-        gather_dy(2, 0, False)
+        shared = new([P, PACK, P + HALF], F32, "shared")
+        act_rows[1, 0] = shared[:, :, 0:P]
+        gather_dy(2, 0, False, None, shared[:, 0, P:].bitcast(BF16))
         for r in range(PACK):
             scale_wide(1, r, 2 + r)
         turn_dy(0, 0, 2)
         turn_dy(1, 0, 2)
         turn_dy(1, 1, 7)
         turn_dy(0, 1, 7)
+        activate_quarter(1, 0)
         fetch_dy(0, 0, 2, True)
         quantize_h(0, 0, ("act01", 0))
         quantize_dy(0, 0, ("act01", 2 * KIB))
@@ -377,28 +381,29 @@ def tile_attend_gxfull_sil_W2_kernel(tc, xT, dyT, w1, ts, tx, cf, offs, out):
         gather_dy(2, 1, True)
         second_product_pair(0, 0, 0, 3)
         turn_dy(2, 0, 1)
+        gate(1, 0, 128, True)
         turn_dy(3, 0, 1)
         turn_dy(3, 1, 6)
         turn_dy(2, 1, 6)
+        later = new([P, PACK, 3 * P], F32, "act1", ("x_win1", KIB - 64))
+        for n in range(3):
+            act_rows[1, (n + 1) * P] = later[:, :, n * P : (n + 1) * P]
+        activate_quarter(1, 128)
         store_pair(0, 0, 0, 3, new([P, E], F32, "early0", ("dy_win3", 0))[:])
-        new_act(1, (0, 1), ("x_win1", KIB - 64))
         fetch_dy(0, 1, 1, True)
-        activate_wide(1, 0, 0, 128)
         quantize_dy(1, 0, None, ("x_win1", 64))
         quantize_dy(0, 1)
-        activate_wide(1, 0, 128, 256)
+        quantize_h(1, 0, None, ("x_win1", 576))
+        activate_quarter(1, 256)
         second_product(0, 2, banks[4][:])
         second_product_pair(0, 0, 1, 5)
         second_product(0, 3, banks[2][:])
         fetch_dy(1, 1, 6, True)
-        gate(1, 0, 128, True)
-        activate_wide(1, 1, 0, 128)
-        quantize_dy(1, 1)
-        store(0, 2, 4, False)
         gate(1, 128, 256, True)
-        quantize_h(1, 0)
+        activate_quarter(1, 384)
+        quantize_dy(1, 1)
         second_product(1, 0, banks[7][:])
-        activate_wide(1, 1, 128, 256)
+        store(0, 2, 4, False)
         gate(1, 256, 384, True)
         store_pair(0, 0, 1, 5, new([P, E], F32, "late0")[:])
         quantize_h(1, 128)

@@ -62,7 +62,7 @@ def tile_attend_gxfull_sil_W2_kernel(tc, xT, dyT, w1, ts, tx, cf, offs, out):
         tx_win = new([P, TOKENS], F32, "tx_win")
         cf_cols = new([P, PACK], F32, "cf_cols")
         nc.scalar.dma_start(tx_win[ROW : ROW + 1, :], tx[0:1, :])
-        nc.sync.dma_start(ts_win[ROW : ROW + 1, :], ts[0:1, :])
+        nc.scalar.dma_start(ts_win[ROW : ROW + 1, :], ts[0:1, :])
         nc.scalar.dma_start(cf_cols[:], cf.rearrange("(p c) o -> p (c o)", c=PACK))
 
         def slots_of(b, lo=0, hi=SLOTS):
@@ -111,11 +111,14 @@ def tile_attend_gxfull_sil_W2_kernel(tc, xT, dyT, w1, ts, tx, cf, offs, out):
 
         def turn_slot_scales(win, name, first_col, on_vector):
             picked = new([P, EXPERTS * SLOTS], F32, name)
-            copy_on(on_vector, picked[:], win[:].indirect(offsets[:]))
+            dst = picked[:].rearrange("p (b r s) -> p b s r", b=EXPERTS, r=PACK) if on_vector else picked[:]
+            copy_on(on_vector, dst, win[:].indirect(offsets[:]))
             for b in reversed(range(EXPERTS)):
                 for r in reversed(range(PACK)):
                     col = first_col + b * PACK + r - ROW
-                    nc.tensor.transpose(banks[0][:, col : col + P], picked[:, b * SLOTS + r : (b + 1) * SLOTS : PACK], ident[:])
+                    first = b * SLOTS + r * P
+                    place_r = picked[:, first : first + P] if on_vector else picked[:, b * SLOTS + r : (b + 1) * SLOTS : PACK]
+                    nc.tensor.transpose(banks[0][:, col : col + P], place_r, ident[:])
 
         spread = {}
 
@@ -207,11 +210,15 @@ def tile_attend_gxfull_sil_W2_kernel(tc, xT, dyT, w1, ts, tx, cf, offs, out):
                 for rr in range(2):
                     product(bank[:, rr, lo : lo + width], x_mx[b, pair], slice(rr * P, (rr + 1) * P), moving, E4M3X4)
 
-        def scale_units(b, half, pair, bank_no, over=None):
+        def scale_units(b, half, pair, bank_no):
             bank = banks[bank_no][:].rearrange("p (r f) -> p r f", r=2)
-            scaled[b, half, pair] = new([P, 2, HALF], F32, f"scaled{b}{half}{pair}", over)[:]
-            cf_half = spread["cf"][:, half * HALF : (half + 1) * HALF].unsqueeze(1).broadcast_to([P, 2, HALF])
-            nc.vector.tensor_tensor(scaled[b, half, pair], bank, cf_half, MULT)
+            scaled[b, half, pair] = new([P, 2, HALF], F32, f"scaled{b}{half}{pair}")[:]
+            cf_half = spread["cf"][:, half * HALF : (half + 1) * HALF]
+            for rr in range(2):
+                r = 2 * pair + rr
+                nc.vector.scalar_tensor_tensor(
+                    scaled[b, half, pair][:, rr, :], bank[:, rr, :], spread["tx"][:, b, r : r + 1], cf_half, MULT, MULT
+                )
 
         def first_product_wide(b, r, bank_no):
             product(banks[bank_no][:], x_mx[b, r // 2], slice((r % 2) * P, (r % 2 + 1) * P), w_mx[b], E4M3X4)
@@ -238,11 +245,7 @@ def tile_attend_gxfull_sil_W2_kernel(tc, xT, dyT, w1, ts, tx, cf, offs, out):
                 act[b, half] = rows[:, n, :, :]
 
         def activate(b, half, pair):
-            for rr in range(2):
-                r = 2 * pair + rr
-                nc.scalar.activation(
-                    act[b, half][:, r, :], scaled[b, half, pair][:, rr, :], SILU, scale=spread["tx"][:, b, r : r + 1]
-                )
+            nc.scalar.activation(act[b, half][:, 2 * pair : 2 * pair + 2, :], scaled[b, half, pair], SILU)
 
         h_in, h_mx = {}, {}
 

from contextlib import ExitStack

import concourse.mybir as mybir
from concourse.masks import make_identity

F32 = mybir.dt.float32
BF16 = mybir.dt.bfloat16
U32 = mybir.dt.uint32
U16 = mybir.dt.uint16
U8 = mybir.dt.uint8
E4M3X4 = mybir.dt.float8_e4m3fn_x4
E5M2X4 = mybir.dt.float8_e5m2_x4
COPY = mybir.ActivationFunctionType.Copy
SILU = mybir.ActivationFunctionType.Silu
MULT = mybir.AluOpType.mult
ADD = mybir.AluOpType.add

P = 128
PACK = 4
EXPERTS = 2
SLOTS = 512
TOKENS = 2048
D = 512
F = 512
E = 512
LIST_COLS = SLOTS // 16
HALF = 256
ROW = P - 1
KIB = 1024
ALIGN = 256
RUN = 2
BYTES_OF = {F32: 4, BF16: 2, U32: 4, U8: 1}

FLOPS = 2 * EXPERTS * SLOTS * F * (D + E)
BYTES = 4 * (D * TOKENS + E * TOKENS + EXPERTS * D * F + 2 * TOKENS + F + EXPERTS * F * E) + 2 * P * EXPERTS * LIST_COLS


def tile_attend_gxfull_sil_W2_kernel(tc, xT, dyT, w1, ts, tx, cf, offs, out):
    nc = tc.nc
    with ExitStack() as ctx:
        keep = ctx.enter_context(tc.tile_pool(name="keep", bufs=1))
        psum = ctx.enter_context(tc.psum_pool(name="psum", bufs=1))
        banks = [psum.tile([P, 512], F32, name=f"bank{n}") for n in range(8)]

        arena = ctx.enter_context(tc.tile_pool(name="arena", bufs=1))
        place = {"end": 0}

        def new(shape, dtype, name, over=None):
            if over is None:
                place[name] = place["end"]
                size = BYTES_OF[dtype]
                for extent in shape[1:]:
                    size = size * extent
                place["end"] = place["end"] + -(-size // ALIGN) * ALIGN
            else:
                place[name] = place[over[0]] + over[1]
            return arena.tile(shape, dtype, name=name, align_bytes=ALIGN if over is None else 64, offset=place[name])

        offsets = keep.tile([P, EXPERTS * LIST_COLS], U16, name="offsets")
        nc.sync.dma_start(offsets[:], offs)
        ts_win = new([P, TOKENS], F32, "ts_win")
        tx_win = new([P, TOKENS], F32, "tx_win")
        cf_cols = new([P, PACK], F32, "cf_cols")
        nc.scalar.dma_start(tx_win[ROW : ROW + 1, :], tx[0:1, :])
        nc.scalar.dma_start(ts_win[ROW : ROW + 1, :], ts[0:1, :])
        nc.scalar.dma_start(cf_cols[:], cf.rearrange("(p c) o -> p (c o)", c=PACK))

        def slots_of(b, lo=0, hi=SLOTS):
            return offsets[:, b * LIST_COLS + lo // 16 : b * LIST_COLS + hi // 16]

        def copy_on(on_vector, dst, src):
            if on_vector:
                nc.vector.tensor_copy(dst, src)
            else:
                nc.scalar.activation(dst, src, COPY)

        def move_on(on_vector, dst, src):
            if on_vector:
                nc.vector.tensor_copy(dst, src)
            else:
                nc.scalar.copy(dst, src)

        warm = new([P, 2], F32, "warm")
        nc.vector.memset(warm[:, 0:1], 0.0)
        nc.scalar.activation(warm[:, 1:2], warm[:, 0:1], SILU)

        ident = new([P, P], F32, "ident")
        nc.gpsimd.memset(ts_win[0:ROW, :], 0.0)
        nc.vector.memset(tx_win[0:ROW, 0 : TOKENS - 1], 0.0)
        nc.vector.memset(tx_win[0:ROW, TOKENS - 1 :], 0.0)
        make_identity(nc, ident[:])

        x_rows = xT.rearrange("(p j) t -> p j t", j=PACK)
        x_win, w_raw, dy_win = {}, {}, {}

        def load_x(j):
            x_win[j] = new([P, TOKENS], F32, f"x_win{j}")
            nc.sync.dma_start(x_win[j][:], x_rows[:, j, :])

        def load_w(b):
            w_raw[b] = new([P, PACK, F], F32, f"w_raw{b}")
            nc.sync.dma_start(w_raw[b][:], w1[b].rearrange("(p j) f -> p j f", j=PACK))

        def load_dy(k):
            dy_win[k] = new([P, TOKENS], F32, f"dy_win{k}")
            nc.sync.dma_start(dy_win[k][:], dyT[k * P : (k + 1) * P, :])

        def turn_cf():
            for c in range(PACK):
                nc.tensor.transpose(banks[1][:, c * P : (c + 1) * P], cf_cols[:, c : c + 1].to_broadcast([P, P]), ident[:])

        def turn_slot_scales(win, name, first_col, on_vector):
            picked = new([P, EXPERTS * SLOTS], F32, name)
            dst = picked[:].rearrange("p (b r s) -> p b s r", b=EXPERTS, r=PACK) if on_vector else picked[:]
            copy_on(on_vector, dst, win[:].indirect(offsets[:]))
            for b in reversed(range(EXPERTS)):
                for r in reversed(range(PACK)):
                    col = first_col + b * PACK + r - ROW
                    first = b * SLOTS + r * P
                    place_r = picked[:, first : first + P] if on_vector else picked[:, b * SLOTS + r : (b + 1) * SLOTS : PACK]
                    nc.tensor.transpose(banks[0][:, col : col + P], place_r, ident[:])

        spread = {}

        def fetch_cf(on_vector, over=None):
            spread["cf"] = new([P, F], F32, "cf_all", over)
            dst = spread["cf"][:].rearrange("p (n c) -> p n c", c=PACK)
            move_on(on_vector, dst, banks[1][:].rearrange("p (c n) -> p n c", c=PACK))

        ts_cols = banks[0][:, P + EXPERTS * PACK : P + 2 * EXPERTS * PACK].rearrange("p (b r) -> p b r", r=PACK)

        def fetch_slot_scales(on_vector, over=None):
            both = new([P, 2 * EXPERTS * PACK], F32, "slot_scales", over)
            move_on(on_vector, both[:], banks[0][:, P : P + 2 * EXPERTS * PACK])
            spread["tx"] = both[:, 0 : EXPERTS * PACK].rearrange("p (b r) -> p b r", r=PACK)
            spread["ts"] = both[:, EXPERTS * PACK :].rearrange("p (b r) -> p b r", r=PACK)

        def quantize(src, name, fmt, over, scales_over=None):
            width = src.shape[1] // PACK
            codes = new([P, width], U32, name + "_codes", over)
            scales = new([P, width], U8, name + "_scales", scales_over)
            nc.vector.quantize_mx(codes[:].bitcast(fmt), scales[:], src)
            return codes, scales

        x_in = {0: new([P, SLOTS * PACK], BF16, "x_in0")}
        x_picked = new([P, PACK, SLOTS], BF16, "x_picked")
        x_mx, w_in, w_mx = {}, {}, {}

        def gather_x_in_place(j):
            dst = x_in[0][:].rearrange("p (r s j) -> p j s r", r=PACK, j=PACK)[:, j, :, :]
            nc.vector.tensor_copy(dst, x_win[j][:].indirect(slots_of(0)))

        def gather_x(j):
            nc.scalar.activation(x_picked[:, j, :], x_win[j][:].indirect(slots_of(1)), COPY)

        def weave_x(pair, over=None):
            x_in[1, pair] = new([P, SLOTS * PACK // 2], BF16, f"x_in1{pair}", over)
            dst = x_in[1, pair][:].rearrange("p (r s h j) -> p s j h r", r=2, h=2, j=PACK)
            src = x_picked[:].rearrange("p j (s h r) -> p s j h r", h=2, r=PACK)
            nc.scalar.copy(dst, src[:, :, :, :, 2 * pair : 2 * pair + 2])

        def quantize_x0():
            codes, scales = quantize(x_in[0][:], "x0", E4M3X4, None)
            for pair in range(2):
                x_mx[0, pair] = (codes[:, pair * HALF : (pair + 1) * HALF], scales[:, pair * HALF : (pair + 1) * HALF])

        def quantize_x1(pair, over=None):
            x_mx[1, pair] = quantize(x_in[1, pair][:], f"x1{pair}", E4M3X4, over)

        def weave_w(b, lo, hi, engine, over=None):
            w_in[b, lo] = new([P, (hi - lo) * PACK], BF16, f"w_in{b}{lo}", over)[:]
            if engine == "gpsimd":
                dst = w_in[b, lo].rearrange("p (c j) -> p c j", j=PACK)
                src = w_raw[b][:].rearrange("p j c -> p c j")
                nc.gpsimd.tensor_scalar(dst, src, 1.0, 0.0, MULT, ADD)
            else:
                dst = w_in[b, lo].rearrange("p (c i j) -> p c j i", i=RUN, j=PACK)
                copy_on(engine == "vector", dst, w_raw[b][:, :, lo:hi].rearrange("p j (c i) -> p c j i", i=RUN))

        def quantize_w(b, lo, hi, over=None):
            codes, scales = quantize(w_in[b, lo], f"w{b}{lo}", E4M3X4, over)
            w_mx[b] = (codes[:], scales[:])
            for first in range(lo, hi, HALF):
                cols = slice(first - lo, first - lo + HALF)
                w_mx[b, first // HALF] = (codes[:, cols], scales[:, cols])

        def quantize_w_quarter(b, lo):
            if lo == 0:
                w_mx[b, 0] = (new([P, HALF], U32, f"w{b}0_codes")[:], new([P, HALF], U8, f"w{b}0_scales")[:])
            cols = slice(lo, lo + P)
            nc.vector.quantize_mx(w_mx[b, 0][0][:, cols].bitcast(E4M3X4), w_mx[b, 0][1][:, cols], w_in[b, lo])

        def product(acc, stationary, cols, moving, fmt):
            nc.tensor.matmul_mx(
                acc,
                lhsT=stationary[0][:, cols].bitcast(E4M3X4),
                lhsT_scale=stationary[1][:, cols],
                rhs=moving[0].bitcast(fmt),
                rhs_scale=moving[1],
                start=True,
                stop=True,
            )

        scaled, act, act_rows = {}, {}, {}

        def first_product(b, half, pair, bank_no, width=HALF):
            bank = banks[bank_no][:].rearrange("p (r f) -> p r f", r=2)
            for lo in range(0, HALF, width):
                moving = (w_mx[b, half][0][:, lo : lo + width], w_mx[b, half][1][:, lo : lo + width])
                for rr in range(2):
                    product(bank[:, rr, lo : lo + width], x_mx[b, pair], slice(rr * P, (rr + 1) * P), moving, E4M3X4)

        def scale_units(b, half, pair, bank_no):
            bank = banks[bank_no][:].rearrange("p (r f) -> p r f", r=2)
            scaled[b, half, pair] = new([P, 2, HALF], F32, f"scaled{b}{half}{pair}")[:]
            cf_half = spread["cf"][:, half * HALF : (half + 1) * HALF]
            for rr in range(2):
                r = 2 * pair + rr
                nc.vector.scalar_tensor_tensor(
                    scaled[b, half, pair][:, rr, :], bank[:, rr, :], spread["tx"][:, b, r : r + 1], cf_half, MULT, MULT
                )

        def first_product_wide(b, r, bank_no):
            product(banks[bank_no][:], x_mx[b, r // 2], slice((r % 2) * P, (r % 2 + 1) * P), w_mx[b], E4M3X4)

        def scale_wide(b, r, bank_no):
            if r == 0:
                scaled[b] = new([P, 2, PACK, HALF], F32, f"scaled{b}")
            nc.vector.scalar_tensor_tensor(
                scaled[b][:, :, r, :],
                banks[bank_no][:].rearrange("p (h f) -> p h f", h=2),
                spread["tx"][:, b, r : r + 1],
                spread["cf"][:].rearrange("p (h f) -> p h f", h=2),
                MULT,
                MULT,
            )

        def activate_quarter(b, lo):
            half, first = divmod(lo, HALF)
            nc.scalar.activation(act_rows[b, lo], scaled[b][:, half, :, first : first + P], SILU)

        def new_act(b, halves, over=None):
            rows = new([P, len(halves), PACK, HALF], F32, f"act{b}{halves[0]}", over)
            for n, half in enumerate(halves):
                act[b, half] = rows[:, n, :, :]

        def activate(b, half, pair):
            nc.scalar.activation(act[b, half][:, 2 * pair : 2 * pair + 2, :], scaled[b, half, pair], SILU)

        h_in, h_mx = {}, {}

        def gate(b, lo, hi, on_vector, over=None):
            if (b, lo) not in h_in:
                h_in[b, lo] = new([P, (hi - lo) * PACK], BF16, f"h_in{b}{lo}", over)[:]
            dst = h_in[b, lo][:, 0 : (hi - lo) * PACK]
            rows = act_rows[b, lo]
            if on_vector:
                nc.vector.tensor_tensor(
                    dst.rearrange("p (c i r) -> p c r i", i=RUN, r=PACK),
                    rows.rearrange("p r (c i) -> p c r i", i=RUN),
                    ts_cols[:, b, :].unsqueeze(1).unsqueeze(3).broadcast_to([P, (hi - lo) // RUN, PACK, RUN]),
                    MULT,
                )
            else:
                nc.gpsimd.tensor_tensor(
                    dst.rearrange("p (c r) -> p c r", r=PACK),
                    rows.rearrange("p r c -> p c r"),
                    spread["ts"][:, b, :].unsqueeze(1).broadcast_to([P, hi - lo, PACK]),
                    MULT,
                )

        def quantize_h(b, lo, over=None, scales_over=None):
            both = quantize(h_in[b, lo], f"h{b}{lo}", E4M3X4, over, scales_over)
            for first in range(0, both[0][:].shape[1], P):
                h_mx[b, (lo + first) // P] = (both, slice(first, first + P))

        dy_picked, dealt, dy_in, dy_mx = {}, {}, {}, {}

        def gather_dy(k, b, on_vector, over=None, into=None):
            dy_picked[k, b] = new([P, SLOTS], BF16, f"dy_picked{k}{b}", over)[:] if into is None else into
            dealt[k, b] = on_vector
            dst = dy_picked[k, b].rearrange("p (u s e) -> p s u e", u=2, e=2) if on_vector else dy_picked[k, b]
            copy_on(on_vector, dst, dy_win[k][:].indirect(slots_of(b)))

        def turn_dy(k, b, bank_no):
            bank = banks[bank_no][:].rearrange("p (u e) -> p u e", u=2)
            words = dy_picked[k, b].bitcast(F32)
            for u in range(2):
                half = words[:, u * P : (u + 1) * P] if dealt[k, b] else words[:, u : SLOTS // 2 : 2]
                nc.tensor.transpose(bank[:, u, (k % 2) * P : (k % 2 + 1) * P], half, ident[:])

        def fetch_dy(b, half, bank_no, on_vector, over=None):
            dy_in[b, half] = new([P, HALF * PACK], BF16, f"dy_in{b}{half}", over)
            dst = dy_in[b, half][:].bitcast(F32).rearrange("p (g i u) -> p g u i", i=2, u=2)
            move_on(on_vector, dst, banks[bank_no][:].rearrange("p (u g i) -> p g u i", u=2, i=2))

        def quantize_dy(b, half, over=None, scales_over=None):
            if half == 0:
                dy_mx[b] = (new([P, E], U32, f"dy{b}_codes", over)[:], new([P, E], U8, f"dy{b}_scales", scales_over)[:])
            cols = slice(half * HALF, (half + 1) * HALF)
            nc.vector.quantize_mx(dy_mx[b][0][:, cols].bitcast(E5M2X4), dy_mx[b][1][:, cols], dy_in[b, half][:])

        def second_product(b, c, acc, lo=0, hi=E):
            moving = (dy_mx[b][0][:, lo:hi], dy_mx[b][1][:, lo:hi])
            product(acc, h_mx[b, c][0], h_mx[b, c][1], moving, E5M2X4)

        def second_product_pair(b, pair, half, bank_no):
            for n in range(2):
                second_product(b, 2 * pair + n, banks[bank_no][:, n * HALF : (n + 1) * HALF], half * HALF, (half + 1) * HALF)

        def store_pair(b, pair, half, bank_no, result):
            nc.scalar.copy(result, banks[bank_no][:])
            rows = out[b, 2 * pair * P : (2 * pair + 2) * P, half * HALF : (half + 1) * HALF]
            nc.sync.dma_start(rows.rearrange("(n p) e -> p n e", p=P), result.rearrange("p (n e) -> p n e", n=2))

        def store(b, c, bank_no, on_vector, lo=0, hi=E):
            result = new([P, hi - lo], F32, f"result{b}{c}{lo}")
            move_on(on_vector, result[:], banks[bank_no][:, 0 : hi - lo])
            nc.sync.dma_start(out[b, c * P : (c + 1) * P, lo:hi], result[:])

        for j in range(PACK):
            load_x(j)
        for b in range(EXPERTS):
            load_w(b)
        for k in range(4):
            load_dy(k)
        turn_cf()
        turn_slot_scales(ts_win, "ts_picked", P + EXPERTS * PACK, True)
        turn_slot_scales(tx_win, "tx_picked", P, False)
        fetch_cf(False)
        for j in range(3):
            gather_x_in_place(j)
            gather_x(j)
        gather_x_in_place(3)
        gather_x(3)
        weave_x(0)
        quantize_x0()
        weave_w(0, 0, 128, "vector", ("ts_win", 0))
        weave_w(0, 128, 256, "vector", ("ts_win", KIB))
        weave_w(0, 256, 512, "scalar", ("tx_win", 0))
        quantize_w_quarter(0, 0)
        quantize_w_quarter(0, 128)
        weave_x(1, ("ts_win", KIB + 128))
        quantize_x1(0, ("ts_win", 64))
        fetch_slot_scales(True, ("ts_win", KIB + 64))
        quantize_w(0, 256, 512)
        weave_w(1, 0, 512, "gpsimd", ("tx_win", 0))
        for half in range(2):
            for pair in range(2):
                first_product(0, half, pair, 2 + 2 * half + pair, P if half + pair == 0 else HALF)
        for half in range(2):
            new_act(0, (half,))
            for pair in range(2):
                scale_units(0, half, pair, 2 + 2 * half + pair)
                activate(0, half, pair)
        act_rows[0, 0], act_rows[0, HALF] = act[0, 0], act[0, 1]
        gate(0, 0, 256, True)
        quantize_x1(1, ("w_raw1", 0))
        quantize_w(1, 0, 512)
        gather_dy(0, 1, True, ("x_in11", 0))
        gate(0, 256, 512, False, ("tx_win", 0))
        gather_dy(0, 0, False)
        for r in range(PACK):
            first_product_wide(1, r, 2 + r)
        gather_dy(1, 0, False)
        gather_dy(1, 1, False)
        shared = new([P, PACK, P + HALF], F32, "shared")
        act_rows[1, 0] = shared[:, :, 0:P]
        gather_dy(2, 0, False, None, shared[:, 0, P:].bitcast(BF16))
        for r in range(PACK):
            scale_wide(1, r, 2 + r)
        turn_dy(0, 0, 2)
        turn_dy(1, 0, 2)
        turn_dy(1, 1, 7)
        turn_dy(0, 1, 7)
        activate_quarter(1, 0)
        fetch_dy(0, 0, 2, True)
        quantize_h(0, 0, ("act01", 0))
        quantize_dy(0, 0, ("act01", 2 * KIB))
        quantize_h(0, 256, ("act01", KIB))
        gather_dy(3, 0, False, ("x_win1", 0))
        gather_dy(3, 1, False)
        fetch_dy(1, 0, 7, True)
        gather_dy(2, 1, True)
        second_product_pair(0, 0, 0, 3)
        turn_dy(2, 0, 1)
        gate(1, 0, 128, True)
        turn_dy(3, 0, 1)
        turn_dy(3, 1, 6)
        turn_dy(2, 1, 6)
        later = new([P, PACK, 3 * P], F32, "act1", ("x_win1", KIB - 64))
        for n in range(3):
            act_rows[1, (n + 1) * P] = later[:, :, n * P : (n + 1) * P]
        activate_quarter(1, 128)
        store_pair(0, 0, 0, 3, new([P, E], F32, "early0", ("dy_win3", 0))[:])
        fetch_dy(0, 1, 1, True)
        quantize_dy(1, 0, None, ("x_win1", 64))
        quantize_dy(0, 1)
        quantize_h(1, 0, None, ("x_win1", 576))
        activate_quarter(1, 256)
        second_product(0, 2, banks[4][:])
        second_product_pair(0, 0, 1, 5)
        second_product(0, 3, banks[2][:])
        fetch_dy(1, 1, 6, True)
        gate(1, 128, 256, True)
        activate_quarter(1, 384)
        quantize_dy(1, 1)
        second_product(1, 0, banks[7][:])
        store(0, 2, 4, False)
        gate(1, 256, 384, True)
        store_pair(0, 0, 1, 5, new([P, E], F32, "late0")[:])
        quantize_h(1, 128)
        quantize_h(1, 256)
        second_product(1, 1, banks[3][:])
        second_product(1, 2, banks[4][:])
        store(0, 3, 2, False)
        gate(1, 384, 512, True)
        quantize_h(1, 384)
        second_product(1, 3, banks[1][:, 0:HALF], 0, HALF)
        second_product(1, 3, banks[6][:, 0:HALF], HALF, E)
        store(1, 0, 7, False)
        store(1, 1, 3, False)
        store(1, 2, 4, True)
        store(1, 3, 1, True, 0, HALF)
        store(1, 3, 6, False, HALF, E)
